import numpy as np
import ml_dtypes


def mxq(x, axis, fmt="e4m3"):
    dtype, down = {"e4m3": (ml_dtypes.float8_e4m3fn, 7), "e5m2": (ml_dtypes.float8_e5m2, 14)}[fmt]
    v = np.moveaxis(np.asarray(x, np.float32).astype(ml_dtypes.bfloat16).astype(np.float64), axis, -1)
    blocks = v.reshape(v.shape[:-1] + (-1, 32))
    amax = np.abs(blocks).max(-1, keepdims=True)
    byte = np.maximum(np.where(amax > 0, np.frexp(amax)[1] - 1 + 127, 0) - down, 1)
    scale = np.exp2(byte - 127.0)
    codes = (blocks / scale).astype(np.float32).astype(dtype).astype(np.float64)
    return np.moveaxis((codes * scale).reshape(v.shape), -1, axis)


WIDE = False


def mx_kscale(k):
    if not WIDE:
        return np.ones(k)
    levels = np.array([10, -10, 5, -5, 0])
    if k % 512:
        return np.exp2(np.random.permutation(np.resize(levels, k // 32))).repeat(32)
    a = np.empty((k // 512, 16))
    for p in range(k // 512):
        a[p, :8] = np.random.permutation(np.resize(levels, 8))
        for g in range(8):
            far = levels[np.abs(levels - a[p, g]) >= 10]
            a[p, g + 8] = far[np.random.randint(len(far))]
    return np.exp2(a.ravel()).repeat(32)


def f64(x):
    return np.asarray(x).astype(np.float64)


def striped(idx):
    return np.tile(idx.reshape(-1, 16).T, (8, 1)).astype(np.uint16)


def unstriped(offs):
    return offs[:16].T.reshape(-1).astype(np.int64)


def relu(v):
    return np.maximum(v, 0.0)


K, T, E, C, N = 1024, 1024, 2, 256, 512
M = 512


def by_expert(wq, xq):
    return np.concatenate([wq[e].T @ xq[:, e * C:(e + 1) * C] for e in range(E)], axis=1)


def setup_inputs():
    n = np.random.standard_normal
    s = mx_kscale(K)[:, None]
    v = mx_kscale(N)
    return {
        "xT": (n((K, T)) * s).astype(np.float32),
        "w": (n((E, K, N)) / np.sqrt(K) / s[None] * v[None, None, :]).astype(np.float32),
        "b": (0.3 * n((N, E)) * v[:, None]).astype(np.float32),
        "wp": (n((N, M)) / np.sqrt(N) / v[:, None]).astype(np.float32),
        "gate": np.tile(np.random.uniform(0.2, 1.0, E * C), (N, 1)).astype(np.float32),
        "offs": striped(np.random.permutation(T)[:E * C]),
    }


def reference(xT, w, b, wp, gate, offs):
    idx = unstriped(offs)
    xq = mxq(f64(xT)[:, idx], 0, "e4m3")
    y = by_expert(mxq(f64(w), 1, "e4m3"), xq)
    y = relu(y + np.repeat(f64(b), C, axis=1))
    c = np.zeros((N, T))
    c[:, idx] = f64(gate) * y
    return mxq(f64(wp), 0, "e4m3").T @ mxq(c, 0, "e4m3")

@@ -1,0 +1,255 @@
+from contextlib import ExitStack
+
+import concourse.mybir as mybir
+
+K, T, E, C, N, M = 1024, 1024, 2, 256, 512, 512
+S = E * C
+FLOPS = 2 * K * N * S + 2 * N * M * S
+
+F32 = mybir.dt.float32
+BF16 = mybir.dt.bfloat16
+U32 = mybir.dt.uint32
+I32 = mybir.dt.int32
+U16 = mybir.dt.uint16
+U8 = mybir.dt.uint8
+FP8X4 = mybir.dt.float8_e4m3fn_x4
+RELU = mybir.ActivationFunctionType.Relu
+MULT = mybir.AluOpType.mult
+ADD = mybir.AluOpType.add
+
+P = 128
+J = 4
+KP = P * J
+PASSES = K // KP
+G = 4
+H = T // 2
+
+
+def tile_moe_nxt_lin_relu_kernel(tc, xT, w, b, wp, gate, offs, out):
+    nc = tc.nc
+    with ExitStack() as ctx:
+        keep = ctx.enter_context(tc.tile_pool(name="keep", bufs=1))
+        psum = ctx.enter_context(tc.psum_pool(name="psum", bufs=1))
+
+        offsets = keep.tile([P, S // 16], U16, name="offsets")
+        bias = keep.tile([P, G * E], F32, name="bias")
+
+        x_chunks = [(1, 0, 512, 256), (1, 512, 1024, 256), (0, 0, 512, 128), (0, 512, 1024, 320)]
+        xraw = {}
+        for k, (a, t0, t1, cut) in enumerate(x_chunks):
+            xraw[a, t0] = keep.tile([P, J, t1 - t0], F32, name=f"xraw{a}{t0}")
+            src = xT[a * KP : (a + 1) * KP, t0:t1]
+            nc.sync.dma_start(xraw[a, t0][:], src.rearrange("(p j) t -> p j t", j=J))
+            if k == 0:
+                nc.sync.dma_start(offsets[:], offs)
+                nc.sync.dma_start(bias[:], b.rearrange("(p t) e -> p (t e)", t=G))
+        wraw = [[keep.tile([P, J, N], F32, name=f"wraw{e}{a}") for a in range(PASSES)] for e in range(E)]
+        wpraw = [keep.tile([P, J, M // 2], F32, name=f"wpraw{h}") for h in range(2)]
+        gates = [keep.tile([P, C], F32, name=f"gates{e}") for e in range(E)]
+
+        def load_w(e, a):
+            nc.sync.dma_start(wraw[e][a][:], w[e, a * KP : (a + 1) * KP, :].rearrange("(p j) n -> p j n", j=J))
+
+        def load_wp(h):
+            nc.sync.dma_start(wpraw[h][:], wp[:, h * 256 : (h + 1) * 256].rearrange("(p j) f -> p j f", j=J))
+
+        def load_gates(e):
+            nc.sync.dma_start(gates[e][:], gate[0:P, e * C : (e + 1) * C])
+
+        load_w(0, 0)
+        load_w(0, 1)
+        load_wp(0)
+        load_w(1, 0)
+        load_gates(0)
+        load_w(1, 1)
+        load_wp(1)
+        load_gates(1)
+
+        warm = keep.tile([P, 8], F32, name="warm")
+        warmed = keep.tile([P, 8], F32, name="warmed")
+        nc.vector.memset(warm[:], 0.0)
+        nc.scalar.activation(warmed[:], warm[:], RELU)
+
+        xbytes = keep.tile([P, T], U8, name="xbytes", align_bytes=64)
+        nc.vector.memset(xbytes[:].bitcast(I32), 0)
+        outt = [keep.tile([P, T], F32, name=f"outt{g}", align_bytes=64) for g in range(G)]
+        for g in range(G):
+            nc.gpsimd.memset(outt[g][:], 0.0)
+
+        xgrouped = [keep.tile([P, T, J], BF16, name=f"xgrouped{a}", align_bytes=64) for a in range(PASSES)]
+        xcodes = [keep.tile([P, T], U32, name=f"xcodes{a}", align_bytes=64) for a in range(PASSES)]
+        gcodes = [keep.tile([P, S], U32, name=f"gcodes{a}", align_bytes=64) for a in range(PASSES)]
+        gbytes = [keep.tile([P, C], U8, name="gbytes0", align_bytes=64)]
+        wgrouped = [
+            [
+                keep.tile([P, G, P, J], BF16, name=f"wgrouped{e}{a}", tag=f"wgrouped{e}{a}", align_bytes=64)
+                for a in range(PASSES)
+            ]
+            for e in range(E)
+        ]
+        wcodes = [[keep.tile([P, N], U32, name=f"wcodes{e}{a}", align_bytes=64) for a in range(PASSES)] for e in range(E)]
+        wbytes = [[keep.tile([P, N], U8, name=f"wbytes{e}{a}", align_bytes=64) for a in range(PASSES)] for e in range(E)]
+        wpgrouped = keep.tile([P, M, J], BF16, name="wpgrouped", align_bytes=64)
+        wpcodes = keep.tile([P, M], U32, name="wpcodes", align_bytes=64)
+        wpbytes = keep.tile([P, M], U8, name="wpbytes", align_bytes=64)
+        y = [keep.tile([P, G, C], F32, name=f"y{e}", tag=f"y{e}", align_bytes=64) for e in range(E)]
+        c = [keep.tile([P, C, J], BF16, name=f"c{e}", align_bytes=64) for e in range(E)]
+        ccodes = keep.tile([P, S], U32, name="ccodes", align_bytes=64)
+        cbytes = keep.tile([P, S], U8, name="cbytes", align_bytes=64)
+        ybank = [psum.tile([P, C], F32, name=f"ybank{t}") for t in range(G)]
+        obank = [psum.tile([P, S], F32, name=f"obank{g}") for g in range(G)]
+
+        def move(engine, dst, src):
+            if engine == "v":
+                nc.vector.tensor_copy(out=dst, in_=src)
+            elif engine == "s":
+                nc.scalar.copy(out=dst, in_=src)
+            else:
+                nc.gpsimd.tensor_scalar(dst, src, 1.0, 0.0, MULT, ADD)
+
+        def group_x(engine, a, t0, lo, hi):
+            move(
+                engine,
+                xgrouped[a][:, t0 + lo : t0 + hi, :].rearrange("p (c i) j -> p c j i", i=4),
+                xraw[a, t0][:, :, lo:hi].rearrange("p j (c i) -> p c j i", i=4),
+            )
+
+        def group_w(engine, e, a, lo, hi):
+            order = "p m t j" if engine == "g" else "p m j t"
+            move(
+                engine,
+                wgrouped[e][a][:, lo:hi, :, :].rearrange("p t m j -> " + order),
+                wraw[e][a][:].rearrange("p j (m t) -> " + order, t=G)[:, :, lo:hi, :]
+                if engine == "g"
+                else wraw[e][a][:].rearrange("p j (m t) -> " + order, t=G)[:, :, :, lo:hi],
+            )
+
+        def group_wp(engine, h, lo, hi):
+            move(
+                engine,
+                wpgrouped[:, h * 256 + lo : h * 256 + hi, :].rearrange("p (c i) j -> p c j i", i=4),
+                wpraw[h][:, :, lo:hi].rearrange("p j (c i) -> p c j i", i=4),
+            )
+
+        def quantize_x(a, t0, t1):
+            nc.vector.quantize_mx(
+                out=xcodes[a][:, t0:t1].bitcast(FP8X4),
+                scales=xbytes[4 * a :, t0:t1],
+                in_=xgrouped[a][:, t0:t1, :].rearrange("p t j -> p (t j)"),
+            )
+
+        def quantize_w(e, a, t0, t1):
+            nc.vector.quantize_mx(
+                out=wcodes[e][a][:, t0 * P : t1 * P].bitcast(FP8X4),
+                scales=wbytes[e][a][:, t0 * P : t1 * P],
+                in_=wgrouped[e][a][:, t0:t1, :, :].rearrange("p t m j -> p (t m j)"),
+            )
+
+        def quantize_wp(f0, f1):
+            nc.vector.quantize_mx(
+                out=wpcodes[:, f0:f1].bitcast(FP8X4),
+                scales=wpbytes[:, f0:f1],
+                in_=wpgrouped[:, f0:f1, :].rearrange("p f j -> p (f j)"),
+            )
+
+        def gather_words(a, s0, s1):
+            nc.vector.tensor_copy(gcodes[a][:, s0:s1], xcodes[a][:].indirect(offsets[:, s0 // 16 : s1 // 16]))
+
+        def gather_bytes(e):
+            nc.vector.tensor_copy(gbytes[e][:], xbytes[:].indirect(offsets[:, e * 16 : (e + 1) * 16]))
+
+        def multiply(e, a, t):
+            nc.tensor.matmul_mx(
+                out=ybank[t][:],
+                lhsT=wcodes[e][a][:, t * P : (t + 1) * P].bitcast(FP8X4),
+                lhsT_scale=wbytes[e][a][:, t * P : (t + 1) * P],
+                rhs=gcodes[a][:, e * C : (e + 1) * C].bitcast(FP8X4),
+                rhs_scale=gbytes[e][4 * a :, :],
+                start=(a == 0),
+                stop=(a == PASSES - 1),
+            )
+
+        def relu(e, t):
+            nc.scalar.activation(y[e][:, t, :], ybank[t][:], RELU, bias=bias[:, t * E + e : t * E + e + 1])
+
+        def apply_gate(engine, e):
+            engine.tensor_tensor(
+                out=c[e][:],
+                in0=y[e][:].rearrange("p t s -> p s t"),
+                in1=gates[e][:].unsqueeze(2).to_broadcast([P, C, J]),
+                op=MULT,
+            )
+
+        def quantize_c(e):
+            nc.vector.quantize_mx(
+                out=ccodes[:, e * C : (e + 1) * C].bitcast(FP8X4),
+                scales=cbytes[:, e * C : (e + 1) * C],
+                in_=c[e][:].rearrange("p s j -> p (s j)"),
+            )
+
+        def project(g, s0, s1):
+            nc.tensor.matmul_mx(
+                out=obank[g][:, s0:s1],
+                lhsT=wpcodes[:, g * P : (g + 1) * P].bitcast(FP8X4),
+                lhsT_scale=wpbytes[:, g * P : (g + 1) * P],
+                rhs=ccodes[:, s0:s1].bitcast(FP8X4),
+                rhs_scale=cbytes[:, s0:s1],
+                start=True,
+                stop=True,
+            )
+            nc.scalar.copy(out=oslots[g][:, s0:s1], in_=obank[g][:, s0:s1])
+
+        def scatter(g, s0, s1):
+            nc.vector.tensor_copy(outt[g][:].indirect(offsets[:, s0 // 16 : s1 // 16]), oslots[g][:, s0:s1])
+
+        for a, t0, t1, cut in x_chunks:
+            group_x("v", a, t0, 0, cut)
+            group_x("s", a, t0, cut, t1 - t0)
+            quantize_x(a, t0, t1)
+            if t1 == T:
+                gather_words(a, 0, S)
+        group_w("g", 0, 0, 0, 2)
+        group_w("s", 0, 0, 2, 4)
+        quantize_w(0, 0, 0, 4)
+        gather_bytes(0)
+        for t in range(G):
+            multiply(0, 0, t)
+        for t in (0, 2):
+            group_w("s", 0, 1, t, t + 1)
+            group_w("v", 0, 1, t + 1, t + 2)
+            quantize_w(0, 1, t, t + 2)
+            for u in (t, t + 1):
+                multiply(0, 1, u)
+                relu(0, u)
+        apply_gate(nc.vector, 0)
+        quantize_c(0)
+        for h, cut in ((0, 32), (1, 64)):
+            group_wp("v", h, 0, cut)
+            group_wp("s", h, cut, 256)
+            quantize_wp(h * 256, h * 256 + 256)
+        gbytes.append(keep.tile([P, C], U8, name="gbytes1", tag="wgrouped01", align_bytes=64))
+        gather_bytes(1)
+        for a in range(PASSES):
+            group_w("s", 1, a, 0, 2)
+            group_w("v", 1, a, 2, 4)
+            quantize_w(1, a, 0, 4)
+            for t in range(G):
+                multiply(1, a, t)
+                if a == PASSES - 1:
+                    relu(1, t)
+        late = keep.tile([P, G - 1, S], F32, name="late", tag="wgrouped11", align_bytes=64)
+        oslots = [late[:, g, :] for g in range(G - 1)]
+        for g in range(G - 1):
+            project(g, 0, C)
+            scatter(g, 0, C)
+        apply_gate(nc.gpsimd, 1)
+        quantize_c(1)
+        last = keep.tile([P, S], F32, name="last", tag="y1", align_bytes=64)
+        oslots.append(last[:])
+        project(3, 0, C)
+        scatter(3, 0, C)
+        for g in range(G):
+            project(g, C, S)
+        for g in range(G):
+            scatter(g, C, S)
+            nc.sync.dma_start(out[g * P : (g + 1) * P, :], outt[g][:])

@@ -4,7 +4,7 @@ import concourse.mybir as mybir
 
 K, T, E, C, N, M = 1024, 1024, 2, 256, 512, 512
 S = E * C
-FLOPS = 2 * K * N * S + 2 * N * M * S
+FLOPS = 2 * K * N * S + 2 * N * M * T
 
 F32 = mybir.dt.float32
 BF16 = mybir.dt.bfloat16
@@ -22,7 +22,9 @@ J = 4
 KP = P * J
 PASSES = K // KP
 G = 4
-H = T // 2
+EARLY = 128
+Q = 256
+CHUNKS = T // Q
 
 
 def tile_moe_nxt_lin_relu_kernel(tc, xT, w, b, wp, gate, offs, out):
@@ -34,7 +36,7 @@ def tile_moe_nxt_lin_relu_kernel(tc, xT, w, b, wp, gate, offs, out):
         offsets = keep.tile([P, S // 16], U16, name="offsets")
         bias = keep.tile([P, G * E], F32, name="bias")
 
-        x_chunks = [(1, 0, 512, 256), (1, 512, 1024, 256), (0, 0, 512, 128), (0, 512, 1024, 320)]
+        x_chunks = [(1, 0, 512, 320), (1, 512, 1024, 320), (0, 0, 512, 192), (0, 512, 1024, 352)]
         xraw = {}
         for k, (a, t0, t1, cut) in enumerate(x_chunks):
             xraw[a, t0] = keep.tile([P, J, t1 - t0], F32, name=f"xraw{a}{t0}")
@@ -45,7 +47,8 @@ def tile_moe_nxt_lin_relu_kernel(tc, xT, w, b, wp, gate, offs, out):
                 nc.sync.dma_start(bias[:], b.rearrange("(p t) e -> p (t e)", t=G))
         wraw = [[keep.tile([P, J, N], F32, name=f"wraw{e}{a}") for a in range(PASSES)] for e in range(E)]
         wpraw = [keep.tile([P, J, M // 2], F32, name=f"wpraw{h}") for h in range(2)]
-        gates = [keep.tile([P, C], F32, name=f"gates{e}") for e in range(E)]
+        early = keep.tile([P, EARLY], F32, name="early")
+        late = keep.tile([P, S - EARLY], F32, name="late")
 
         def load_w(e, a):
             nc.sync.dma_start(wraw[e][a][:], w[e, a * KP : (a + 1) * KP, :].rearrange("(p j) n -> p j n", j=J))
@@ -53,17 +56,14 @@ def tile_moe_nxt_lin_relu_kernel(tc, xT, w, b, wp, gate, offs, out):
         def load_wp(h):
             nc.sync.dma_start(wpraw[h][:], wp[:, h * 256 : (h + 1) * 256].rearrange("(p j) f -> p j f", j=J))
 
-        def load_gates(e):
-            nc.sync.dma_start(gates[e][:], gate[0:P, e * C : (e + 1) * C])
-
         load_w(0, 0)
         load_w(0, 1)
-        load_wp(0)
         load_w(1, 0)
-        load_gates(0)
+        nc.sync.dma_start(early[:], gate[0:P, 0:EARLY])
         load_w(1, 1)
+        load_wp(0)
+        nc.sync.dma_start(late[:], gate[0:P, EARLY:S])
         load_wp(1)
-        load_gates(1)
 
         warm = keep.tile([P, 8], F32, name="warm")
         warmed = keep.tile([P, 8], F32, name="warmed")
@@ -72,32 +72,32 @@ def tile_moe_nxt_lin_relu_kernel(tc, xT, w, b, wp, gate, offs, out):
 
         xbytes = keep.tile([P, T], U8, name="xbytes", align_bytes=64)
         nc.vector.memset(xbytes[:].bitcast(I32), 0)
-        outt = [keep.tile([P, T], F32, name=f"outt{g}", align_bytes=64) for g in range(G)]
-        for g in range(G):
-            nc.gpsimd.memset(outt[g][:], 0.0)
+        window = [keep.tile([P, T], F32, name=f"window{u}", align_bytes=64) for u in range(2)]
+        for u in range(2):
+            nc.gpsimd.memset(window[u][:], 0.0)
 
         xgrouped = [keep.tile([P, T, J], BF16, name=f"xgrouped{a}", align_bytes=64) for a in range(PASSES)]
         xcodes = [keep.tile([P, T], U32, name=f"xcodes{a}", align_bytes=64) for a in range(PASSES)]
-        gcodes = [keep.tile([P, S], U32, name=f"gcodes{a}", align_bytes=64) for a in range(PASSES)]
-        gbytes = [keep.tile([P, C], U8, name="gbytes0", align_bytes=64)]
-        wgrouped = [
-            [
-                keep.tile([P, G, P, J], BF16, name=f"wgrouped{e}{a}", tag=f"wgrouped{e}{a}", align_bytes=64)
-                for a in range(PASSES)
-            ]
+        gcodes = {}
+        gbytes = {}
+        wgrouped = {
+            (e, a, u): keep.tile([P, 2, P, J], BF16, name=f"wgrouped{e}{a}{u}", align_bytes=64)
             for e in range(E)
-        ]
+            for a in range(PASSES)
+            for u in range(2)
+        }
         wcodes = [[keep.tile([P, N], U32, name=f"wcodes{e}{a}", align_bytes=64) for a in range(PASSES)] for e in range(E)]
         wbytes = [[keep.tile([P, N], U8, name=f"wbytes{e}{a}", align_bytes=64) for a in range(PASSES)] for e in range(E)]
         wpgrouped = keep.tile([P, M, J], BF16, name="wpgrouped", align_bytes=64)
         wpcodes = keep.tile([P, M], U32, name="wpcodes", align_bytes=64)
         wpbytes = keep.tile([P, M], U8, name="wpbytes", align_bytes=64)
-        y = [keep.tile([P, G, C], F32, name=f"y{e}", tag=f"y{e}", align_bytes=64) for e in range(E)]
-        c = [keep.tile([P, C, J], BF16, name=f"c{e}", align_bytes=64) for e in range(E)]
-        ccodes = keep.tile([P, S], U32, name="ccodes", align_bytes=64)
-        cbytes = keep.tile([P, S], U8, name="cbytes", align_bytes=64)
-        ybank = [psum.tile([P, C], F32, name=f"ybank{t}") for t in range(G)]
-        obank = [psum.tile([P, S], F32, name=f"obank{g}") for g in range(G)]
+        y = [[keep.tile([P, 2, C], F32, name=f"y{e}{u}", align_bytes=64) for u in range(2)] for e in range(E)]
+        c = [[keep.tile([P, C, 2], BF16, name=f"c{e}{u}", align_bytes=64) for u in range(2)] for e in range(E)]
+        woven = [keep.tile([P, Q, 2], F32, name=f"woven{q}", align_bytes=64) for q in range(CHUNKS)]
+        ccodes = [keep.tile([P, Q], U32, name=f"ccodes{q}", align_bytes=64) for q in range(CHUNKS)]
+        cbytes = [keep.tile([P, Q], U8, name=f"cbytes{q}", align_bytes=64) for q in range(CHUNKS)]
+        result = [[keep.tile([P, 2, Q], F32, name=f"result{q}{h}", align_bytes=64) for h in range(2)] for q in range(CHUNKS)]
+        ybank = [psum.tile([P, C], F32, name=f"ybank{t}", tag=f"bank{t}") for t in range(G)]
 
         def move(engine, dst, src):
             if engine == "v":
@@ -114,15 +114,10 @@ def tile_moe_nxt_lin_relu_kernel(tc, xT, w, b, wp, gate, offs, out):
                 xraw[a, t0][:, :, lo:hi].rearrange("p j (c i) -> p c j i", i=4),
             )
 
-        def group_w(engine, e, a, lo, hi):
+        def group_w(engine, e, a, u):
             order = "p m t j" if engine == "g" else "p m j t"
-            move(
-                engine,
-                wgrouped[e][a][:, lo:hi, :, :].rearrange("p t m j -> " + order),
-                wraw[e][a][:].rearrange("p j (m t) -> " + order, t=G)[:, :, lo:hi, :]
-                if engine == "g"
-                else wraw[e][a][:].rearrange("p j (m t) -> " + order, t=G)[:, :, :, lo:hi],
-            )
+            columns = wraw[e][a][:].rearrange("p j (m u t) -> p j m u t", u=2, t=2)[:, :, :, u, :]
+            move(engine, wgrouped[e, a, u][:].rearrange("p t m j -> " + order), columns.rearrange("p j m t -> " + order))
 
         def group_wp(engine, h, lo, hi):
             move(
@@ -138,11 +133,11 @@ def tile_moe_nxt_lin_relu_kernel(tc, xT, w, b, wp, gate, offs, out):
                 in_=xgrouped[a][:, t0:t1, :].rearrange("p t j -> p (t j)"),
             )
 
-        def quantize_w(e, a, t0, t1):
+        def quantize_w(e, a, u):
             nc.vector.quantize_mx(
-                out=wcodes[e][a][:, t0 * P : t1 * P].bitcast(FP8X4),
-                scales=wbytes[e][a][:, t0 * P : t1 * P],
-                in_=wgrouped[e][a][:, t0:t1, :, :].rearrange("p t m j -> p (t m j)"),
+                out=wcodes[e][a][:, u * 2 * P : (u + 1) * 2 * P].bitcast(FP8X4),
+                scales=wbytes[e][a][:, u * 2 * P : (u + 1) * 2 * P],
+                in_=wgrouped[e, a, u][:].rearrange("p t m j -> p (t m j)"),
             )
 
         def quantize_wp(f0, f1):
@@ -152,10 +147,14 @@ def tile_moe_nxt_lin_relu_kernel(tc, xT, w, b, wp, gate, offs, out):
                 in_=wpgrouped[:, f0:f1, :].rearrange("p f j -> p (f j)"),
             )
 
-        def gather_words(a, s0, s1):
-            nc.vector.tensor_copy(gcodes[a][:, s0:s1], xcodes[a][:].indirect(offsets[:, s0 // 16 : s1 // 16]))
+        def gather_words(a, e0, e1, tag):
+            words = keep.tile([P, (e1 - e0) * C], U32, name=f"gcodes{a}{e0}", tag=tag, align_bytes=64)
+            nc.vector.tensor_copy(words[:], xcodes[a][:].indirect(offsets[:, e0 * 16 : e1 * 16]))
+            for e in range(e0, e1):
+                gcodes[a, e] = words[:, (e - e0) * C : (e - e0 + 1) * C]
 
-        def gather_bytes(e):
+        def gather_bytes(e, tag):
+            gbytes[e] = keep.tile([P, C], U8, name=f"gbytes{e}", tag=tag, align_bytes=64)
             nc.vector.tensor_copy(gbytes[e][:], xbytes[:].indirect(offsets[:, e * 16 : (e + 1) * 16]))
 
         def multiply(e, a, t):
@@ -163,93 +162,119 @@ def tile_moe_nxt_lin_relu_kernel(tc, xT, w, b, wp, gate, offs, out):
                 out=ybank[t][:],
                 lhsT=wcodes[e][a][:, t * P : (t + 1) * P].bitcast(FP8X4),
                 lhsT_scale=wbytes[e][a][:, t * P : (t + 1) * P],
-                rhs=gcodes[a][:, e * C : (e + 1) * C].bitcast(FP8X4),
+                rhs=gcodes[a, e].bitcast(FP8X4),
                 rhs_scale=gbytes[e][4 * a :, :],
                 start=(a == 0),
                 stop=(a == PASSES - 1),
             )
 
         def relu(e, t):
-            nc.scalar.activation(y[e][:, t, :], ybank[t][:], RELU, bias=bias[:, t * E + e : t * E + e + 1])
+            nc.scalar.activation(
+                y[e][t // 2][:, t % 2, :], ybank[t][:], RELU, bias=bias[:, t * E + e : t * E + e + 1]
+            )
 
-        def apply_gate(engine, e):
+        def apply_gate(engine, e, u, s0=0, s1=C):
+            first = e * C + s0
+            weights = early[:] if first < EARLY else late[:, first - EARLY : first - EARLY + s1 - s0]
             engine.tensor_tensor(
-                out=c[e][:],
-                in0=y[e][:].rearrange("p t s -> p s t"),
-                in1=gates[e][:].unsqueeze(2).to_broadcast([P, C, J]),
+                out=c[e][u][:, s0:s1, :],
+                in0=y[e][u][:, :, s0:s1].rearrange("p t s -> p s t"),
+                in1=weights.unsqueeze(2).to_broadcast([P, s1 - s0, 2]),
                 op=MULT,
             )
 
-        def quantize_c(e):
+        def scatter(e, u, s0=0, s1=C):
+            nc.vector.tensor_copy(
+                window[u][:].indirect(offsets[:, (e * C + s0) // 16 : (e * C + s1) // 16]),
+                c[e][u][:, s0:s1, :].rearrange("p s t -> p (s t)").bitcast(F32),
+            )
+
+        def weave(engine, q, u):
+            move(engine, woven[q][:, :, u], window[u][:, q * Q : (q + 1) * Q])
+
+        def quantize_c(q):
             nc.vector.quantize_mx(
-                out=ccodes[:, e * C : (e + 1) * C].bitcast(FP8X4),
-                scales=cbytes[:, e * C : (e + 1) * C],
-                in_=c[e][:].rearrange("p s j -> p (s j)"),
+                out=ccodes[q][:].bitcast(FP8X4),
+                scales=cbytes[q][:],
+                in_=woven[q][:].rearrange("p t u -> p (t u)").bitcast(BF16),
             )
 
-        def project(g, s0, s1):
-            nc.tensor.matmul_mx(
-                out=obank[g][:, s0:s1],
-                lhsT=wpcodes[:, g * P : (g + 1) * P].bitcast(FP8X4),
-                lhsT_scale=wpbytes[:, g * P : (g + 1) * P],
-                rhs=ccodes[:, s0:s1].bitcast(FP8X4),
-                rhs_scale=cbytes[:, s0:s1],
-                start=True,
-                stop=True,
-            )
-            nc.scalar.copy(out=oslots[g][:, s0:s1], in_=obank[g][:, s0:s1])
-
-        def scatter(g, s0, s1):
-            nc.vector.tensor_copy(outt[g][:].indirect(offsets[:, s0 // 16 : s1 // 16]), oslots[g][:, s0:s1])
+        def project(engine, q, h):
+            bank = psum.tile([P, 2, Q], F32, name=f"obank{q}{h}", tag=f"bank{(4 + 2 * q + h) % 8}")
+            for i in range(2):
+                g = 2 * h + i
+                nc.tensor.matmul_mx(
+                    out=bank[:, i, :],
+                    lhsT=wpcodes[:, g * P : (g + 1) * P].bitcast(FP8X4),
+                    lhsT_scale=wpbytes[:, g * P : (g + 1) * P],
+                    rhs=ccodes[q][:].bitcast(FP8X4),
+                    rhs_scale=cbytes[q][:],
+                    start=True,
+                    stop=True,
+                )
+            move(engine, result[q][h][:], bank[:])
+            rows = out[2 * h * P : (2 * h + 2) * P, q * Q : (q + 1) * Q]
+            nc.sync.dma_start(rows.rearrange("(i p) t -> p i t", p=P), result[q][h][:])
 
         for a, t0, t1, cut in x_chunks:
             group_x("v", a, t0, 0, cut)
             group_x("s", a, t0, cut, t1 - t0)
             quantize_x(a, t0, t1)
-            if t1 == T:
-                gather_words(a, 0, S)
-        group_w("g", 0, 0, 0, 2)
-        group_w("s", 0, 0, 2, 4)
-        quantize_w(0, 0, 0, 4)
-        gather_bytes(0)
-        for t in range(G):
-            multiply(0, 0, t)
-        for t in (0, 2):
-            group_w("s", 0, 1, t, t + 1)
-            group_w("v", 0, 1, t + 1, t + 2)
-            quantize_w(0, 1, t, t + 2)
-            for u in (t, t + 1):
-                multiply(0, 1, u)
-                relu(0, u)
-        apply_gate(nc.vector, 0)
+            if t1 == T and a == 1:
+                gather_words(1, 0, E, "gcodes1")
+        gather_words(0, 0, 1, "gcodes00")
+        gather_bytes(0, "gbytes0")
+        group_w("g", 0, 0, 0)
+        group_w("s", 0, 0, 1)
+        for u in range(2):
+            quantize_w(0, 0, u)
+        group_w("v", 0, 1, 0)
+        group_w("s", 0, 1, 1)
+        for u in range(2):
+            quantize_w(0, 1, u)
+            for t in (2 * u, 2 * u + 1):
+                multiply(0, 0, t)
+            for t in (2 * u, 2 * u + 1):
+                multiply(0, 1, t)
+                relu(0, t)
+        gather_words(0, 1, E, "wgrouped010")
+        gather_bytes(1, "wgrouped011")
+        group_w("v", 1, 0, 0)
+        group_w("s", 1, 0, 1)
+        apply_gate(nc.vector, 0, 0, 0, EARLY)
+        apply_gate(nc.gpsimd, 0, 1, 0, EARLY)
+        scatter(0, 0, 0, EARLY)
+        for u in range(2):
+            quantize_w(1, 0, u)
+        scatter(0, 1, 0, EARLY)
+        group_w("s", 1, 1, 0)
+        group_w("s", 1, 1, 1)
+        for u in range(2):
+            quantize_w(1, 1, u)
+            for t in (2 * u, 2 * u + 1):
+                multiply(1, 0, t)
+            for t in (2 * u, 2 * u + 1):
+                multiply(1, 1, t)
+                relu(1, t)
+        apply_gate(nc.vector, 0, 0, EARLY, C)
+        apply_gate(nc.gpsimd, 0, 1, EARLY, C)
+        scatter(0, 0, EARLY, C)
+        scatter(0, 1, EARLY, C)
+        apply_gate(nc.vector, 1, 0)
+        apply_gate(nc.gpsimd, 1, 1)
+        scatter(1, 0)
+        group_wp("s", 0, 0, 256)
+        group_wp("s", 1, 0, 256)
+        for q in range(CHUNKS):
+            weave("s", q, 0)
+        scatter(1, 1)
+        weave("v", 0, 1)
+        quantize_wp(0, 256)
         quantize_c(0)
-        for h, cut in ((0, 32), (1, 64)):
-            group_wp("v", h, 0, cut)
-            group_wp("s", h, cut, 256)
-            quantize_wp(h * 256, h * 256 + 256)
-        gbytes.append(keep.tile([P, C], U8, name="gbytes1", tag="wgrouped01", align_bytes=64))
-        gather_bytes(1)
-        for a in range(PASSES):
-            group_w("s", 1, a, 0, 2)
-            group_w("v", 1, a, 2, 4)
-            quantize_w(1, a, 0, 4)
-            for t in range(G):
-                multiply(1, a, t)
-                if a == PASSES - 1:
-                    relu(1, t)
-        late = keep.tile([P, G - 1, S], F32, name="late", tag="wgrouped11", align_bytes=64)
-        oslots = [late[:, g, :] for g in range(G - 1)]
-        for g in range(G - 1):
-            project(g, 0, C)
-            scatter(g, 0, C)
-        apply_gate(nc.gpsimd, 1)
-        quantize_c(1)
-        last = keep.tile([P, S], F32, name="last", tag="y1", align_bytes=64)
-        oslots.append(last[:])
-        project(3, 0, C)
-        scatter(3, 0, C)
-        for g in range(G):
-            project(g, C, S)
-        for g in range(G):
-            scatter(g, C, S)
-            nc.sync.dma_start(out[g * P : (g + 1) * P, :], outt[g][:])
+        quantize_wp(256, 512)
+        for q in range(1, CHUNKS):
+            weave("v", q, 1)
+            quantize_c(q)
+        for q in range(CHUNKS):
+            for h in range(2):
+                project("v" if q >= 2 and h == 1 else "s", q, h)

@@ -22,7 +22,6 @@ J = 4
 KP = P * J
 PASSES = K // KP
 G = 4
-EARLY = 128
 Q = 256
 CHUNKS = T // Q
 
@@ -34,9 +33,9 @@ def tile_moe_nxt_lin_relu_kernel(tc, xT, w, b, wp, gate, offs, out):
         psum = ctx.enter_context(tc.psum_pool(name="psum", bufs=1))
 
         offsets = keep.tile([P, S // 16], U16, name="offsets")
-        bias = keep.tile([P, G * E], F32, name="bias")
+        bias = keep.tile([P, G * E], F32, name="bias", align_bytes=64)
 
-        x_chunks = [(1, 0, 512, 320), (1, 512, 1024, 320), (0, 0, 512, 192), (0, 512, 1024, 352)]
+        x_chunks = [(1, 0, 512, 320), (1, 512, 1024, 320), (0, 0, 512, 192), (0, 512, 768, 64), (0, 768, 1024, 160)]
         xraw = {}
         for k, (a, t0, t1, cut) in enumerate(x_chunks):
             xraw[a, t0] = keep.tile([P, J, t1 - t0], F32, name=f"xraw{a}{t0}")
@@ -45,10 +44,9 @@ def tile_moe_nxt_lin_relu_kernel(tc, xT, w, b, wp, gate, offs, out):
             if k == 0:
                 nc.sync.dma_start(offsets[:], offs)
                 nc.sync.dma_start(bias[:], b.rearrange("(p t) e -> p (t e)", t=G))
-        wraw = [[keep.tile([P, J, N], F32, name=f"wraw{e}{a}") for a in range(PASSES)] for e in range(E)]
+        wraw = [[keep.tile([P, J, N], F32, name=f"wraw{e}{a}", align_bytes=64) for a in range(PASSES)] for e in range(E)]
         wpraw = [keep.tile([P, J, M // 2], F32, name=f"wpraw{h}") for h in range(2)]
-        early = keep.tile([P, EARLY], F32, name="early")
-        late = keep.tile([P, S - EARLY], F32, name="late")
+        gates = [keep.tile([P, C], F32, name=f"gates{e}") for e in range(E)]
 
         def load_w(e, a):
             nc.sync.dma_start(wraw[e][a][:], w[e, a * KP : (a + 1) * KP, :].rearrange("(p j) n -> p j n", j=J))
@@ -59,10 +57,10 @@ def tile_moe_nxt_lin_relu_kernel(tc, xT, w, b, wp, gate, offs, out):
         load_w(0, 0)
         load_w(0, 1)
         load_w(1, 0)
-        nc.sync.dma_start(early[:], gate[0:P, 0:EARLY])
+        nc.sync.dma_start(gates[0][:], gate[0:P, 0:C])
         load_w(1, 1)
+        nc.sync.dma_start(gates[1][:], gate[0:P, C:S])
         load_wp(0)
-        nc.sync.dma_start(late[:], gate[0:P, EARLY:S])
         load_wp(1)
 
         warm = keep.tile([P, 8], F32, name="warm")
@@ -72,9 +70,9 @@ def tile_moe_nxt_lin_relu_kernel(tc, xT, w, b, wp, gate, offs, out):
 
         xbytes = keep.tile([P, T], U8, name="xbytes", align_bytes=64)
         nc.vector.memset(xbytes[:].bitcast(I32), 0)
-        window = [keep.tile([P, T], F32, name=f"window{u}", align_bytes=64) for u in range(2)]
+        window = [keep.tile([P, (2 - u) * T], F32, name=f"window{u}", align_bytes=64) for u in range(2)]
         for u in range(2):
-            nc.gpsimd.memset(window[u][:], 0.0)
+            nc.gpsimd.memset(window[u][:, 0:T], 0.0)
 
         xgrouped = [keep.tile([P, T, J], BF16, name=f"xgrouped{a}", align_bytes=64) for a in range(PASSES)]
         xcodes = [keep.tile([P, T], U32, name=f"xcodes{a}", align_bytes=64) for a in range(PASSES)]
@@ -88,11 +86,9 @@ def tile_moe_nxt_lin_relu_kernel(tc, xT, w, b, wp, gate, offs, out):
         }
         wcodes = [[keep.tile([P, N], U32, name=f"wcodes{e}{a}", align_bytes=64) for a in range(PASSES)] for e in range(E)]
         wbytes = [[keep.tile([P, N], U8, name=f"wbytes{e}{a}", align_bytes=64) for a in range(PASSES)] for e in range(E)]
-        wpgrouped = keep.tile([P, M, J], BF16, name="wpgrouped", align_bytes=64)
-        wpcodes = keep.tile([P, M], U32, name="wpcodes", align_bytes=64)
         wpbytes = keep.tile([P, M], U8, name="wpbytes", align_bytes=64)
         y = [[keep.tile([P, 2, C], F32, name=f"y{e}{u}", align_bytes=64) for u in range(2)] for e in range(E)]
-        c = [[keep.tile([P, C, 2], BF16, name=f"c{e}{u}", align_bytes=64) for u in range(2)] for e in range(E)]
+        c = {}
         woven = [keep.tile([P, Q, 2], F32, name=f"woven{q}", align_bytes=64) for q in range(CHUNKS)]
         ccodes = [keep.tile([P, Q], U32, name=f"ccodes{q}", align_bytes=64) for q in range(CHUNKS)]
         cbytes = [keep.tile([P, Q], U8, name=f"cbytes{q}", align_bytes=64) for q in range(CHUNKS)]
@@ -173,24 +169,24 @@ def tile_moe_nxt_lin_relu_kernel(tc, xT, w, b, wp, gate, offs, out):
                 y[e][t // 2][:, t % 2, :], ybank[t][:], RELU, bias=bias[:, t * E + e : t * E + e + 1]
             )
 
-        def apply_gate(engine, e, u, s0=0, s1=C):
-            first = e * C + s0
-            weights = early[:] if first < EARLY else late[:, first - EARLY : first - EARLY + s1 - s0]
-            engine.tensor_tensor(
-                out=c[e][u][:, s0:s1, :],
+        def apply_gate(e, u, tag, s0=0, s1=C):
+            c[e, u, s0] = keep.tile([P, s1 - s0, 2], BF16, name=f"c{e}{u}{s0}", tag=tag, align_bytes=64)
+            nc.vector.tensor_tensor(
+                out=c[e, u, s0][:],
                 in0=y[e][u][:, :, s0:s1].rearrange("p t s -> p s t"),
-                in1=weights.unsqueeze(2).to_broadcast([P, s1 - s0, 2]),
+                in1=gates[e][:, s0:s1].unsqueeze(2).to_broadcast([P, s1 - s0, 2]),
                 op=MULT,
             )
 
         def scatter(e, u, s0=0, s1=C):
             nc.vector.tensor_copy(
                 window[u][:].indirect(offsets[:, (e * C + s0) // 16 : (e * C + s1) // 16]),
-                c[e][u][:, s0:s1, :].rearrange("p s t -> p (s t)").bitcast(F32),
+                c[e, u, s0][:].rearrange("p s t -> p (s t)").bitcast(F32),
             )
 
-        def weave(engine, q, u):
-            move(engine, woven[q][:, :, u], window[u][:, q * Q : (q + 1) * Q])
+        def weave(engine, q):
+            both = window[0][:].rearrange("p (u t) -> p t u", u=2)
+            move(engine, woven[q][:], both[:, q * Q : (q + 1) * Q, :])
 
         def quantize_c(q):
             nc.vector.quantize_mx(
@@ -220,60 +216,47 @@ def tile_moe_nxt_lin_relu_kernel(tc, xT, w, b, wp, gate, offs, out):
             group_x("v", a, t0, 0, cut)
             group_x("s", a, t0, cut, t1 - t0)
             quantize_x(a, t0, t1)
-            if t1 == T and a == 1:
-                gather_words(1, 0, E, "gcodes1")
-        gather_words(0, 0, 1, "gcodes00")
+            if t1 == T:
+                gather_words(a, 0, E, f"gcodes{a}")
         gather_bytes(0, "gbytes0")
-        group_w("g", 0, 0, 0)
-        group_w("s", 0, 0, 1)
-        for u in range(2):
-            quantize_w(0, 0, u)
-        group_w("v", 0, 1, 0)
-        group_w("s", 0, 1, 1)
-        for u in range(2):
-            quantize_w(0, 1, u)
-            for t in (2 * u, 2 * u + 1):
-                multiply(0, 0, t)
-            for t in (2 * u, 2 * u + 1):
-                multiply(0, 1, t)
-                relu(0, t)
-        gather_words(0, 1, E, "wgrouped010")
-        gather_bytes(1, "wgrouped011")
-        group_w("v", 1, 0, 0)
-        group_w("s", 1, 0, 1)
-        apply_gate(nc.vector, 0, 0, 0, EARLY)
-        apply_gate(nc.gpsimd, 0, 1, 0, EARLY)
-        scatter(0, 0, 0, EARLY)
-        for u in range(2):
-            quantize_w(1, 0, u)
-        scatter(0, 1, 0, EARLY)
-        group_w("s", 1, 1, 0)
-        group_w("s", 1, 1, 1)
-        for u in range(2):
-            quantize_w(1, 1, u)
-            for t in (2 * u, 2 * u + 1):
-                multiply(1, 0, t)
-            for t in (2 * u, 2 * u + 1):
-                multiply(1, 1, t)
-                relu(1, t)
-        apply_gate(nc.vector, 0, 0, EARLY, C)
-        apply_gate(nc.gpsimd, 0, 1, EARLY, C)
-        scatter(0, 0, EARLY, C)
-        scatter(0, 1, EARLY, C)
-        apply_gate(nc.vector, 1, 0)
-        apply_gate(nc.gpsimd, 1, 1)
-        scatter(1, 0)
-        group_wp("s", 0, 0, 256)
-        group_wp("s", 1, 0, 256)
-        for q in range(CHUNKS):
-            weave("s", q, 0)
+        gather_bytes(1, "gbytes1")
+        for a in range(PASSES):
+            group_w("v" if a else "s", 0, a, 1)
+            group_w("s", 0, a, 0)
+            for u in (1, 0):
+                quantize_w(0, a, u)
+                for t in (2 * u, 2 * u + 1):
+                    multiply(0, a, t)
+                    if a == PASSES - 1:
+                        relu(0, t)
+        apply_gate(0, 1, "c01a", 0, 128)
+        apply_gate(0, 1, "c01b", 128, 256)
+        scatter(0, 1, 0, 128)
+        scatter(0, 1, 128, 256)
+        group_w("v", 1, 0, 1)
+        for a in range(PASSES):
+            for u in (1, 0):
+                if (a, u) != (0, 1):
+                    group_w("s", 1, a, u)
+                quantize_w(1, a, u)
+                for t in (2 * u, 2 * u + 1):
+                    multiply(1, a, t)
+                    if a == PASSES - 1:
+                        relu(1, t)
+        apply_gate(0, 0, "wgrouped111")
+        scatter(0, 0)
+        apply_gate(1, 1, "c11")
         scatter(1, 1)
-        weave("v", 0, 1)
-        quantize_wp(0, 256)
-        quantize_c(0)
-        quantize_wp(256, 512)
-        for q in range(1, CHUNKS):
-            weave("v", q, 1)
+        wpgrouped = keep.tile([P, M, J], BF16, name="wpgrouped", tag="wgrouped110", align_bytes=64)
+        wpcodes = keep.tile([P, M], U32, name="wpcodes", tag="y11", align_bytes=64)
+        apply_gate(1, 0, "c11")
+        for h in range(2):
+            group_wp("s", h, 0, 256)
+            quantize_wp(h * 256, h * 256 + 256)
+        nc.scalar.copy(out=window[0][:, T : 2 * T], in_=window[1][:])
+        scatter(1, 0)
+        for q in range(CHUNKS):
+            weave("s" if q == 1 else "v", q)
             quantize_c(q)
         for q in range(CHUNKS):
             for h in range(2):

@@ -24,6 +24,7 @@ PASSES = K // KP
 G = 4
 Q = 256
 CHUNKS = T // Q
+H = T // 2
 
 
 def tile_moe_nxt_lin_relu_kernel(tc, xT, w, b, wp, gate, offs, out):
@@ -35,9 +36,10 @@ def tile_moe_nxt_lin_relu_kernel(tc, xT, w, b, wp, gate, offs, out):
         offsets = keep.tile([P, S // 16], U16, name="offsets")
         bias = keep.tile([P, G * E], F32, name="bias", align_bytes=64)
 
-        x_chunks = [(1, 0, 512, 320), (1, 512, 1024, 320), (0, 0, 512, 192), (0, 512, 768, 64), (0, 768, 1024, 160)]
+        x_loads = [(1, 0, 1024), (0, 0, 1024)]
+        x_pieces = [(1, 0, 512, 352), (1, 512, 1024, 352), (0, 0, 512, 352), (0, 512, 1024, 288)]
         xraw = {}
-        for k, (a, t0, t1, cut) in enumerate(x_chunks):
+        for k, (a, t0, t1) in enumerate(x_loads):
             xraw[a, t0] = keep.tile([P, J, t1 - t0], F32, name=f"xraw{a}{t0}")
             src = xT[a * KP : (a + 1) * KP, t0:t1]
             nc.sync.dma_start(xraw[a, t0][:], src.rearrange("(p j) t -> p j t", j=J))
@@ -92,7 +94,7 @@ def tile_moe_nxt_lin_relu_kernel(tc, xT, w, b, wp, gate, offs, out):
         woven = [keep.tile([P, Q, 2], F32, name=f"woven{q}", align_bytes=64) for q in range(CHUNKS)]
         ccodes = [keep.tile([P, Q], U32, name=f"ccodes{q}", align_bytes=64) for q in range(CHUNKS)]
         cbytes = [keep.tile([P, Q], U8, name=f"cbytes{q}", align_bytes=64) for q in range(CHUNKS)]
-        result = [[keep.tile([P, 2, Q], F32, name=f"result{q}{h}", align_bytes=64) for h in range(2)] for q in range(CHUNKS)]
+        result = [[keep.tile([P, H], F32, name=f"result{h}{g}", align_bytes=64) for g in range(G)] for h in range(2)]
         ybank = [psum.tile([P, C], F32, name=f"ybank{t}", tag=f"bank{t}") for t in range(G)]
 
         def move(engine, dst, src):
@@ -103,11 +105,12 @@ def tile_moe_nxt_lin_relu_kernel(tc, xT, w, b, wp, gate, offs, out):
             else:
                 nc.gpsimd.tensor_scalar(dst, src, 1.0, 0.0, MULT, ADD)
 
-        def group_x(engine, a, t0, lo, hi):
+        def group_x(engine, a, lo, hi):
+            t0 = max(s for (pa, s, end) in x_loads if pa == a and s <= lo)
             move(
                 engine,
-                xgrouped[a][:, t0 + lo : t0 + hi, :].rearrange("p (c i) j -> p c j i", i=4),
-                xraw[a, t0][:, :, lo:hi].rearrange("p j (c i) -> p c j i", i=4),
+                xgrouped[a][:, lo:hi, :].rearrange("p (c i) j -> p c j i", i=4),
+                xraw[a, t0][:, :, lo - t0 : hi - t0].rearrange("p j (c i) -> p c j i", i=4),
             )
 
         def group_w(engine, e, a, u):
@@ -195,12 +198,12 @@ def tile_moe_nxt_lin_relu_kernel(tc, xT, w, b, wp, gate, offs, out):
                 in_=woven[q][:].rearrange("p t u -> p (t u)").bitcast(BF16),
             )
 
-        def project(engine, q, h):
-            bank = psum.tile([P, 2, Q], F32, name=f"obank{q}{h}", tag=f"bank{(4 + 2 * q + h) % 8}")
+        def project(engine, h, g):
+            bank = psum.tile([P, H], F32, name=f"obank{h}{g}", tag=f"bank{(4 + 4 * h + g) % 8}")
             for i in range(2):
-                g = 2 * h + i
+                q = 2 * h + i
                 nc.tensor.matmul_mx(
-                    out=bank[:, i, :],
+                    out=bank[:, i * Q : (i + 1) * Q],
                     lhsT=wpcodes[:, g * P : (g + 1) * P].bitcast(FP8X4),
                     lhsT_scale=wpbytes[:, g * P : (g + 1) * P],
                     rhs=ccodes[q][:].bitcast(FP8X4),
@@ -208,18 +211,18 @@ def tile_moe_nxt_lin_relu_kernel(tc, xT, w, b, wp, gate, offs, out):
                     start=True,
                     stop=True,
                 )
-            move(engine, result[q][h][:], bank[:])
-            rows = out[2 * h * P : (2 * h + 2) * P, q * Q : (q + 1) * Q]
-            nc.sync.dma_start(rows.rearrange("(i p) t -> p i t", p=P), result[q][h][:])
+            move(engine, result[h][g][:], bank[:])
+            nc.sync.dma_start(out[g * P : (g + 1) * P, h * H : (h + 1) * H], result[h][g][:])
 
-        for a, t0, t1, cut in x_chunks:
-            group_x("v", a, t0, 0, cut)
-            group_x("s", a, t0, cut, t1 - t0)
+        for a, t0, t1, cut in x_pieces:
+            if cut > 0:
+                group_x("v", a, t0, t0 + cut)
+            if t0 + cut < t1:
+                group_x("s", a, t0 + cut, t1)
             quantize_x(a, t0, t1)
             if t1 == T:
                 gather_words(a, 0, E, f"gcodes{a}")
         gather_bytes(0, "gbytes0")
-        gather_bytes(1, "gbytes1")
         for a in range(PASSES):
             group_w("v" if a else "s", 0, a, 1)
             group_w("s", 0, a, 0)
@@ -229,11 +232,10 @@ def tile_moe_nxt_lin_relu_kernel(tc, xT, w, b, wp, gate, offs, out):
                     multiply(0, a, t)
                     if a == PASSES - 1:
                         relu(0, t)
-        apply_gate(0, 1, "c01a", 0, 128)
-        apply_gate(0, 1, "c01b", 128, 256)
-        scatter(0, 1, 0, 128)
-        scatter(0, 1, 128, 256)
+        gather_bytes(1, "wgrouped010")
         group_w("v", 1, 0, 1)
+        apply_gate(0, 1, "c01a")
+        scatter(0, 1)
         for a in range(PASSES):
             for u in (1, 0):
                 if (a, u) != (0, 1):
@@ -258,6 +260,6 @@ def tile_moe_nxt_lin_relu_kernel(tc, xT, w, b, wp, gate, offs, out):
         for q in range(CHUNKS):
             weave("s" if q == 1 else "v", q)
             quantize_c(q)
-        for q in range(CHUNKS):
-            for h in range(2):
-                project("v" if q >= 2 and h == 1 else "s", q, h)
+        for h in range(2):
+            for g in range(G):
+                project("v" if h == 1 and g % 2 == 1 else "s", h, g)

@@ -24,7 +24,6 @@ PASSES = K // KP
 G = 4
 Q = 256
 CHUNKS = T // Q
-H = T // 2
 
 
 def tile_moe_nxt_lin_relu_kernel(tc, xT, w, b, wp, gate, offs, out):
@@ -36,8 +35,8 @@ def tile_moe_nxt_lin_relu_kernel(tc, xT, w, b, wp, gate, offs, out):
         offsets = keep.tile([P, S // 16], U16, name="offsets")
         bias = keep.tile([P, G * E], F32, name="bias", align_bytes=64)
 
-        x_loads = [(1, 0, 1024), (0, 0, 1024)]
-        x_pieces = [(1, 0, 512, 352), (1, 512, 1024, 352), (0, 0, 512, 352), (0, 512, 1024, 288)]
+        x_loads = [(1, 0, 1024), (0, 0, 512), (0, 512, 1024)]
+        x_pieces = [(1, 0, 512, 320), (1, 512, 1024, 320), (0, 0, 512, 128), (0, 512, 1024, 320)]
         xraw = {}
         for k, (a, t0, t1) in enumerate(x_loads):
             xraw[a, t0] = keep.tile([P, J, t1 - t0], F32, name=f"xraw{a}{t0}")
@@ -94,7 +93,6 @@ def tile_moe_nxt_lin_relu_kernel(tc, xT, w, b, wp, gate, offs, out):
         woven = [keep.tile([P, Q, 2], F32, name=f"woven{q}", align_bytes=64) for q in range(CHUNKS)]
         ccodes = [keep.tile([P, Q], U32, name=f"ccodes{q}", align_bytes=64) for q in range(CHUNKS)]
         cbytes = [keep.tile([P, Q], U8, name=f"cbytes{q}", align_bytes=64) for q in range(CHUNKS)]
-        result = [[keep.tile([P, H], F32, name=f"result{h}{g}", align_bytes=64) for g in range(G)] for h in range(2)]
         ybank = [psum.tile([P, C], F32, name=f"ybank{t}", tag=f"bank{t}") for t in range(G)]
 
         def move(engine, dst, src):
@@ -187,9 +185,9 @@ def tile_moe_nxt_lin_relu_kernel(tc, xT, w, b, wp, gate, offs, out):
                 c[e, u, s0][:].rearrange("p s t -> p (s t)").bitcast(F32),
             )
 
-        def weave(engine, q):
+        def weave(engine, q, lo=0, hi=Q):
             both = window[0][:].rearrange("p (u t) -> p t u", u=2)
-            move(engine, woven[q][:], both[:, q * Q : (q + 1) * Q, :])
+            move(engine, woven[q][:, lo:hi, :], both[:, q * Q + lo : q * Q + hi, :])
 
         def quantize_c(q):
             nc.vector.quantize_mx(
@@ -198,12 +196,12 @@ def tile_moe_nxt_lin_relu_kernel(tc, xT, w, b, wp, gate, offs, out):
                 in_=woven[q][:].rearrange("p t u -> p (t u)").bitcast(BF16),
             )
 
-        def project(engine, h, g):
-            bank = psum.tile([P, H], F32, name=f"obank{h}{g}", tag=f"bank{(4 + 4 * h + g) % 8}")
-            for i in range(2):
-                q = 2 * h + i
+        def project(engine, q0, q1, g, tag):
+            width = (q1 - q0) * Q
+            bank = psum.tile([P, width], F32, name=f"obank{q0}{g}", tag=tag)
+            for q in range(q0, q1):
                 nc.tensor.matmul_mx(
-                    out=bank[:, i * Q : (i + 1) * Q],
+                    out=bank[:, (q - q0) * Q : (q - q0 + 1) * Q],
                     lhsT=wpcodes[:, g * P : (g + 1) * P].bitcast(FP8X4),
                     lhsT_scale=wpbytes[:, g * P : (g + 1) * P],
                     rhs=ccodes[q][:].bitcast(FP8X4),
@@ -211,8 +209,9 @@ def tile_moe_nxt_lin_relu_kernel(tc, xT, w, b, wp, gate, offs, out):
                     start=True,
                     stop=True,
                 )
-            move(engine, result[h][g][:], bank[:])
-            nc.sync.dma_start(out[g * P : (g + 1) * P, h * H : (h + 1) * H], result[h][g][:])
+            result = keep.tile([P, width], F32, name=f"result{q0}{g}", align_bytes=64)
+            move(engine, result[:], bank[:])
+            nc.sync.dma_start(out[g * P : (g + 1) * P, q0 * Q : q1 * Q], result[:])
 
         for a, t0, t1, cut in x_pieces:
             if cut > 0:
@@ -224,7 +223,7 @@ def tile_moe_nxt_lin_relu_kernel(tc, xT, w, b, wp, gate, offs, out):
                 gather_words(a, 0, E, f"gcodes{a}")
         gather_bytes(0, "gbytes0")
         for a in range(PASSES):
-            group_w("v" if a else "s", 0, a, 1)
+            group_w("v" if a else "g", 0, a, 1)
             group_w("s", 0, a, 0)
             for u in (1, 0):
                 quantize_w(0, a, u)
@@ -257,9 +256,14 @@ def tile_moe_nxt_lin_relu_kernel(tc, xT, w, b, wp, gate, offs, out):
             quantize_wp(h * 256, h * 256 + 256)
         nc.scalar.copy(out=window[0][:, T : 2 * T], in_=window[1][:])
         scatter(1, 0)
-        for q in range(CHUNKS):
-            weave("s" if q == 1 else "v", q)
+        weave("v", 0, 0, 160)
+        weave("s", 0, 160, Q)
+        quantize_c(0)
+        for q in range(1, CHUNKS):
+            weave("v", q)
             quantize_c(q)
-        for h in range(2):
+        for q in range(2):
             for g in range(G):
-                project("v" if h == 1 and g % 2 == 1 else "s", h, g)
+                project("v" if q == 1 and g % 2 == 1 else "s", q, q + 1, g, f"bank{(4 + 4 * q + g) % 8}")
+        for g in range(G):
+            project("v" if g % 2 == 1 else "s", 2, 4, g, f"bank{4 + g}")

@@ -44,7 +44,7 @@ def tile_moe_nxt_lin_relu_kernel(tc, xT, w, b, wp, gate, offs, out):
             nc.sync.dma_start(xraw[a, t0][:], src.rearrange("(p j) t -> p j t", j=J))
             if k == 0:
                 nc.sync.dma_start(offsets[:], offs)
-                nc.sync.dma_start(bias[:], b.rearrange("(p t) e -> p (t e)", t=G))
+                nc.scalar.dma_start(bias[:], b.rearrange("(p t) e -> p (t e)", t=G))
         wraw = [[keep.tile([P, J, N], F32, name=f"wraw{e}{a}", align_bytes=64) for a in range(PASSES)] for e in range(E)]
         wpraw = [keep.tile([P, J, M // 2], F32, name=f"wpraw{h}") for h in range(2)]
         gates = [keep.tile([P, C], F32, name=f"gates{e}") for e in range(E)]
@@ -84,7 +84,10 @@ def tile_moe_nxt_lin_relu_kernel(tc, xT, w, b, wp, gate, offs, out):
             for e in range(E)
             for a in range(PASSES)
             for u in range(2)
+            if (e, a, u) != (1, 1, 1)
         }
+        spare = window[0][:, T : T + 2 * P * J // 2].bitcast(BF16)
+        wgrouped[1, 1, 1] = spare.rearrange("p (t m j) -> p t m j", t=2, j=J)
         wcodes = [[keep.tile([P, N], U32, name=f"wcodes{e}{a}", align_bytes=64) for a in range(PASSES)] for e in range(E)]
         wbytes = [[keep.tile([P, N], U8, name=f"wbytes{e}{a}", align_bytes=64) for a in range(PASSES)] for e in range(E)]
         wpbytes = keep.tile([P, M], U8, name="wpbytes", align_bytes=64)
@@ -196,22 +199,25 @@ def tile_moe_nxt_lin_relu_kernel(tc, xT, w, b, wp, gate, offs, out):
                 in_=woven[q][:].rearrange("p t u -> p (t u)").bitcast(BF16),
             )
 
-        def project(engine, q0, q1, g, tag):
+        def project(q0, q1, g0, engines, first_bank):
             width = (q1 - q0) * Q
-            bank = psum.tile([P, width], F32, name=f"obank{q0}{g}", tag=tag)
-            for q in range(q0, q1):
-                nc.tensor.matmul_mx(
-                    out=bank[:, (q - q0) * Q : (q - q0 + 1) * Q],
-                    lhsT=wpcodes[:, g * P : (g + 1) * P].bitcast(FP8X4),
-                    lhsT_scale=wpbytes[:, g * P : (g + 1) * P],
-                    rhs=ccodes[q][:].bitcast(FP8X4),
-                    rhs_scale=cbytes[q][:],
-                    start=True,
-                    stop=True,
-                )
-            result = keep.tile([P, width], F32, name=f"result{q0}{g}", align_bytes=64)
-            move(engine, result[:], bank[:])
-            nc.sync.dma_start(out[g * P : (g + 1) * P, q0 * Q : q1 * Q], result[:])
+            result = keep.tile([P, len(engines), width], F32, name=f"result{q0}{g0}", align_bytes=64)
+            for i, engine in enumerate(engines):
+                g = g0 + i
+                bank = psum.tile([P, width], F32, name=f"obank{q0}{g}", tag=f"bank{(first_bank + i) % 8}")
+                for q in range(q0, q1):
+                    nc.tensor.matmul_mx(
+                        out=bank[:, (q - q0) * Q : (q - q0 + 1) * Q],
+                        lhsT=wpcodes[:, g * P : (g + 1) * P].bitcast(FP8X4),
+                        lhsT_scale=wpbytes[:, g * P : (g + 1) * P],
+                        rhs=ccodes[q][:].bitcast(FP8X4),
+                        rhs_scale=cbytes[q][:],
+                        start=True,
+                        stop=True,
+                    )
+                move(engine, result[:, i, :], bank[:])
+            rows = out[g0 * P : (g0 + len(engines)) * P, q0 * Q : q1 * Q]
+            nc.sync.dma_start(rows.rearrange("(i p) t -> p i t", p=P), result[:])
 
         for a, t0, t1, cut in x_pieces:
             if cut > 0:
@@ -231,7 +237,7 @@ def tile_moe_nxt_lin_relu_kernel(tc, xT, w, b, wp, gate, offs, out):
                     multiply(0, a, t)
                     if a == PASSES - 1:
                         relu(0, t)
-        gather_bytes(1, "wgrouped010")
+        gather_bytes(1, "wraw01")
         group_w("v", 1, 0, 1)
         apply_gate(0, 1, "c01a")
         scatter(0, 1)
@@ -240,19 +246,21 @@ def tile_moe_nxt_lin_relu_kernel(tc, xT, w, b, wp, gate, offs, out):
                 if (a, u) != (0, 1):
                     group_w("s", 1, a, u)
                 quantize_w(1, a, u)
+                if (a, u) == (1, 0):
+                    wpgrouped = keep.tile([P, M, J], BF16, name="wpgrouped", tag="wraw11", align_bytes=64)
+                    for h in range(2):
+                        group_wp("s", h, 0, 256)
                 for t in (2 * u, 2 * u + 1):
                     multiply(1, a, t)
                     if a == PASSES - 1:
                         relu(1, t)
-        apply_gate(0, 0, "wgrouped111")
+        apply_gate(0, 0, "c00")
         scatter(0, 0)
         apply_gate(1, 1, "c11")
         scatter(1, 1)
-        wpgrouped = keep.tile([P, M, J], BF16, name="wpgrouped", tag="wgrouped110", align_bytes=64)
         wpcodes = keep.tile([P, M], U32, name="wpcodes", tag="y11", align_bytes=64)
         apply_gate(1, 0, "c11")
         for h in range(2):
-            group_wp("s", h, 0, 256)
             quantize_wp(h * 256, h * 256 + 256)
         nc.scalar.copy(out=window[0][:, T : 2 * T], in_=window[1][:])
         scatter(1, 0)
@@ -262,8 +270,10 @@ def tile_moe_nxt_lin_relu_kernel(tc, xT, w, b, wp, gate, offs, out):
         for q in range(1, CHUNKS):
             weave("v", q)
             quantize_c(q)
-        for q in range(2):
-            for g in range(G):
-                project("v" if q == 1 and g % 2 == 1 else "s", q, q + 1, g, f"bank{(4 + 4 * q + g) % 8}")
-        for g in range(G):
-            project("v" if g % 2 == 1 else "s", 2, 4, g, f"bank{4 + g}")
+        project(0, 1, 0, "s", 4)
+        project(0, 1, 1, "s", 5)
+        project(0, 1, 2, "ss", 6)
+        project(1, 2, 0, "ss", 0)
+        project(1, 2, 2, "sv", 2)
+        project(2, 4, 0, "sv", 4)
+        project(2, 4, 2, "sv", 6)

@@ -71,7 +71,7 @@ def tile_moe_nxt_lin_relu_kernel(tc, xT, w, b, wp, gate, offs, out):
 
         xbytes = keep.tile([P, T], U8, name="xbytes", align_bytes=64)
         nc.vector.memset(xbytes[:].bitcast(I32), 0)
-        window = [keep.tile([P, (2 - u) * T], F32, name=f"window{u}", align_bytes=64) for u in range(2)]
+        window = [keep.tile([P, T + (1 - u) * P * J], F32, name=f"window{u}", align_bytes=64) for u in range(2)]
         for u in range(2):
             nc.gpsimd.memset(window[u][:, 0:T], 0.0)
 
@@ -84,15 +84,16 @@ def tile_moe_nxt_lin_relu_kernel(tc, xT, w, b, wp, gate, offs, out):
             for e in range(E)
             for a in range(PASSES)
             for u in range(2)
-            if (e, a, u) != (1, 1, 1)
+            if (e, a, u) != (1, 1, 0)
         }
         spare = window[0][:, T : T + 2 * P * J // 2].bitcast(BF16)
-        wgrouped[1, 1, 1] = spare.rearrange("p (t m j) -> p t m j", t=2, j=J)
+        wgrouped[1, 1, 0] = spare.rearrange("p (t m j) -> p t m j", t=2, j=J)
         wcodes = [[keep.tile([P, N], U32, name=f"wcodes{e}{a}", align_bytes=64) for a in range(PASSES)] for e in range(E)]
         wbytes = [[keep.tile([P, N], U8, name=f"wbytes{e}{a}", align_bytes=64) for a in range(PASSES)] for e in range(E)]
         wpbytes = keep.tile([P, M], U8, name="wpbytes", align_bytes=64)
         y = [[keep.tile([P, 2, C], F32, name=f"y{e}{u}", align_bytes=64) for u in range(2)] for e in range(E)]
         c = {}
+        halves = [keep.tile([P, 2, Q], F32, name=f"halves{q}", align_bytes=64) for q in range(CHUNKS)]
         woven = [keep.tile([P, Q, 2], F32, name=f"woven{q}", align_bytes=64) for q in range(CHUNKS)]
         ccodes = [keep.tile([P, Q], U32, name=f"ccodes{q}", align_bytes=64) for q in range(CHUNKS)]
         cbytes = [keep.tile([P, Q], U8, name=f"cbytes{q}", align_bytes=64) for q in range(CHUNKS)]
@@ -173,9 +174,9 @@ def tile_moe_nxt_lin_relu_kernel(tc, xT, w, b, wp, gate, offs, out):
                 y[e][t // 2][:, t % 2, :], ybank[t][:], RELU, bias=bias[:, t * E + e : t * E + e + 1]
             )
 
-        def apply_gate(e, u, tag, s0=0, s1=C):
+        def apply_gate(e, u, tag, s0=0, s1=C, engine=nc.vector):
             c[e, u, s0] = keep.tile([P, s1 - s0, 2], BF16, name=f"c{e}{u}{s0}", tag=tag, align_bytes=64)
-            nc.vector.tensor_tensor(
+            engine.tensor_tensor(
                 out=c[e, u, s0][:],
                 in0=y[e][u][:, :, s0:s1].rearrange("p t s -> p s t"),
                 in1=gates[e][:, s0:s1].unsqueeze(2).to_broadcast([P, s1 - s0, 2]),
@@ -189,8 +190,10 @@ def tile_moe_nxt_lin_relu_kernel(tc, xT, w, b, wp, gate, offs, out):
             )
 
         def weave(engine, q, lo=0, hi=Q):
-            both = window[0][:].rearrange("p (u t) -> p t u", u=2)
-            move(engine, woven[q][:, lo:hi, :], both[:, q * Q + lo : q * Q + hi, :])
+            move(engine, woven[q][:, lo:hi, :], halves[q][:, :, lo:hi].rearrange("p u t -> p t u"))
+
+        def stage(engine, q, u):
+            move(engine, halves[q][:, u, :], window[u][:, q * Q : (q + 1) * Q])
 
         def quantize_c(q):
             nc.vector.quantize_mx(
@@ -244,36 +247,41 @@ def tile_moe_nxt_lin_relu_kernel(tc, xT, w, b, wp, gate, offs, out):
         for a in range(PASSES):
             for u in (1, 0):
                 if (a, u) != (0, 1):
-                    group_w("s", 1, a, u)
+                    group_w("v" if (a, u) == (1, 1) else "s", 1, a, u)
                 quantize_w(1, a, u)
-                if (a, u) == (1, 0):
-                    wpgrouped = keep.tile([P, M, J], BF16, name="wpgrouped", tag="wraw11", align_bytes=64)
-                    for h in range(2):
-                        group_wp("s", h, 0, 256)
                 for t in (2 * u, 2 * u + 1):
                     multiply(1, a, t)
                     if a == PASSES - 1:
                         relu(1, t)
-        apply_gate(0, 0, "c00")
+        apply_gate(0, 0, "wgrouped101", engine=nc.gpsimd)
         scatter(0, 0)
         apply_gate(1, 1, "c11")
         scatter(1, 1)
-        wpcodes = keep.tile([P, M], U32, name="wpcodes", tag="y11", align_bytes=64)
-        apply_gate(1, 0, "c11")
+        wpgrouped = keep.tile([P, M, J], BF16, name="wpgrouped", tag="bias", align_bytes=64)
+        wpcodes = keep.tile([P, M], U32, name="wpcodes", align_bytes=64)
+        apply_gate(1, 0, "y11", engine=nc.gpsimd)
         for h in range(2):
+            group_wp("s", h, 0, 256)
             quantize_wp(h * 256, h * 256 + 256)
-        nc.scalar.copy(out=window[0][:, T : 2 * T], in_=window[1][:])
+        for q in range(CHUNKS):
+            stage("s", q, 1)
         scatter(1, 0)
-        weave("v", 0, 0, 160)
-        weave("s", 0, 160, Q)
+        for q in range(CHUNKS):
+            stage("s" if q else "v", q, 0)
+        weave("v", 0)
         quantize_c(0)
         for q in range(1, CHUNKS):
             weave("v", q)
             quantize_c(q)
         project(0, 1, 0, "s", 4)
         project(0, 1, 1, "s", 5)
-        project(0, 1, 2, "ss", 6)
-        project(1, 2, 0, "ss", 0)
-        project(1, 2, 2, "sv", 2)
-        project(2, 4, 0, "sv", 4)
-        project(2, 4, 2, "sv", 6)
+        project(0, 1, 2, "s", 6)
+        project(0, 1, 3, "s", 7)
+        project(1, 2, 0, "s", 0)
+        project(1, 2, 1, "v", 1)
+        project(1, 2, 2, "s", 2)
+        project(1, 2, 3, "v", 3)
+        project(2, 4, 0, "s", 4)
+        project(2, 4, 1, "v", 5)
+        project(2, 4, 2, "s", 6)
+        project(2, 4, 3, "v", 7)

@@ -175,9 +175,10 @@ def tile_moe_nxt_lin_relu_kernel(tc, xT, w, b, wp, gate, offs, out):
             )
 
         def apply_gate(e, u, tag, s0=0, s1=C, engine=nc.vector):
-            c[e, u, s0] = keep.tile([P, s1 - s0, 2], BF16, name=f"c{e}{u}{s0}", tag=tag, align_bytes=64)
+            if s0 == 0:
+                c[e, u, 0] = keep.tile([P, C, 2], BF16, name=f"c{e}{u}", tag=tag, align_bytes=64)
             engine.tensor_tensor(
-                out=c[e, u, s0][:],
+                out=c[e, u, 0][:, s0:s1, :],
                 in0=y[e][u][:, :, s0:s1].rearrange("p t s -> p s t"),
                 in1=gates[e][:, s0:s1].unsqueeze(2).to_broadcast([P, s1 - s0, 2]),
                 op=MULT,
@@ -253,22 +254,24 @@ def tile_moe_nxt_lin_relu_kernel(tc, xT, w, b, wp, gate, offs, out):
                     multiply(1, a, t)
                     if a == PASSES - 1:
                         relu(1, t)
-        apply_gate(0, 0, "wgrouped101", engine=nc.gpsimd)
+        apply_gate(0, 0, "wgrouped101", 0, 208, nc.gpsimd)
+        apply_gate(0, 0, None, 208, C)
         scatter(0, 0)
         apply_gate(1, 1, "c11")
         scatter(1, 1)
         wpgrouped = keep.tile([P, M, J], BF16, name="wpgrouped", tag="bias", align_bytes=64)
         wpcodes = keep.tile([P, M], U32, name="wpcodes", align_bytes=64)
-        apply_gate(1, 0, "y11", engine=nc.gpsimd)
+        apply_gate(1, 0, "y11", 0, 256, nc.gpsimd)
         for h in range(2):
             group_wp("s", h, 0, 256)
             quantize_wp(h * 256, h * 256 + 256)
-        for q in range(CHUNKS):
+        move("s", woven[0][:, :, 1], window[1][:, 0:Q])
+        for q in range(1, CHUNKS):
             stage("s", q, 1)
         scatter(1, 0)
-        for q in range(CHUNKS):
-            stage("s" if q else "v", q, 0)
-        weave("v", 0)
+        move("v", woven[0][:, :, 0], window[0][:, 0:Q])
+        for q in range(1, CHUNKS):
+            stage("s", q, 0)
         quantize_c(0)
         for q in range(1, CHUNKS):
             weave("v", q)

@@ -115,10 +115,10 @@ def tile_moe_nxt_lin_relu_kernel(tc, xT, w, b, wp, gate, offs, out):
                 xraw[a, t0][:, :, lo - t0 : hi - t0].rearrange("p j (c i) -> p c j i", i=4),
             )
 
-        def group_w(engine, e, a, u):
+        def group_w(engine, e, a, u, m0=0, m1=P):
             order = "p m t j" if engine == "g" else "p m j t"
-            columns = wraw[e][a][:].rearrange("p j (m u t) -> p j m u t", u=2, t=2)[:, :, :, u, :]
-            move(engine, wgrouped[e, a, u][:].rearrange("p t m j -> " + order), columns.rearrange("p j m t -> " + order))
+            columns = wraw[e][a][:].rearrange("p j (m u t) -> p j m u t", u=2, t=2)[:, :, m0:m1, u, :]
+            move(engine, wgrouped[e, a, u][:, :, m0:m1, :].rearrange("p t m j -> " + order), columns.rearrange("p j m t -> " + order))
 
         def group_wp(engine, h, lo, hi):
             move(
@@ -248,7 +248,11 @@ def tile_moe_nxt_lin_relu_kernel(tc, xT, w, b, wp, gate, offs, out):
         for a in range(PASSES):
             for u in (1, 0):
                 if (a, u) != (0, 1):
-                    group_w("v" if (a, u) == (1, 1) else "s", 1, a, u)
+                    if (a, u) == (1, 0):
+                        group_w("v", 1, a, u, 0, 80)
+                        group_w("s", 1, a, u, 80, P)
+                    else:
+                        group_w("s", 1, a, u)
                 quantize_w(1, a, u)
                 for t in (2 * u, 2 * u + 1):
                     multiply(1, a, t)

@@ -84,10 +84,10 @@ def tile_moe_nxt_lin_relu_kernel(tc, xT, w, b, wp, gate, offs, out):
             for e in range(E)
             for a in range(PASSES)
             for u in range(2)
-            if (e, a, u) != (1, 1, 0)
+            if (e, a, u) != (1, 1, 1)
         }
         spare = window[0][:, T : T + 2 * P * J // 2].bitcast(BF16)
-        wgrouped[1, 1, 0] = spare.rearrange("p (t m j) -> p t m j", t=2, j=J)
+        wgrouped[1, 1, 1] = spare.rearrange("p (t m j) -> p t m j", t=2, j=J)
         wcodes = [[keep.tile([P, N], U32, name=f"wcodes{e}{a}", align_bytes=64) for a in range(PASSES)] for e in range(E)]
         wbytes = [[keep.tile([P, N], U8, name=f"wbytes{e}{a}", align_bytes=64) for a in range(PASSES)] for e in range(E)]
         wpbytes = keep.tile([P, M], U8, name="wpbytes", align_bytes=64)
@@ -196,32 +196,30 @@ def tile_moe_nxt_lin_relu_kernel(tc, xT, w, b, wp, gate, offs, out):
         def stage(engine, q, u):
             move(engine, halves[q][:, u, :], window[u][:, q * Q : (q + 1) * Q])
 
-        def quantize_c(q):
+        def quantize_c(q, lo=0, hi=Q):
             nc.vector.quantize_mx(
-                out=ccodes[q][:].bitcast(FP8X4),
-                scales=cbytes[q][:],
-                in_=woven[q][:].rearrange("p t u -> p (t u)").bitcast(BF16),
+                out=ccodes[q][:, lo:hi].bitcast(FP8X4),
+                scales=cbytes[q][:, lo:hi],
+                in_=woven[q][:, lo:hi, :].rearrange("p t u -> p (t u)").bitcast(BF16),
             )
 
-        def project(q0, q1, g0, engines, first_bank):
-            width = (q1 - q0) * Q
-            result = keep.tile([P, len(engines), width], F32, name=f"result{q0}{g0}", align_bytes=64)
-            for i, engine in enumerate(engines):
-                g = g0 + i
-                bank = psum.tile([P, width], F32, name=f"obank{q0}{g}", tag=f"bank{(first_bank + i) % 8}")
-                for q in range(q0, q1):
-                    nc.tensor.matmul_mx(
-                        out=bank[:, (q - q0) * Q : (q - q0 + 1) * Q],
-                        lhsT=wpcodes[:, g * P : (g + 1) * P].bitcast(FP8X4),
-                        lhsT_scale=wpbytes[:, g * P : (g + 1) * P],
-                        rhs=ccodes[q][:].bitcast(FP8X4),
-                        rhs_scale=cbytes[q][:],
-                        start=True,
-                        stop=True,
-                    )
-                move(engine, result[:, i, :], bank[:])
-            rows = out[g0 * P : (g0 + len(engines)) * P, q0 * Q : q1 * Q]
-            nc.sync.dma_start(rows.rearrange("(i p) t -> p i t", p=P), result[:])
+        def project(t0, t1, g, engine, number):
+            bank = psum.tile([P, t1 - t0], F32, name=f"obank{t0}{g}", tag=f"bank{number}")
+            for lo in range(t0, t1, Q):
+                hi = min(lo + Q, t1)
+                q = lo // Q
+                nc.tensor.matmul_mx(
+                    out=bank[:, lo - t0 : hi - t0],
+                    lhsT=wpcodes[:, g * P : (g + 1) * P].bitcast(FP8X4),
+                    lhsT_scale=wpbytes[:, g * P : (g + 1) * P],
+                    rhs=ccodes[q][:, lo - q * Q : hi - q * Q].bitcast(FP8X4),
+                    rhs_scale=cbytes[q][:, lo - q * Q : hi - q * Q],
+                    start=True,
+                    stop=True,
+                )
+            result = keep.tile([P, t1 - t0], F32, name=f"result{t0}{g}", align_bytes=64)
+            move(engine, result[:], bank[:])
+            nc.sync.dma_start(out[g * P : (g + 1) * P, t0:t1], result[:])
 
         for a, t0, t1, cut in x_pieces:
             if cut > 0:
@@ -249,8 +247,8 @@ def tile_moe_nxt_lin_relu_kernel(tc, xT, w, b, wp, gate, offs, out):
             for u in (1, 0):
                 if (a, u) != (0, 1):
                     if (a, u) == (1, 0):
-                        group_w("v", 1, a, u, 0, 80)
-                        group_w("s", 1, a, u, 80, P)
+                        group_w("v", 1, a, u, 0, 88)
+                        group_w("s", 1, a, u, 88, P)
                     else:
                         group_w("s", 1, a, u)
                 quantize_w(1, a, u)
@@ -273,22 +271,26 @@ def tile_moe_nxt_lin_relu_kernel(tc, xT, w, b, wp, gate, offs, out):
         for q in range(1, CHUNKS):
             stage("s", q, 1)
         scatter(1, 0)
-        move("v", woven[0][:, :, 0], window[0][:, 0:Q])
+        for lo in (0, Q // 2):
+            move("v", woven[0][:, lo : lo + Q // 2, 0], window[0][:, lo : lo + Q // 2])
+        for lo in (0, Q // 2):
+            quantize_c(0, lo, lo + Q // 2)
         for q in range(1, CHUNKS):
             stage("s", q, 0)
-        quantize_c(0)
         for q in range(1, CHUNKS):
             weave("v", q)
             quantize_c(q)
-        project(0, 1, 0, "s", 4)
-        project(0, 1, 1, "s", 5)
-        project(0, 1, 2, "s", 6)
-        project(0, 1, 3, "s", 7)
-        project(1, 2, 0, "s", 0)
-        project(1, 2, 1, "v", 1)
-        project(1, 2, 2, "s", 2)
-        project(1, 2, 3, "v", 3)
-        project(2, 4, 0, "s", 4)
-        project(2, 4, 1, "v", 5)
-        project(2, 4, 2, "s", 6)
-        project(2, 4, 3, "v", 7)
+        project(0, 128, 0, "s", 4)
+        project(0, 128, 1, "s", 5)
+        project(128, 256, 0, "s", 6)
+        project(128, 256, 1, "s", 7)
+        project(0, 256, 2, "s", 0)
+        project(0, 256, 3, "s", 1)
+        project(256, 512, 0, "s", 2)
+        project(256, 512, 1, "v", 3)
+        project(256, 512, 2, "s", 4)
+        project(256, 512, 3, "v", 5)
+        project(512, 1024, 0, "s", 6)
+        project(512, 1024, 1, "v", 7)
+        project(512, 1024, 2, "s", 0)
+        project(512, 1024, 3, "v", 1)

@@ -1,6 +1,7 @@
 from contextlib import ExitStack
 
 import concourse.mybir as mybir
+from concourse.masks import make_identity
 
 K, T, E, C, N, M = 1024, 1024, 2, 256, 512, 512
 S = E * C
@@ -24,6 +25,26 @@ PASSES = K // KP
 G = 4
 Q = 256
 CHUNKS = T // Q
+H = C // 2
+R = S // P
+GA = "v"
+CT = "c00"
+XV = 320
+XB = 128
+W01A = 88
+W01B = 48
+W00G = 104
+W11A = 128
+W11B = 32
+G0 = 208
+WARM = 0
+SW = ()
+SORDER = (1, 2, 3)
+WPTAG = "wpgrouped"
+WPC = [(0, 256), (256, 512)]
+MID = 0
+FIRST = 256
+PIECES = [(0,256,0,1,"s"),(0,256,1,2,"s"),(0,256,2,3,"s"),(0,256,3,4,"s"),(256,512,0,1,"s"),(256,512,1,2,"s"),(256,512,2,3,"s"),(256,512,3,4,"s"),(512,1024,0,1,"v"),(512,1024,1,2,"s"),(512,1024,2,3,"v"),(512,1024,3,4,"s")]
 
 
 def tile_moe_nxt_lin_relu_kernel(tc, xT, w, b, wp, gate, offs, out):
@@ -34,12 +55,14 @@ def tile_moe_nxt_lin_relu_kernel(tc, xT, w, b, wp, gate, offs, out):
 
         offsets = keep.tile([P, S // 16], U16, name="offsets")
         bias = keep.tile([P, G * E], F32, name="bias", align_bytes=64)
+        gate_row = keep.tile([P, S // P], F32, name="gate_row")
 
         x_loads = [(1, 0, 1024), (0, 0, 512), (0, 512, 1024)]
-        x_pieces = [(1, 0, 512, 320), (1, 512, 1024, 320), (0, 0, 512, 128), (0, 512, 1024, 320)]
+        x_pieces = [(1, 0, 512, XV), (1, 512, 1024, XV), (0, 0, 512, XB), (0, 512, 1024, XV)]
         xraw = {}
+        nc.scalar.dma_start(gate_row[:], gate[0, :].rearrange("(p c) -> p c", c=S // P))
         for k, (a, t0, t1) in enumerate(x_loads):
-            xraw[a, t0] = keep.tile([P, J, t1 - t0], F32, name=f"xraw{a}{t0}")
+            xraw[a, t0] = keep.tile([P, J, t1 - t0], F32, name=f"xraw{a}{t0}", align_bytes=64)
             src = xT[a * KP : (a + 1) * KP, t0:t1]
             nc.sync.dma_start(xraw[a, t0][:], src.rearrange("(p j) t -> p j t", j=J))
             if k == 0:
@@ -47,33 +70,26 @@ def tile_moe_nxt_lin_relu_kernel(tc, xT, w, b, wp, gate, offs, out):
                 nc.scalar.dma_start(bias[:], b.rearrange("(p t) e -> p (t e)", t=G))
         wraw = [[keep.tile([P, J, N], F32, name=f"wraw{e}{a}", align_bytes=64) for a in range(PASSES)] for e in range(E)]
         wpraw = [keep.tile([P, J, M // 2], F32, name=f"wpraw{h}") for h in range(2)]
-        gates = [keep.tile([P, C], F32, name=f"gates{e}") for e in range(E)]
-
-        def load_w(e, a):
-            nc.sync.dma_start(wraw[e][a][:], w[e, a * KP : (a + 1) * KP, :].rearrange("(p j) n -> p j n", j=J))
-
-        def load_wp(h):
+        for e in range(E):
+            for a in range(PASSES):
+                nc.sync.dma_start(wraw[e][a][:], w[e, a * KP : (a + 1) * KP, :].rearrange("(p j) n -> p j n", j=J))
+        for h in range(2):
             nc.sync.dma_start(wpraw[h][:], wp[:, h * 256 : (h + 1) * 256].rearrange("(p j) f -> p j f", j=J))
 
-        load_w(0, 0)
-        load_w(0, 1)
-        load_w(1, 0)
-        nc.sync.dma_start(gates[0][:], gate[0:P, 0:C])
-        load_w(1, 1)
-        nc.sync.dma_start(gates[1][:], gate[0:P, C:S])
-        load_wp(0)
-        load_wp(1)
-
-        warm = keep.tile([P, 8], F32, name="warm")
-        warmed = keep.tile([P, 8], F32, name="warmed")
-        nc.vector.memset(warm[:], 0.0)
-        nc.scalar.activation(warmed[:], warm[:], RELU)
+        identity = keep.tile([P, P], F32, name="identity")
+        make_identity(nc, identity[:])
+        gbank = psum.tile([P, S // P, P], F32, name="gbank", tag="bank6")
+        for r in range(S // P):
+            nc.tensor.transpose(gbank[:, r, :], gate_row[:, r : r + 1].to_broadcast([P, P]), identity[:])
 
         xbytes = keep.tile([P, T], U8, name="xbytes", align_bytes=64)
         nc.vector.memset(xbytes[:].bitcast(I32), 0)
         window = [keep.tile([P, T + (1 - u) * P * J], F32, name=f"window{u}", align_bytes=64) for u in range(2)]
-        for u in range(2):
-            nc.gpsimd.memset(window[u][:, 0:T], 0.0)
+        zeros = keep.tile([P, 8], F32, name="zeros")
+        nc.vector.memset(zeros[:], 0.0)
+        nc.scalar.activation(window[1][:, 0:8], zeros[:], RELU)
+        nc.gpsimd.memset(window[1][:, 8:T], 0.0)
+        nc.gpsimd.memset(window[0][:, 0:T], 0.0)
 
         xgrouped = [keep.tile([P, T, J], BF16, name=f"xgrouped{a}", align_bytes=64) for a in range(PASSES)]
         xcodes = [keep.tile([P, T], U32, name=f"xcodes{a}", align_bytes=64) for a in range(PASSES)]
@@ -84,12 +100,13 @@ def tile_moe_nxt_lin_relu_kernel(tc, xT, w, b, wp, gate, offs, out):
             for e in range(E)
             for a in range(PASSES)
             for u in range(2)
-            if (e, a, u) != (1, 1, 1)
+            if (e, a, u) != (1, 1, 0)
         }
         spare = window[0][:, T : T + 2 * P * J // 2].bitcast(BF16)
-        wgrouped[1, 1, 1] = spare.rearrange("p (t m j) -> p t m j", t=2, j=J)
-        wcodes = [[keep.tile([P, N], U32, name=f"wcodes{e}{a}", align_bytes=64) for a in range(PASSES)] for e in range(E)]
-        wbytes = [[keep.tile([P, N], U8, name=f"wbytes{e}{a}", align_bytes=64) for a in range(PASSES)] for e in range(E)]
+        wgrouped[1, 1, 0] = spare.rearrange("p (t m j) -> p t m j", t=2, j=J)
+        wcodes = {}
+        wbytes = {}
+        wpcodes = {}
         wpbytes = keep.tile([P, M], U8, name="wpbytes", align_bytes=64)
         y = [[keep.tile([P, 2, C], F32, name=f"y{e}{u}", align_bytes=64) for u in range(2)] for e in range(E)]
         c = {}
@@ -97,7 +114,7 @@ def tile_moe_nxt_lin_relu_kernel(tc, xT, w, b, wp, gate, offs, out):
         woven = [keep.tile([P, Q, 2], F32, name=f"woven{q}", align_bytes=64) for q in range(CHUNKS)]
         ccodes = [keep.tile([P, Q], U32, name=f"ccodes{q}", align_bytes=64) for q in range(CHUNKS)]
         cbytes = [keep.tile([P, Q], U8, name=f"cbytes{q}", align_bytes=64) for q in range(CHUNKS)]
-        ybank = [psum.tile([P, C], F32, name=f"ybank{t}", tag=f"bank{t}") for t in range(G)]
+        ybank = {}
 
         def move(engine, dst, src):
             if engine == "v":
@@ -116,15 +133,17 @@ def tile_moe_nxt_lin_relu_kernel(tc, xT, w, b, wp, gate, offs, out):
             )
 
         def group_w(engine, e, a, u, m0=0, m1=P):
+            if m0 == m1:
+                return
             order = "p m t j" if engine == "g" else "p m j t"
             columns = wraw[e][a][:].rearrange("p j (m u t) -> p j m u t", u=2, t=2)[:, :, m0:m1, u, :]
             move(engine, wgrouped[e, a, u][:, :, m0:m1, :].rearrange("p t m j -> " + order), columns.rearrange("p j m t -> " + order))
 
-        def group_wp(engine, h, lo, hi):
+        def group_wp(engine, lo, hi):
             move(
                 engine,
-                wpgrouped[:, h * 256 + lo : h * 256 + hi, :].rearrange("p (c i) j -> p c j i", i=4),
-                wpraw[h][:, :, lo:hi].rearrange("p j (c i) -> p c j i", i=4),
+                wpgrouped[:, lo:hi, :].rearrange("p (c i) j -> p c j i", i=4),
+                wpraw[lo // 256][:, :, lo % 256 : lo % 256 + hi - lo].rearrange("p j (c i) -> p c j i", i=4),
             )
 
         def quantize_x(a, t0, t1):
@@ -134,18 +153,20 @@ def tile_moe_nxt_lin_relu_kernel(tc, xT, w, b, wp, gate, offs, out):
                 in_=xgrouped[a][:, t0:t1, :].rearrange("p t j -> p (t j)"),
             )
 
-        def quantize_w(e, a, u):
+        def quantize_w(e, a, u, tag=None):
+            wcodes[e, a, u] = keep.tile([P, 2 * P], U32, name=f"wcodes{e}{a}{u}", tag=tag or f"wcodes{e}{a}{u}", align_bytes=64)
+            wbytes[e, a, u] = keep.tile([P, 2 * P], U8, name=f"wbytes{e}{a}{u}", align_bytes=64)
             nc.vector.quantize_mx(
-                out=wcodes[e][a][:, u * 2 * P : (u + 1) * 2 * P].bitcast(FP8X4),
-                scales=wbytes[e][a][:, u * 2 * P : (u + 1) * 2 * P],
+                out=wcodes[e, a, u][:].bitcast(FP8X4),
+                scales=wbytes[e, a, u][:],
                 in_=wgrouped[e, a, u][:].rearrange("p t m j -> p (t m j)"),
             )
 
-        def quantize_wp(f0, f1):
+        def quantize_wp(h):
             nc.vector.quantize_mx(
-                out=wpcodes[:, f0:f1].bitcast(FP8X4),
-                scales=wpbytes[:, f0:f1],
-                in_=wpgrouped[:, f0:f1, :].rearrange("p f j -> p (f j)"),
+                out=wpcodes[h].bitcast(FP8X4),
+                scales=wpbytes[:, h * 256 : (h + 1) * 256],
+                in_=wpgrouped[:, h * 256 : (h + 1) * 256, :].rearrange("p f j -> p (f j)"),
             )
 
         def gather_words(a, e0, e1, tag):
@@ -158,36 +179,59 @@ def tile_moe_nxt_lin_relu_kernel(tc, xT, w, b, wp, gate, offs, out):
             gbytes[e] = keep.tile([P, C], U8, name=f"gbytes{e}", tag=tag, align_bytes=64)
             nc.vector.tensor_copy(gbytes[e][:], xbytes[:].indirect(offsets[:, e * 16 : (e + 1) * 16]))
 
-        def multiply(e, a, t):
+        def multiply(e, a, t, s0, s1, number):
+            if a == 0:
+                ybank[e, t, s0] = psum.tile([P, s1 - s0], F32, name=f"ybank{e}{t}{s0}", tag=f"bank{number}")
             nc.tensor.matmul_mx(
-                out=ybank[t][:],
-                lhsT=wcodes[e][a][:, t * P : (t + 1) * P].bitcast(FP8X4),
-                lhsT_scale=wbytes[e][a][:, t * P : (t + 1) * P],
-                rhs=gcodes[a, e].bitcast(FP8X4),
-                rhs_scale=gbytes[e][4 * a :, :],
+                out=ybank[e, t, s0][:],
+                lhsT=wcodes[e, a, t // 2][:, t % 2 * P : (t % 2 + 1) * P].bitcast(FP8X4),
+                lhsT_scale=wbytes[e, a, t // 2][:, t % 2 * P : (t % 2 + 1) * P],
+                rhs=gcodes[a, e][:, s0:s1].bitcast(FP8X4),
+                rhs_scale=gbytes[e][4 * a :, s0:s1],
                 start=(a == 0),
                 stop=(a == PASSES - 1),
             )
 
-        def relu(e, t):
+        def relu(e, t, s0, s1):
             nc.scalar.activation(
-                y[e][t // 2][:, t % 2, :], ybank[t][:], RELU, bias=bias[:, t * E + e : t * E + e + 1]
+                y[e][t // 2][:, t % 2, s0:s1], ybank[e, t, s0][:], RELU, bias=bias[:, t * E + e : t * E + e + 1]
             )
 
-        def apply_gate(e, u, tag, s0=0, s1=C, engine=nc.vector):
-            if s0 == 0:
-                c[e, u, 0] = keep.tile([P, C, 2], BF16, name=f"c{e}{u}", tag=tag, align_bytes=64)
-            engine.tensor_tensor(
-                out=c[e, u, 0][:, s0:s1, :],
-                in0=y[e][u][:, :, s0:s1].rearrange("p t s -> p s t"),
-                in1=gates[e][:, s0:s1].unsqueeze(2).to_broadcast([P, s1 - s0, 2]),
+        def expert_pair(e, a, u, cuts):
+            for s0, s1, first in cuts:
+                for t in (2 * u, 2 * u + 1):
+                    multiply(e, a, t, s0, s1, first + t % 2)
+                    if a == PASSES - 1:
+                        relu(e, t, s0, s1)
+
+        def gate_vector(e, u, s0, s1):
+            shape = [P, (s1 - s0) // R, R, 2]
+            nc.vector.tensor_tensor(
+                out=c[e, u, s0][:].rearrange("p (m r) t -> p m r t", r=R),
+                in0=y[e][u][:, :, s0:s1].rearrange("p t (m r) -> p m r t", r=R),
+                in1=gbank[:, :, (e * C + s0) // R : (e * C + s1) // R].rearrange("p r m -> p m r").unsqueeze(3).to_broadcast(shape),
                 op=MULT,
             )
 
-        def scatter(e, u, s0=0, s1=C):
+        def gate_gpsimd(e, u, s0, s1):
+            nc.gpsimd.tensor_tensor(
+                out=c[e, u, s0][:],
+                in0=y[e][u][:, :, s0:s1].rearrange("p t s -> p s t"),
+                in1=gates[:, e * C + s0 : e * C + s1].unsqueeze(2).to_broadcast([P, s1 - s0, 2]),
+                op=MULT,
+            )
+
+        def apply_gate(engine, e, u, s0, s1, tag=None, part=None):
+            if part is None:
+                c[e, u, s0] = keep.tile([P, s1 - s0, 2], BF16, name=f"c{e}{u}{s0}", tag=tag or f"c{e}{u}{s0}", align_bytes=64)
+            else:
+                c[e, u, s0] = part[:, s0:s1, :]
+            (gate_vector if engine == "v" else gate_gpsimd)(e, u, s0, s1)
+
+        def scatter(e, u, s0, s1, values):
             nc.vector.tensor_copy(
                 window[u][:].indirect(offsets[:, (e * C + s0) // 16 : (e * C + s1) // 16]),
-                c[e, u, s0][:].rearrange("p s t -> p (s t)").bitcast(F32),
+                values.rearrange("p s t -> p (s t)").bitcast(F32),
             )
 
         def weave(engine, q, lo=0, hi=Q):
@@ -203,94 +247,115 @@ def tile_moe_nxt_lin_relu_kernel(tc, xT, w, b, wp, gate, offs, out):
                 in_=woven[q][:, lo:hi, :].rearrange("p t u -> p (t u)").bitcast(BF16),
             )
 
-        def project(t0, t1, g, engine, number):
-            bank = psum.tile([P, t1 - t0], F32, name=f"obank{t0}{g}", tag=f"bank{number}")
-            for lo in range(t0, t1, Q):
-                hi = min(lo + Q, t1)
-                q = lo // Q
-                nc.tensor.matmul_mx(
-                    out=bank[:, lo - t0 : hi - t0],
-                    lhsT=wpcodes[:, g * P : (g + 1) * P].bitcast(FP8X4),
-                    lhsT_scale=wpbytes[:, g * P : (g + 1) * P],
-                    rhs=ccodes[q][:, lo - q * Q : hi - q * Q].bitcast(FP8X4),
-                    rhs_scale=cbytes[q][:, lo - q * Q : hi - q * Q],
-                    start=True,
-                    stop=True,
-                )
-            result = keep.tile([P, t1 - t0], F32, name=f"result{t0}{g}", align_bytes=64)
+        def project(t0, t1, g0, g1, engine, number):
+            width = t1 - t0
+            bank = psum.tile([P, g1 - g0, width], F32, name=f"obank{t0}{g0}", tag=f"bank{number}")
+            for g in range(g0, g1):
+                for lo in range(t0, t1, Q):
+                    hi = min(lo + Q, t1)
+                    q = lo // Q
+                    nc.tensor.matmul_mx(
+                        out=bank[:, g - g0, lo - t0 : hi - t0],
+                        lhsT=wpcodes[g // 2][:, g % 2 * P : (g % 2 + 1) * P].bitcast(FP8X4),
+                        lhsT_scale=wpbytes[:, g * P : (g + 1) * P],
+                        rhs=ccodes[q][:, lo - q * Q : hi - q * Q].bitcast(FP8X4),
+                        rhs_scale=cbytes[q][:, lo - q * Q : hi - q * Q],
+                        start=True,
+                        stop=True,
+                    )
+            result = keep.tile([P, g1 - g0, width], F32, name=f"result{t0}{g0}", align_bytes=64)
             move(engine, result[:], bank[:])
-            nc.sync.dma_start(out[g * P : (g + 1) * P, t0:t1], result[:])
+            nc.sync.dma_start(out[g0 * P : g1 * P, t0:t1].rearrange("(g p) t -> p g t", p=P), result[:])
 
         for a, t0, t1, cut in x_pieces:
-            if cut > 0:
-                group_x("v", a, t0, t0 + cut)
-            if t0 + cut < t1:
-                group_x("s", a, t0 + cut, t1)
+            group_x("v", a, t0, t0 + cut)
+            group_x("s", a, t0 + cut, t1)
             quantize_x(a, t0, t1)
             if t1 == T:
                 gather_words(a, 0, E, f"gcodes{a}")
+        gates = keep.tile([P, S], F32, name="gates", tag="xraw10", align_bytes=64)
+        nc.scalar.copy(out=gates[:].rearrange("p (m r) -> p m r", r=R), in_=gbank[:].rearrange("p r m -> p m r"))
         gather_bytes(0, "gbytes0")
-        for a in range(PASSES):
-            group_w("v" if a else "g", 0, a, 1)
-            group_w("s", 0, a, 0)
-            for u in (1, 0):
-                quantize_w(0, a, u)
-                for t in (2 * u, 2 * u + 1):
-                    multiply(0, a, t)
-                    if a == PASSES - 1:
-                        relu(0, t)
+        early = [(0, H, 2), (H, C, 4)]
+        late = [(0, C, 0)]
+        group_w("g", 0, 0, 1, 0, W00G)
+        group_w("s", 0, 0, 0)
+        group_w("s", 0, 0, 1, W00G, P)
+        quantize_w(0, 0, 0)
+        expert_pair(0, 0, 0, late)
+        quantize_w(0, 0, 1)
+        expert_pair(0, 0, 1, early)
+        group_w("v", 0, 1, 1, 0, W01A)
+        group_w("s", 0, 1, 1, W01A, P)
+        group_w("v", 0, 1, 0, 0, W01B)
+        group_w("s", 0, 1, 0, W01B, P)
+        quantize_w(0, 1, 1)
+        expert_pair(0, 1, 1, early)
+        quantize_w(0, 1, 0)
+        expert_pair(0, 1, 0, late)
         gather_bytes(1, "wraw01")
-        group_w("v", 1, 0, 1)
-        apply_gate(0, 1, "c01a")
-        scatter(0, 1)
-        for a in range(PASSES):
-            for u in (1, 0):
-                if (a, u) != (0, 1):
-                    if (a, u) == (1, 0):
-                        group_w("v", 1, a, u, 0, 88)
-                        group_w("s", 1, a, u, 88, P)
-                    else:
-                        group_w("s", 1, a, u)
-                quantize_w(1, a, u)
-                for t in (2 * u, 2 * u + 1):
-                    multiply(1, a, t)
-                    if a == PASSES - 1:
-                        relu(1, t)
-        apply_gate(0, 0, "wgrouped101", 0, 208, nc.gpsimd)
-        apply_gate(0, 0, None, 208, C)
-        scatter(0, 0)
-        apply_gate(1, 1, "c11")
-        scatter(1, 1)
-        wpgrouped = keep.tile([P, M, J], BF16, name="wpgrouped", tag="bias", align_bytes=64)
-        wpcodes = keep.tile([P, M], U32, name="wpcodes", align_bytes=64)
-        apply_gate(1, 0, "y11", 0, 256, nc.gpsimd)
-        for h in range(2):
-            group_wp("s", h, 0, 256)
-            quantize_wp(h * 256, h * 256 + 256)
+        c01 = keep.tile([P, C, 2], BF16, name="c01", align_bytes=64)
+        apply_gate("v", 0, 1, 0, H, part=c01)
+        apply_gate("v", 0, 1, H, C, part=c01)
+        scatter(0, 1, 0, C, c01[:])
+        c00 = keep.tile([P, C, 2], BF16, name="c00", tag=CT, align_bytes=64)
+        apply_gate("g", 0, 0, 0, G0, part=c00)
+        apply_gate("v", 0, 0, G0, C, part=c00)
+        group_w("s", 1, 0, 1)
+        group_w("s", 1, 0, 0)
+        quantize_w(1, 0, 1)
+        expert_pair(1, 0, 1, early)
+        group_w("v", 1, 1, 1, 0, W11A)
+        group_w("s", 1, 1, 1, W11A, P)
+        group_w("v", 1, 1, 0, 0, W11B)
+        group_w("s", 1, 1, 0, W11B, P)
+        quantize_w(1, 1, 1)
+        expert_pair(1, 1, 1, early)
+        quantize_w(1, 1, 0)
+        quantize_w(1, 0, 0, "wgrouped111")
+        expert_pair(1, 0, 0, late)
+        expert_pair(1, 1, 0, late)
+        scatter(0, 0, 0, C, c00[:])
+        wpgrouped = keep.tile([P, M, J], BF16, name="wpgrouped", tag=WPTAG, align_bytes=64)
+        for lo, hi in WPC:
+            group_wp("s", lo, hi)
+        c11 = keep.tile([P, C, 2], BF16, name="c11", align_bytes=64)
+        apply_gate("g", 1, 1, 0, H, part=c11)
+        apply_gate("v", 1, 1, H, C, part=c11)
+        apply_gate("g", 1, 0, 0, C)
+        scatter(1, 1, 0, C, c11[:])
         move("s", woven[0][:, :, 1], window[1][:, 0:Q])
         for q in range(1, CHUNKS):
             stage("s", q, 1)
-        scatter(1, 0)
-        for lo in (0, Q // 2):
-            move("v", woven[0][:, lo : lo + Q // 2, 0], window[0][:, lo : lo + Q // 2])
-        for lo in (0, Q // 2):
-            quantize_c(0, lo, lo + Q // 2)
-        for q in range(1, CHUNKS):
+        if MID:
+            wpcodes[0] = keep.tile([P, 256], U32, name="wpcodes0", tag="c11", align_bytes=64)[:]
+            quantize_wp(0)
+        scatter(1, 0, 0, C, c[1, 0, 0][:])
+        last = keep.tile([P, 512], U32, name="wpcodes1", tag="c100", align_bytes=64)
+        wpcodes[1] = last[:, 0:256]
+        for n in range(WARM):
+            idle = psum.tile([P, C], F32, name=f"idle{n}", tag="bank6")
+            nc.tensor.matmul_mx(out=idle[:], lhsT=wpcodes[0][:, 0:P].bitcast(FP8X4), lhsT_scale=wpbytes[:, 0:P], rhs=wpcodes[0].bitcast(FP8X4), rhs_scale=wpbytes[:, 0:C], start=True, stop=True)
+        move("v", woven[0][:, 0:FIRST, 0], window[0][:, 0:FIRST])
+        if MID:
+            quantize_wp(1)
+        else:
+            wpcodes[0] = last[:, 256:512]
+            quantize_wp(0)
+        quantize_c(0, 0, FIRST)
+        if FIRST < Q:
+            move("v", woven[0][:, 128:256, 0], window[0][:, 128:256])
+        if not MID:
+            quantize_wp(1)
+        for q in SORDER:
             stage("s", q, 0)
-        for q in range(1, CHUNKS):
-            weave("v", q)
-            quantize_c(q)
-        project(0, 128, 0, "s", 4)
-        project(0, 128, 1, "s", 5)
-        project(128, 256, 0, "s", 6)
-        project(128, 256, 1, "s", 7)
-        project(0, 256, 2, "s", 0)
-        project(0, 256, 3, "s", 1)
-        project(256, 512, 0, "s", 2)
-        project(256, 512, 1, "v", 3)
-        project(256, 512, 2, "s", 4)
-        project(256, 512, 3, "v", 5)
-        project(512, 1024, 0, "s", 6)
-        project(512, 1024, 1, "v", 7)
-        project(512, 1024, 2, "s", 0)
-        project(512, 1024, 3, "v", 1)
+        if FIRST < Q:
+            quantize_c(0, 128, 256)
+        weave("v", 1)
+        weave("v", 2)
+        quantize_c(1)
+        weave("v", 3)
+        quantize_c(2)
+        quantize_c(3)
+        for n, (t0, t1, g0, g1, eng) in enumerate(PIECES):
+            project(t0, t1, g0, g1, eng, (n + 7) % 8)

@@ -35,8 +35,8 @@ W01A = 88
 W01B = 48
 W00G = 104
 W11A = 128
-W11B = 32
-G0 = 208
+W11B = 40
+G0 = 224
 WARM = 0
 SW = ()
 SORDER = (1, 2, 3)
@@ -215,9 +215,9 @@ def tile_moe_nxt_lin_relu_kernel(tc, xT, w, b, wp, gate, offs, out):
 
         def gate_gpsimd(e, u, s0, s1):
             nc.gpsimd.tensor_tensor(
-                out=c[e, u, s0][:],
-                in0=y[e][u][:, :, s0:s1].rearrange("p t s -> p s t"),
-                in1=gates[:, e * C + s0 : e * C + s1].unsqueeze(2).to_broadcast([P, s1 - s0, 2]),
+                out=c[e, u, s0][:].rearrange("p s t -> p t s"),
+                in0=y[e][u][:, :, s0:s1],
+                in1=gates[:, e * C + s0 : e * C + s1].unsqueeze(1).to_broadcast([P, 2, s1 - s0]),
                 op=MULT,
             )
 
@@ -300,7 +300,8 @@ def tile_moe_nxt_lin_relu_kernel(tc, xT, w, b, wp, gate, offs, out):
         scatter(0, 1, 0, C, c01[:])
         c00 = keep.tile([P, C, 2], BF16, name="c00", tag=CT, align_bytes=64)
         apply_gate("g", 0, 0, 0, G0, part=c00)
-        apply_gate("v", 0, 0, G0, C, part=c00)
+        if G0 < C:
+            apply_gate("v", 0, 0, G0, C, part=c00)
         group_w("s", 1, 0, 1)
         group_w("s", 1, 0, 0)
         quantize_w(1, 0, 1)

@@ -34,9 +34,16 @@ XB = 128
 W01A = 88
 W01B = 48
 W00G = 104
-W11A = 128
-W11B = 40
-G0 = 224
+W11A = 0
+W11B = 88
+G0 = 208
+B1 = 48
+Q2 = 1
+WG = 320
+A1 = 96
+W10G = 96
+GU = 0
+W1 = 0
 WARM = 0
 SW = ()
 SORDER = (1, 2, 3)
@@ -100,13 +107,12 @@ def tile_moe_nxt_lin_relu_kernel(tc, xT, w, b, wp, gate, offs, out):
             for e in range(E)
             for a in range(PASSES)
             for u in range(2)
-            if (e, a, u) != (1, 1, 0)
+            if (e, a, u) != (1, 1, 1)
         }
         spare = window[0][:, T : T + 2 * P * J // 2].bitcast(BF16)
-        wgrouped[1, 1, 0] = spare.rearrange("p (t m j) -> p t m j", t=2, j=J)
+        wgrouped[1, 1, 1] = spare.rearrange("p (t m j) -> p t m j", t=2, j=J)
         wcodes = {}
         wbytes = {}
-        wpcodes = {}
         wpbytes = keep.tile([P, M], U8, name="wpbytes", align_bytes=64)
         y = [[keep.tile([P, 2, C], F32, name=f"y{e}{u}", align_bytes=64) for u in range(2)] for e in range(E)]
         c = {}
@@ -140,10 +146,11 @@ def tile_moe_nxt_lin_relu_kernel(tc, xT, w, b, wp, gate, offs, out):
             move(engine, wgrouped[e, a, u][:, :, m0:m1, :].rearrange("p t m j -> " + order), columns.rearrange("p j m t -> " + order))
 
         def group_wp(engine, lo, hi):
+            order = "p c i j" if engine == "g" else "p c j i"
             move(
                 engine,
-                wpgrouped[:, lo:hi, :].rearrange("p (c i) j -> p c j i", i=4),
-                wpraw[lo // 256][:, :, lo % 256 : lo % 256 + hi - lo].rearrange("p j (c i) -> p c j i", i=4),
+                wpgrouped[lo // P][:, lo % P : lo % P + hi - lo, :].rearrange("p (c i) j -> " + order, i=4),
+                wpraw[lo // 256][:, :, lo % 256 : lo % 256 + hi - lo].rearrange("p j (c i) -> " + order, i=4),
             )
 
         def quantize_x(a, t0, t1):
@@ -162,11 +169,11 @@ def tile_moe_nxt_lin_relu_kernel(tc, xT, w, b, wp, gate, offs, out):
                 in_=wgrouped[e, a, u][:].rearrange("p t m j -> p (t m j)"),
             )
 
-        def quantize_wp(h):
+        def quantize_wp(g0, g1):
             nc.vector.quantize_mx(
-                out=wpcodes[h].bitcast(FP8X4),
-                scales=wpbytes[:, h * 256 : (h + 1) * 256],
-                in_=wpgrouped[:, h * 256 : (h + 1) * 256, :].rearrange("p f j -> p (f j)"),
+                out=wpcodes[:, g0 * P : g1 * P].bitcast(FP8X4),
+                scales=wpbytes[:, g0 * P : g1 * P],
+                in_=wpgrouped[g0][:, 0 : (g1 - g0) * P, :].rearrange("p f j -> p (f j)"),
             )
 
         def gather_words(a, e0, e1, tag):
@@ -180,10 +187,10 @@ def tile_moe_nxt_lin_relu_kernel(tc, xT, w, b, wp, gate, offs, out):
             nc.vector.tensor_copy(gbytes[e][:], xbytes[:].indirect(offsets[:, e * 16 : (e + 1) * 16]))
 
         def multiply(e, a, t, s0, s1, number):
-            if a == 0:
-                ybank[e, t, s0] = psum.tile([P, s1 - s0], F32, name=f"ybank{e}{t}{s0}", tag=f"bank{number}")
+            if a == 0 and number is not None:
+                ybank[e, t, s0] = psum.tile([P, s1 - s0], F32, name=f"ybank{e}{t}{s0}", tag=f"bank{number}")[:]
             nc.tensor.matmul_mx(
-                out=ybank[e, t, s0][:],
+                out=ybank[e, t, s0],
                 lhsT=wcodes[e, a, t // 2][:, t % 2 * P : (t % 2 + 1) * P].bitcast(FP8X4),
                 lhsT_scale=wbytes[e, a, t // 2][:, t % 2 * P : (t % 2 + 1) * P],
                 rhs=gcodes[a, e][:, s0:s1].bitcast(FP8X4),
@@ -194,7 +201,7 @@ def tile_moe_nxt_lin_relu_kernel(tc, xT, w, b, wp, gate, offs, out):
 
         def relu(e, t, s0, s1):
             nc.scalar.activation(
-                y[e][t // 2][:, t % 2, s0:s1], ybank[e, t, s0][:], RELU, bias=bias[:, t * E + e : t * E + e + 1]
+                y[e][t // 2][:, t % 2, s0:s1], ybank[e, t, s0], RELU, bias=bias[:, t * E + e : t * E + e + 1]
             )
 
         def expert_pair(e, a, u, cuts):
@@ -220,6 +227,15 @@ def tile_moe_nxt_lin_relu_kernel(tc, xT, w, b, wp, gate, offs, out):
                 in1=gates[:, e * C + s0 : e * C + s1].unsqueeze(1).to_broadcast([P, 2, s1 - s0]),
                 op=MULT,
             )
+
+        def late_pair(e, s0, s1, number):
+            bank = psum.tile([P, 2, s1 - s0], F32, name=f"late{e}{s0}", tag=f"bank{number}")
+            for t in range(2):
+                ybank[e, t, s0] = bank[:, t, :]
+                for a in range(PASSES):
+                    multiply(e, a, t, s0, s1, None)
+            for t in range(2):
+                relu(e, t, s0, s1)
 
         def apply_gate(engine, e, u, s0, s1, tag=None, part=None):
             if part is None:
@@ -256,7 +272,7 @@ def tile_moe_nxt_lin_relu_kernel(tc, xT, w, b, wp, gate, offs, out):
                     q = lo // Q
                     nc.tensor.matmul_mx(
                         out=bank[:, g - g0, lo - t0 : hi - t0],
-                        lhsT=wpcodes[g // 2][:, g % 2 * P : (g % 2 + 1) * P].bitcast(FP8X4),
+                        lhsT=wpcodes[:, g * P : (g + 1) * P].bitcast(FP8X4),
                         lhsT_scale=wpbytes[:, g * P : (g + 1) * P],
                         rhs=ccodes[q][:, lo - q * Q : hi - q * Q].bitcast(FP8X4),
                         rhs_scale=cbytes[q][:, lo - q * Q : hi - q * Q],
@@ -302,10 +318,16 @@ def tile_moe_nxt_lin_relu_kernel(tc, xT, w, b, wp, gate, offs, out):
         apply_gate("g", 0, 0, 0, G0, part=c00)
         if G0 < C:
             apply_gate("v", 0, 0, G0, C, part=c00)
-        group_w("s", 1, 0, 1)
-        group_w("s", 1, 0, 0)
+        group_w("g", 1, 0, GU, 0, W10G)
+        group_w("s", 1, 0, 1 - GU)
+        group_w("s", 1, 0, GU, W10G, P)
         quantize_w(1, 0, 1)
+        for n in range(W1):
+            idle = psum.tile([P, C], F32, name=f"idle1{n}", tag="bank7")
+            nc.tensor.matmul_mx(out=idle[:], lhsT=wcodes[1, 0, 1][:, 0:P].bitcast(FP8X4), lhsT_scale=wbytes[1, 0, 1][:, 0:P], rhs=wcodes[1, 0, 1][:].bitcast(FP8X4), rhs_scale=wbytes[1, 0, 1][:], start=True, stop=True)
         expert_pair(1, 0, 1, early)
+        quantize_w(1, 0, 0)
+        expert_pair(1, 0, 0, late)
         group_w("v", 1, 1, 1, 0, W11A)
         group_w("s", 1, 1, 1, W11A, P)
         group_w("v", 1, 1, 0, 0, W11B)
@@ -313,41 +335,39 @@ def tile_moe_nxt_lin_relu_kernel(tc, xT, w, b, wp, gate, offs, out):
         quantize_w(1, 1, 1)
         expert_pair(1, 1, 1, early)
         quantize_w(1, 1, 0)
-        quantize_w(1, 0, 0, "wgrouped111")
-        expert_pair(1, 0, 0, late)
         expert_pair(1, 1, 0, late)
         scatter(0, 0, 0, C, c00[:])
-        wpgrouped = keep.tile([P, M, J], BF16, name="wpgrouped", tag=WPTAG, align_bytes=64)
-        for lo, hi in WPC:
-            group_wp("s", lo, hi)
+        first = keep.tile([P, P, J], BF16, name="wpfirst", align_bytes=64)
+        rest = keep.tile([P, M - P, J], BF16, name="wprest", tag="bias", align_bytes=64)
+        wpgrouped = [first[:]] + [rest[:, g * P :, :] for g in range(G - 1)]
+        group_wp("s", 0, P)
+        group_wp("s", P, 2 * P)
+        if WG > 2 * P:
+            group_wp("s", 2 * P, WG)
         c11 = keep.tile([P, C, 2], BF16, name="c11", align_bytes=64)
-        apply_gate("g", 1, 1, 0, H, part=c11)
-        apply_gate("v", 1, 1, H, C, part=c11)
-        apply_gate("g", 1, 0, 0, C)
+        apply_gate("g", 1, 1, 0, A1, part=c11)
+        apply_gate("v", 1, 1, A1, C, part=c11)
+        c10 = keep.tile([P, C, 2], BF16, name="c10", align_bytes=64)
+        if B1 > 0:
+            apply_gate("v", 1, 0, 0, B1, part=c10)
+        apply_gate("g", 1, 0, B1, C, part=c10)
+        group_wp("g", WG, M)
         scatter(1, 1, 0, C, c11[:])
         move("s", woven[0][:, :, 1], window[1][:, 0:Q])
         for q in range(1, CHUNKS):
             stage("s", q, 1)
-        if MID:
-            wpcodes[0] = keep.tile([P, 256], U32, name="wpcodes0", tag="c11", align_bytes=64)[:]
-            quantize_wp(0)
-        scatter(1, 0, 0, C, c[1, 0, 0][:])
-        last = keep.tile([P, 512], U32, name="wpcodes1", tag="c100", align_bytes=64)
-        wpcodes[1] = last[:, 0:256]
-        for n in range(WARM):
-            idle = psum.tile([P, C], F32, name=f"idle{n}", tag="bank6")
-            nc.tensor.matmul_mx(out=idle[:], lhsT=wpcodes[0][:, 0:P].bitcast(FP8X4), lhsT_scale=wpbytes[:, 0:P], rhs=wpcodes[0].bitcast(FP8X4), rhs_scale=wpbytes[:, 0:C], start=True, stop=True)
+        scatter(1, 0, 0, C, c10[:])
+        wpcodes = keep.tile([P, M], U32, name="wpcodes", tag="c10", align_bytes=64)
         move("v", woven[0][:, 0:FIRST, 0], window[0][:, 0:FIRST])
-        if MID:
-            quantize_wp(1)
-        else:
-            wpcodes[0] = last[:, 256:512]
-            quantize_wp(0)
+        quantize_wp(0, 1)
+        if Q2:
+            quantize_wp(1, 2)
         quantize_c(0, 0, FIRST)
+        if not Q2:
+            quantize_wp(1, 2)
         if FIRST < Q:
             move("v", woven[0][:, 128:256, 0], window[0][:, 128:256])
-        if not MID:
-            quantize_wp(1)
+        quantize_wp(2, 4)
         for q in SORDER:
             stage("s", q, 0)
         if FIRST < Q:
@@ -359,4 +379,4 @@ def tile_moe_nxt_lin_relu_kernel(tc, xT, w, b, wp, gate, offs, out):
         quantize_c(2)
         quantize_c(3)
         for n, (t0, t1, g0, g1, eng) in enumerate(PIECES):
-            project(t0, t1, g0, g1, eng, (n + 7) % 8)
+            project(t0, t1, g0, g1, eng, n % 8)

@@ -30,17 +30,23 @@ R = S // P
 GA = "v"
 CT = "c00"
 XV = 320
-XB = 128
+XB = 112
 W01A = 88
 W01B = 48
-W00G = 104
+W00G = 88
 W11A = 0
-W11B = 88
+W11B = 104
 G0 = 208
 B1 = 48
 Q2 = 1
-WG = 320
-A1 = 96
+HOOK = 0
+WARM2 = 0
+GT = "xraw0512"
+W00V = 0
+SPLIT = 0
+XV1 = 320
+WG = 384
+A1 = 88
 W10G = 96
 GU = 0
 W1 = 0
@@ -65,7 +71,7 @@ def tile_moe_nxt_lin_relu_kernel(tc, xT, w, b, wp, gate, offs, out):
         gate_row = keep.tile([P, S // P], F32, name="gate_row")
 
         x_loads = [(1, 0, 1024), (0, 0, 512), (0, 512, 1024)]
-        x_pieces = [(1, 0, 512, XV), (1, 512, 1024, XV), (0, 0, 512, XB), (0, 512, 1024, XV)]
+        x_pieces = [(1, 0, 512, XV1), (1, 512, 1024, XV1), (0, 0, 512, XB), (0, 512, 1024, XV)]
         xraw = {}
         nc.scalar.dma_start(gate_row[:], gate[0, :].rearrange("(p c) -> p c", c=S // P))
         for k, (a, t0, t1) in enumerate(x_loads):
@@ -98,17 +104,11 @@ def tile_moe_nxt_lin_relu_kernel(tc, xT, w, b, wp, gate, offs, out):
         nc.gpsimd.memset(window[1][:, 8:T], 0.0)
         nc.gpsimd.memset(window[0][:, 0:T], 0.0)
 
-        xgrouped = [keep.tile([P, T, J], BF16, name=f"xgrouped{a}", align_bytes=64) for a in range(PASSES)]
+        xgrouped = {}
         xcodes = [keep.tile([P, T], U32, name=f"xcodes{a}", align_bytes=64) for a in range(PASSES)]
         gcodes = {}
         gbytes = {}
-        wgrouped = {
-            (e, a, u): keep.tile([P, 2, P, J], BF16, name=f"wgrouped{e}{a}{u}", align_bytes=64)
-            for e in range(E)
-            for a in range(PASSES)
-            for u in range(2)
-            if (e, a, u) != (1, 1, 1)
-        }
+        wgrouped = {}
         spare = window[0][:, T : T + 2 * P * J // 2].bitcast(BF16)
         wgrouped[1, 1, 1] = spare.rearrange("p (t m j) -> p t m j", t=2, j=J)
         wcodes = {}
@@ -130,17 +130,21 @@ def tile_moe_nxt_lin_relu_kernel(tc, xT, w, b, wp, gate, offs, out):
             else:
                 nc.gpsimd.tensor_scalar(dst, src, 1.0, 0.0, MULT, ADD)
 
-        def group_x(engine, a, lo, hi):
+        def group_x(engine, a, first, lo, hi):
             t0 = max(s for (pa, s, end) in x_loads if pa == a and s <= lo)
+            order = "p c i j" if engine == "g" else "p c j i"
             move(
                 engine,
-                xgrouped[a][:, lo:hi, :].rearrange("p (c i) j -> p c j i", i=4),
-                xraw[a, t0][:, :, lo - t0 : hi - t0].rearrange("p j (c i) -> p c j i", i=4),
+                xgrouped[a, first][:, lo - first : hi - first, :].rearrange("p (c i) j -> " + order, i=4),
+                xraw[a, t0][:, :, lo - t0 : hi - t0].rearrange("p j (c i) -> " + order, i=4),
             )
 
-        def group_w(engine, e, a, u, m0=0, m1=P):
+        def group_w(engine, e, a, u, m0=0, m1=P, tag=None):
             if m0 == m1:
                 return
+            if (e, a, u) not in wgrouped:
+                name = f"wgrouped{e}{a}{u}"
+                wgrouped[e, a, u] = keep.tile([P, 2, P, J], BF16, name=name, tag=tag or name, align_bytes=64)[:]
             order = "p m t j" if engine == "g" else "p m j t"
             columns = wraw[e][a][:].rearrange("p j (m u t) -> p j m u t", u=2, t=2)[:, :, m0:m1, u, :]
             move(engine, wgrouped[e, a, u][:, :, m0:m1, :].rearrange("p t m j -> " + order), columns.rearrange("p j m t -> " + order))
@@ -157,7 +161,7 @@ def tile_moe_nxt_lin_relu_kernel(tc, xT, w, b, wp, gate, offs, out):
             nc.vector.quantize_mx(
                 out=xcodes[a][:, t0:t1].bitcast(FP8X4),
                 scales=xbytes[4 * a :, t0:t1],
-                in_=xgrouped[a][:, t0:t1, :].rearrange("p t j -> p (t j)"),
+                in_=xgrouped[a, t0][:].rearrange("p t j -> p (t j)"),
             )
 
         def quantize_w(e, a, u, tag=None):
@@ -166,12 +170,12 @@ def tile_moe_nxt_lin_relu_kernel(tc, xT, w, b, wp, gate, offs, out):
             nc.vector.quantize_mx(
                 out=wcodes[e, a, u][:].bitcast(FP8X4),
                 scales=wbytes[e, a, u][:],
-                in_=wgrouped[e, a, u][:].rearrange("p t m j -> p (t m j)"),
+                in_=wgrouped[e, a, u].rearrange("p t m j -> p (t m j)"),
             )
 
         def quantize_wp(g0, g1):
             nc.vector.quantize_mx(
-                out=wpcodes[:, g0 * P : g1 * P].bitcast(FP8X4),
+                out=wpcodes[g0][:, 0 : (g1 - g0) * P].bitcast(FP8X4),
                 scales=wpbytes[:, g0 * P : g1 * P],
                 in_=wpgrouped[g0][:, 0 : (g1 - g0) * P, :].rearrange("p f j -> p (f j)"),
             )
@@ -272,7 +276,7 @@ def tile_moe_nxt_lin_relu_kernel(tc, xT, w, b, wp, gate, offs, out):
                     q = lo // Q
                     nc.tensor.matmul_mx(
                         out=bank[:, g - g0, lo - t0 : hi - t0],
-                        lhsT=wpcodes[:, g * P : (g + 1) * P].bitcast(FP8X4),
+                        lhsT=wpcodes[g][:, 0:P].bitcast(FP8X4),
                         lhsT_scale=wpbytes[:, g * P : (g + 1) * P],
                         rhs=ccodes[q][:, lo - q * Q : hi - q * Q].bitcast(FP8X4),
                         rhs_scale=cbytes[q][:, lo - q * Q : hi - q * Q],
@@ -283,20 +287,31 @@ def tile_moe_nxt_lin_relu_kernel(tc, xT, w, b, wp, gate, offs, out):
             move(engine, result[:], bank[:])
             nc.sync.dma_start(out[g0 * P : g1 * P, t0:t1].rearrange("(g p) t -> p g t", p=P), result[:])
 
-        for a, t0, t1, cut in x_pieces:
-            group_x("v", a, t0, t0 + cut)
-            group_x("s", a, t0 + cut, t1)
+        def piece(a, t0, t1, shares, tag=None):
+            name = f"xgrouped{a}{t0}"
+            xgrouped[a, t0] = keep.tile([P, t1 - t0, J], BF16, name=name, tag=tag or name, align_bytes=64)
+            lo = t0
+            for engine, count in shares:
+                group_x(engine, a, t0, lo, lo + count)
+                lo = lo + count
             quantize_x(a, t0, t1)
-            if t1 == T:
-                gather_words(a, 0, E, f"gcodes{a}")
-        gates = keep.tile([P, S], F32, name="gates", tag="xraw10", align_bytes=64)
+
+        piece(1, 0, 512, [("v", XV1), ("s", 512 - XV1)])
+        piece(1, 512, T, [("v", XV1), ("s", 512 - XV1)])
+        gather_words(1, 0, E, "gcodes1")
+        piece(0, 256, 512, [("s", 256)])
+        piece(0, 0, 256, [("v", XB), ("s", 256 - XB)])
+        piece(0, 512, T, [("v", XV), ("s", 512 - XV)])
+        gather_words(0, 0, E, "gcodes0")
+        gates = keep.tile([P, S], F32, name="gates", tag=GT, align_bytes=64)
         nc.scalar.copy(out=gates[:].rearrange("p (m r) -> p m r", r=R), in_=gbank[:].rearrange("p r m -> p m r"))
         gather_bytes(0, "gbytes0")
         early = [(0, H, 2), (H, C, 4)]
         late = [(0, C, 0)]
-        group_w("g", 0, 0, 1, 0, W00G)
+        group_w("g", 0, 0, 1, 0, W00G, "xgrouped0512")
         group_w("s", 0, 0, 0)
-        group_w("s", 0, 0, 1, W00G, P)
+        group_w("v", 0, 0, 1, W00G, W00G + W00V)
+        group_w("s", 0, 0, 1, W00G + W00V, P)
         quantize_w(0, 0, 0)
         expert_pair(0, 0, 0, late)
         quantize_w(0, 0, 1)
@@ -318,7 +333,7 @@ def tile_moe_nxt_lin_relu_kernel(tc, xT, w, b, wp, gate, offs, out):
         apply_gate("g", 0, 0, 0, G0, part=c00)
         if G0 < C:
             apply_gate("v", 0, 0, G0, C, part=c00)
-        group_w("g", 1, 0, GU, 0, W10G)
+        group_w("g", 1, 0, GU, 0, W10G, "wgrouped010")
         group_w("s", 1, 0, 1 - GU)
         group_w("s", 1, 0, GU, W10G, P)
         quantize_w(1, 0, 1)
@@ -351,32 +366,42 @@ def tile_moe_nxt_lin_relu_kernel(tc, xT, w, b, wp, gate, offs, out):
         if B1 > 0:
             apply_gate("v", 1, 0, 0, B1, part=c10)
         apply_gate("g", 1, 0, B1, C, part=c10)
-        group_wp("g", WG, M)
+        if WG < M:
+            group_wp("g", WG, M)
         scatter(1, 1, 0, C, c11[:])
         move("s", woven[0][:, :, 1], window[1][:, 0:Q])
         for q in range(1, CHUNKS):
             stage("s", q, 1)
+        wpcodes = {}
+        if HOOK:
+            wpcodes[0] = keep.tile([P, P], U32, name="wpcodes0", tag="c11", align_bytes=64)[:]
+            quantize_wp(0, 1)
         scatter(1, 0, 0, C, c10[:])
-        wpcodes = keep.tile([P, M], U32, name="wpcodes", tag="c10", align_bytes=64)
-        move("v", woven[0][:, 0:FIRST, 0], window[0][:, 0:FIRST])
-        quantize_wp(0, 1)
-        if Q2:
-            quantize_wp(1, 2)
-        quantize_c(0, 0, FIRST)
-        if not Q2:
-            quantize_wp(1, 2)
-        if FIRST < Q:
-            move("v", woven[0][:, 128:256, 0], window[0][:, 128:256])
-        quantize_wp(2, 4)
+        for n in range(WARM2):
+            idle = psum.tile([P, P], F32, name=f"idle{n}", tag="bank7")
+            nc.tensor.matmul_mx(out=idle[:], lhsT=wpcodes[0].bitcast(FP8X4), lhsT_scale=wpbytes[:, 0:P], rhs=wpcodes[0].bitcast(FP8X4), rhs_scale=wpbytes[:, 0:P], start=True, stop=True)
+        pair = keep.tile([P, 2 * P], U32, name="wpcodes1", tag="c10", align_bytes=64)
+        wpcodes[1] = pair[:, P:]
+        move("v", woven[0][:, :, 0], window[0][:, 0:Q])
+        if not HOOK:
+            wpcodes[0] = pair[:, 0:P]
+            quantize_wp(0, 1)
+        quantize_wp(1, 2)
+        quantize_c(0)
+        pair = keep.tile([P, 2 * P], U32, name="wpcodes2", tag="woven0" if WG == M else "wpcodes2", align_bytes=64)
+        wpcodes[2] = pair[:]
+        wpcodes[3] = pair[:, P:]
         for q in SORDER:
             stage("s", q, 0)
-        if FIRST < Q:
-            quantize_c(0, 128, 256)
-        weave("v", 1)
+        if WG == M:
+            weave("v", 1)
+        quantize_wp(2, 4)
+        if WG < M:
+            weave("v", 1)
         weave("v", 2)
         quantize_c(1)
         weave("v", 3)
         quantize_c(2)
         quantize_c(3)
         for n, (t0, t1, g0, g1, eng) in enumerate(PIECES):
-            project(t0, t1, g0, g1, eng, n % 8)
+            project(t0, t1, g0, g1, eng, n % 7 if WARM2 else n % 8)

@@ -32,20 +32,23 @@ CT = "c00"
 XV = 320
 XB = 112
 W01A = 88
-W01B = 48
-W00G = 88
+W01B = 56
+W00G = 96
 W11A = 0
 W11B = 104
 G0 = 208
 B1 = 48
 Q2 = 1
-HOOK = 0
-WARM2 = 0
+HOOK = 1
+T3 = "wpfirst"
+T2 = "wpcodes2"
+EACH = 256
+WARM2 = 8
 GT = "xraw0512"
 W00V = 0
 SPLIT = 0
 XV1 = 320
-WG = 384
+WG = 256
 A1 = 88
 W10G = 96
 GU = 0
@@ -57,7 +60,7 @@ WPTAG = "wpgrouped"
 WPC = [(0, 256), (256, 512)]
 MID = 0
 FIRST = 256
-PIECES = [(0,256,0,1,"s"),(0,256,1,2,"s"),(0,256,2,3,"s"),(0,256,3,4,"s"),(256,512,0,1,"s"),(256,512,1,2,"s"),(256,512,2,3,"s"),(256,512,3,4,"s"),(512,1024,0,1,"v"),(512,1024,1,2,"s"),(512,1024,2,3,"v"),(512,1024,3,4,"s")]
+PIECES = [(0,256,0,1,"s"),(0,256,1,2,"s"),(0,256,2,3,"s"),(0,256,3,4,"s"),(256,512,0,2,"sv"),(256,512,2,4,"sv"),(512,1024,0,1,"s"),(512,1024,1,2,"v"),(512,1024,2,3,"s"),(512,1024,3,4,"v")]
 
 
 def tile_moe_nxt_lin_relu_kernel(tc, xT, w, b, wp, gate, offs, out):
@@ -267,24 +270,27 @@ def tile_moe_nxt_lin_relu_kernel(tc, xT, w, b, wp, gate, offs, out):
                 in_=woven[q][:, lo:hi, :].rearrange("p t u -> p (t u)").bitcast(BF16),
             )
 
-        def project(t0, t1, g0, g1, engine, number):
+        def project(t0, t1, g0, g1, engines, banks):
             width = t1 - t0
-            bank = psum.tile([P, g1 - g0, width], F32, name=f"obank{t0}{g0}", tag=f"bank{number}")
-            for g in range(g0, g1):
-                for lo in range(t0, t1, Q):
-                    hi = min(lo + Q, t1)
-                    q = lo // Q
-                    nc.tensor.matmul_mx(
-                        out=bank[:, g - g0, lo - t0 : hi - t0],
-                        lhsT=wpcodes[g][:, 0:P].bitcast(FP8X4),
-                        lhsT_scale=wpbytes[:, g * P : (g + 1) * P],
-                        rhs=ccodes[q][:, lo - q * Q : hi - q * Q].bitcast(FP8X4),
-                        rhs_scale=cbytes[q][:, lo - q * Q : hi - q * Q],
-                        start=True,
-                        stop=True,
-                    )
+            each = min(g1 - g0, max(1, EACH // width))
             result = keep.tile([P, g1 - g0, width], F32, name=f"result{t0}{g0}", align_bytes=64)
-            move(engine, result[:], bank[:])
+            for n, first in enumerate(range(g0, g1, each)):
+                number = banks.pop(0)
+                banks.append(number)
+                bank = psum.tile([P, each, width], F32, name=f"obank{t0}{first}", tag=f"bank{number}")
+                for g in range(first, first + each):
+                    for lo in range(t0, t1, Q):
+                        q = lo // Q
+                        nc.tensor.matmul_mx(
+                            out=bank[:, g - first, lo - t0 : lo - t0 + Q],
+                            lhsT=wpcodes[g][:, 0:P].bitcast(FP8X4),
+                            lhsT_scale=wpbytes[:, g * P : (g + 1) * P],
+                            rhs=ccodes[q][:].bitcast(FP8X4),
+                            rhs_scale=cbytes[q][:],
+                            start=True,
+                            stop=True,
+                        )
+                move(engines[n], result[:, first - g0 : first - g0 + each, :], bank[:])
             nc.sync.dma_start(out[g0 * P : g1 * P, t0:t1].rearrange("(g p) t -> p g t", p=P), result[:])
 
         def piece(a, t0, t1, shares, tag=None):
@@ -353,33 +359,39 @@ def tile_moe_nxt_lin_relu_kernel(tc, xT, w, b, wp, gate, offs, out):
         expert_pair(1, 1, 0, late)
         scatter(0, 0, 0, C, c00[:])
         first = keep.tile([P, P, J], BF16, name="wpfirst", align_bytes=64)
-        rest = keep.tile([P, M - P, J], BF16, name="wprest", tag="bias", align_bytes=64)
-        wpgrouped = [first[:]] + [rest[:, g * P :, :] for g in range(G - 1)]
-        group_wp("s", 0, P)
-        group_wp("s", P, 2 * P)
-        if WG > 2 * P:
-            group_wp("s", 2 * P, WG)
+        middle = keep.tile([P, 2 * P, J], BF16, name="wpmiddle", tag="bias", align_bytes=64)
+        wpgrouped = [first[:], middle[:], middle[:, P:, :]]
+        for g in range(3):
+            group_wp("s", g * P, (g + 1) * P)
         c11 = keep.tile([P, C, 2], BF16, name="c11", align_bytes=64)
         apply_gate("g", 1, 1, 0, A1, part=c11)
         apply_gate("v", 1, 1, A1, C, part=c11)
         c10 = keep.tile([P, C, 2], BF16, name="c10", align_bytes=64)
-        if B1 > 0:
-            apply_gate("v", 1, 0, 0, B1, part=c10)
+        apply_gate("v", 1, 0, 0, B1, part=c10)
         apply_gate("g", 1, 0, B1, C, part=c10)
-        if WG < M:
-            group_wp("g", WG, M)
         scatter(1, 1, 0, C, c11[:])
+        wpcodes = {}
+        if HOOK:
+            wpcodes[0] = keep.tile([P, P], U32, name="wpcodes0", tag="y10", align_bytes=64)[:]
+            quantize_wp(0, 1)
+        fourth = keep.tile([P, P, J], BF16, name="wpfourth", tag=T3, align_bytes=64)
+        wpgrouped.append(fourth[:])
+        group_wp("g", 3 * P, M)
         move("s", woven[0][:, :, 1], window[1][:, 0:Q])
         for q in range(1, CHUNKS):
             stage("s", q, 1)
-        wpcodes = {}
-        if HOOK:
-            wpcodes[0] = keep.tile([P, P], U32, name="wpcodes0", tag="c11", align_bytes=64)[:]
-            quantize_wp(0, 1)
         scatter(1, 0, 0, C, c10[:])
+        idle = psum.tile([P, C], F32, name="idle", tag="bank7")
         for n in range(WARM2):
-            idle = psum.tile([P, P], F32, name=f"idle{n}", tag="bank7")
-            nc.tensor.matmul_mx(out=idle[:], lhsT=wpcodes[0].bitcast(FP8X4), lhsT_scale=wpbytes[:, 0:P], rhs=wpcodes[0].bitcast(FP8X4), rhs_scale=wpbytes[:, 0:P], start=True, stop=True)
+            nc.tensor.matmul_mx(
+                out=idle[:],
+                lhsT=wpcodes[0].bitcast(FP8X4),
+                lhsT_scale=wpbytes[:, 0:P],
+                rhs=gcodes[0, 0].bitcast(FP8X4),
+                rhs_scale=gbytes[0][:],
+                start=(n == 0),
+                stop=(n == WARM2 - 1),
+            )
         pair = keep.tile([P, 2 * P], U32, name="wpcodes1", tag="c10", align_bytes=64)
         wpcodes[1] = pair[:, P:]
         move("v", woven[0][:, :, 0], window[0][:, 0:Q])
@@ -388,20 +400,19 @@ def tile_moe_nxt_lin_relu_kernel(tc, xT, w, b, wp, gate, offs, out):
             quantize_wp(0, 1)
         quantize_wp(1, 2)
         quantize_c(0)
-        pair = keep.tile([P, 2 * P], U32, name="wpcodes2", tag="woven0" if WG == M else "wpcodes2", align_bytes=64)
+        pair = keep.tile([P, 2 * P], U32, name="wpcodes2", tag=T2, align_bytes=64)
         wpcodes[2] = pair[:]
         wpcodes[3] = pair[:, P:]
-        for q in SORDER:
+        for q in range(1, CHUNKS):
             stage("s", q, 0)
-        if WG == M:
-            weave("v", 1)
-        quantize_wp(2, 4)
-        if WG < M:
-            weave("v", 1)
+        quantize_wp(2, 3)
+        quantize_wp(3, 4)
+        weave("v", 1)
         weave("v", 2)
         quantize_c(1)
         weave("v", 3)
         quantize_c(2)
         quantize_c(3)
-        for n, (t0, t1, g0, g1, eng) in enumerate(PIECES):
-            project(t0, t1, g0, g1, eng, n % 7 if WARM2 else n % 8)
+        banks = list(range(7 if WARM2 else 8))
+        for t0, t1, g0, g1, engines in PIECES:
+            project(t0, t1, g0, g1, engines, banks)

@@ -39,11 +39,16 @@ W11B = 104
 G0 = 208
 B1 = 48
 Q2 = 1
-HOOK = 1
-T3 = "wpfirst"
+HOOK = 0
+T3 = "y10"
 T2 = "wpcodes2"
-EACH = 256
-WARM2 = 8
+BANK = 512
+LATE = 0
+W3 = "v"
+W2 = "s"
+T0 = "xraw0512"
+CUTS = [0, 256, 512, 768, 1024]
+WARM2 = 0
 GT = "xraw0512"
 W00V = 0
 SPLIT = 0
@@ -60,7 +65,7 @@ WPTAG = "wpgrouped"
 WPC = [(0, 256), (256, 512)]
 MID = 0
 FIRST = 256
-PIECES = [(0,256,0,1,"s"),(0,256,1,2,"s"),(0,256,2,3,"s"),(0,256,3,4,"s"),(256,512,0,2,"sv"),(256,512,2,4,"sv"),(512,1024,0,1,"s"),(512,1024,1,2,"v"),(512,1024,2,3,"s"),(512,1024,3,4,"v")]
+PIECES = [(0,256,0,"s"),(0,256,1,"s"),(0,256,2,"s"),(0,256,3,"s"),(256,512,0,"s"),(256,512,1,"s"),(512,1024,0,"v"),(256,1024,2,"sv"),(512,1024,1,"s"),(256,1024,3,"sv")]
 
 
 def tile_moe_nxt_lin_relu_kernel(tc, xT, w, b, wp, gate, offs, out):
@@ -270,28 +275,26 @@ def tile_moe_nxt_lin_relu_kernel(tc, xT, w, b, wp, gate, offs, out):
                 in_=woven[q][:, lo:hi, :].rearrange("p t u -> p (t u)").bitcast(BF16),
             )
 
-        def project(t0, t1, g0, g1, engines, banks):
-            width = t1 - t0
-            each = min(g1 - g0, max(1, EACH // width))
-            result = keep.tile([P, g1 - g0, width], F32, name=f"result{t0}{g0}", align_bytes=64)
-            for n, first in enumerate(range(g0, g1, each)):
+        def project(t0, t1, g, engines, banks):
+            result = keep.tile([P, t1 - t0], F32, name=f"result{t0}{g}", align_bytes=64)
+            edges = [t0] + [t for t in (BANK,) if t0 < t < t1 and t1 - t0 > BANK] + [t1]
+            for engine, b0, b1 in zip(engines, edges, edges[1:]):
                 number = banks.pop(0)
                 banks.append(number)
-                bank = psum.tile([P, each, width], F32, name=f"obank{t0}{first}", tag=f"bank{number}")
-                for g in range(first, first + each):
-                    for lo in range(t0, t1, Q):
-                        q = lo // Q
+                bank = psum.tile([P, b1 - b0], F32, name=f"obank{b0}{g}", tag=f"bank{number}")
+                for lo, hi in zip(CUTS, CUTS[1:]):
+                    if b0 <= lo and hi <= b1:
                         nc.tensor.matmul_mx(
-                            out=bank[:, g - first, lo - t0 : lo - t0 + Q],
+                            out=bank[:, lo - b0 : hi - b0],
                             lhsT=wpcodes[g][:, 0:P].bitcast(FP8X4),
                             lhsT_scale=wpbytes[:, g * P : (g + 1) * P],
-                            rhs=ccodes[q][:].bitcast(FP8X4),
-                            rhs_scale=cbytes[q][:],
+                            rhs=ccodes[lo // Q][:, lo % Q : lo % Q + hi - lo].bitcast(FP8X4),
+                            rhs_scale=cbytes[lo // Q][:, lo % Q : lo % Q + hi - lo],
                             start=True,
                             stop=True,
                         )
-                move(engines[n], result[:, first - g0 : first - g0 + each, :], bank[:])
-            nc.sync.dma_start(out[g0 * P : g1 * P, t0:t1].rearrange("(g p) t -> p g t", p=P), result[:])
+                move(engine, result[:, b0 - t0 : b1 - t0], bank[:])
+            nc.sync.dma_start(out[g * P : (g + 1) * P, t0:t1], result[:])
 
         def piece(a, t0, t1, shares, tag=None):
             name = f"xgrouped{a}{t0}"
@@ -370,49 +373,30 @@ def tile_moe_nxt_lin_relu_kernel(tc, xT, w, b, wp, gate, offs, out):
         apply_gate("v", 1, 0, 0, B1, part=c10)
         apply_gate("g", 1, 0, B1, C, part=c10)
         scatter(1, 1, 0, C, c11[:])
-        wpcodes = {}
-        if HOOK:
-            wpcodes[0] = keep.tile([P, P], U32, name="wpcodes0", tag="y10", align_bytes=64)[:]
-            quantize_wp(0, 1)
-        fourth = keep.tile([P, P, J], BF16, name="wpfourth", tag=T3, align_bytes=64)
+        fourth = keep.tile([P, P, J], BF16, name="wpfourth", tag="y10", align_bytes=64)
         wpgrouped.append(fourth[:])
         group_wp("g", 3 * P, M)
         move("s", woven[0][:, :, 1], window[1][:, 0:Q])
         for q in range(1, CHUNKS):
             stage("s", q, 1)
         scatter(1, 0, 0, C, c10[:])
-        idle = psum.tile([P, C], F32, name="idle", tag="bank7")
-        for n in range(WARM2):
-            nc.tensor.matmul_mx(
-                out=idle[:],
-                lhsT=wpcodes[0].bitcast(FP8X4),
-                lhsT_scale=wpbytes[:, 0:P],
-                rhs=gcodes[0, 0].bitcast(FP8X4),
-                rhs_scale=gbytes[0][:],
-                start=(n == 0),
-                stop=(n == WARM2 - 1),
-            )
-        pair = keep.tile([P, 2 * P], U32, name="wpcodes1", tag="c10", align_bytes=64)
-        wpcodes[1] = pair[:, P:]
+        wpcodes = {0: keep.tile([P, P], U32, name="wpcodes0", tag=T0, align_bytes=64)[:]}
+        quantize_wp(0, 1)
+        others = keep.tile([P, 3 * P], U32, name="wpcodes1", tag="c10", align_bytes=64)
+        for g in range(1, G):
+            wpcodes[g] = others[:, (g - 1) * P :]
         move("v", woven[0][:, :, 0], window[0][:, 0:Q])
-        if not HOOK:
-            wpcodes[0] = pair[:, 0:P]
-            quantize_wp(0, 1)
-        quantize_wp(1, 2)
+        quantize_wp(1, 3)
         quantize_c(0)
-        pair = keep.tile([P, 2 * P], U32, name="wpcodes2", tag=T2, align_bytes=64)
-        wpcodes[2] = pair[:]
-        wpcodes[3] = pair[:, P:]
         for q in range(1, CHUNKS):
             stage("s", q, 0)
-        quantize_wp(2, 3)
         quantize_wp(3, 4)
         weave("v", 1)
-        weave("v", 2)
+        weave(W2, 2)
         quantize_c(1)
         weave("v", 3)
         quantize_c(2)
         quantize_c(3)
-        banks = list(range(7 if WARM2 else 8))
-        for t0, t1, g0, g1, engines in PIECES:
-            project(t0, t1, g0, g1, engines, banks)
+        banks = list(range(8))
+        for t0, t1, g, engines in PIECES:
+            project(t0, t1, g, engines, banks)

@@ -22,50 +22,20 @@ P = 128
 J = 4
 KP = P * J
 PASSES = K // KP
-G = 4
-Q = 256
-CHUNKS = T // Q
-H = C // 2
+G = M // P
 R = S // P
-GA = "v"
-CT = "c00"
-XV = 320
-XB = 112
-W01A = 88
-W01B = 56
-W00G = 96
-W11A = 0
-W11B = 104
-G0 = 208
-B1 = 48
-Q2 = 1
-HOOK = 0
-T3 = "y10"
-T2 = "wpcodes2"
-BANK = 512
-LATE = 0
-W3 = "v"
-W2 = "s"
-T0 = "xraw0512"
-CUTS = [0, 256, 512, 768, 1024]
-WARM2 = 0
-GT = "xraw0512"
-W00V = 0
-SPLIT = 0
-XV1 = 320
-WG = 256
-A1 = 88
-W10G = 96
-GU = 0
-W1 = 0
-WARM = 0
-SW = ()
-SORDER = (1, 2, 3)
-WPTAG = "wpgrouped"
-WPC = [(0, 256), (256, 512)]
-MID = 0
-FIRST = 256
-PIECES = [(0,256,0,"s"),(0,256,1,"s"),(0,256,2,"s"),(0,256,3,"s"),(256,512,0,"s"),(256,512,1,"s"),(512,1024,0,"v"),(256,1024,2,"sv"),(512,1024,1,"s"),(256,1024,3,"sv")]
+HALF = T // 2
+Q = T // 4
+CHUNKS = T // Q
+BANKS = 8
+RANGES = [(0, Q), (Q, 2 * Q), (2 * Q, T)]
+
+EIGHTHS = 5
+X_BUSY = 112
+W_LAST = 104
+W_GPSIMD = 88
+LATE_GPSIMD = 208
+EARLY_GPSIMD = 64
 
 
 def tile_moe_nxt_lin_relu_kernel(tc, xT, w, b, wp, gate, offs, out):
@@ -74,329 +44,270 @@ def tile_moe_nxt_lin_relu_kernel(tc, xT, w, b, wp, gate, offs, out):
         keep = ctx.enter_context(tc.tile_pool(name="keep", bufs=1))
         psum = ctx.enter_context(tc.psum_pool(name="psum", bufs=1))
 
-        offsets = keep.tile([P, S // 16], U16, name="offsets")
-        bias = keep.tile([P, G * E], F32, name="bias", align_bytes=64)
-        gate_row = keep.tile([P, S // P], F32, name="gate_row")
+        def sbuf(shape, dtype, name, tag=None):
+            return keep.tile(shape, dtype, name=name, tag=tag or name, align_bytes=64)[:]
 
-        x_loads = [(1, 0, 1024), (0, 0, 512), (0, 512, 1024)]
-        x_pieces = [(1, 0, 512, XV1), (1, 512, 1024, XV1), (0, 0, 512, XB), (0, 512, 1024, XV)]
+        offsets = keep.tile([P, S // 16], U16, name="offsets")
+        bias = sbuf([P, J * E], F32, "bias")
+        gate_row = sbuf([P, R], F32, "gate_row")
+        nc.scalar.dma_start(gate_row, gate[0, :].rearrange("(p r) -> p r", r=R))
+        x_loads = [(1, 0, T), (0, 0, HALF), (0, HALF, T)]
         xraw = {}
-        nc.scalar.dma_start(gate_row[:], gate[0, :].rearrange("(p c) -> p c", c=S // P))
-        for k, (a, t0, t1) in enumerate(x_loads):
-            xraw[a, t0] = keep.tile([P, J, t1 - t0], F32, name=f"xraw{a}{t0}", align_bytes=64)
-            src = xT[a * KP : (a + 1) * KP, t0:t1]
-            nc.sync.dma_start(xraw[a, t0][:], src.rearrange("(p j) t -> p j t", j=J))
-            if k == 0:
+        for a, t0, t1 in x_loads:
+            xraw[a, t0] = sbuf([P, J, t1 - t0], F32, f"xraw{a}{t0}")
+            nc.sync.dma_start(xraw[a, t0], xT[a * KP : (a + 1) * KP, t0:t1].rearrange("(p j) t -> p j t", j=J))
+            if a == 1:
                 nc.sync.dma_start(offsets[:], offs)
-                nc.scalar.dma_start(bias[:], b.rearrange("(p t) e -> p (t e)", t=G))
-        wraw = [[keep.tile([P, J, N], F32, name=f"wraw{e}{a}", align_bytes=64) for a in range(PASSES)] for e in range(E)]
-        wpraw = [keep.tile([P, J, M // 2], F32, name=f"wpraw{h}") for h in range(2)]
+                nc.scalar.dma_start(bias, b.rearrange("(p t) e -> p (t e)", t=J))
+        wraw = {}
         for e in range(E):
             for a in range(PASSES):
-                nc.sync.dma_start(wraw[e][a][:], w[e, a * KP : (a + 1) * KP, :].rearrange("(p j) n -> p j n", j=J))
+                wraw[e, a] = sbuf([P, J, N], F32, f"wraw{e}{a}")
+                nc.sync.dma_start(wraw[e, a], w[e, a * KP : (a + 1) * KP, :].rearrange("(p j) n -> p j n", j=J))
+        wpraw = []
         for h in range(2):
-            nc.sync.dma_start(wpraw[h][:], wp[:, h * 256 : (h + 1) * 256].rearrange("(p j) f -> p j f", j=J))
+            wpraw.append(sbuf([P, J, M // 2], F32, f"wpraw{h}"))
+            nc.sync.dma_start(wpraw[h], wp[:, h * M // 2 : (h + 1) * M // 2].rearrange("(p j) f -> p j f", j=J))
 
-        identity = keep.tile([P, P], F32, name="identity")
-        make_identity(nc, identity[:])
-        gbank = psum.tile([P, S // P, P], F32, name="gbank", tag="bank6")
-        for r in range(S // P):
-            nc.tensor.transpose(gbank[:, r, :], gate_row[:, r : r + 1].to_broadcast([P, P]), identity[:])
+        identity = sbuf([P, P], F32, "identity")
+        make_identity(nc, identity)
+        gbank = psum.tile([P, R, P], F32, name="gbank", tag="bank6")
+        for r in range(R):
+            nc.tensor.transpose(gbank[:, r, :], gate_row[:, r : r + 1].to_broadcast([P, P]), identity)
 
         xbytes = keep.tile([P, T], U8, name="xbytes", align_bytes=64)
         nc.vector.memset(xbytes[:].bitcast(I32), 0)
         window = [keep.tile([P, T + (1 - u) * P * J], F32, name=f"window{u}", align_bytes=64) for u in range(2)]
-        zeros = keep.tile([P, 8], F32, name="zeros")
-        nc.vector.memset(zeros[:], 0.0)
-        nc.scalar.activation(window[1][:, 0:8], zeros[:], RELU)
+        zeros = sbuf([P, 8], F32, "zeros")
+        nc.vector.memset(zeros, 0.0)
+        nc.scalar.activation(window[1][:, 0:8], zeros, RELU)
         nc.gpsimd.memset(window[1][:, 8:T], 0.0)
         nc.gpsimd.memset(window[0][:, 0:T], 0.0)
 
-        xgrouped = {}
         xcodes = [keep.tile([P, T], U32, name=f"xcodes{a}", align_bytes=64) for a in range(PASSES)]
         gcodes = {}
         gbytes = {}
-        wgrouped = {}
-        spare = window[0][:, T : T + 2 * P * J // 2].bitcast(BF16)
-        wgrouped[1, 1, 1] = spare.rearrange("p (t m j) -> p t m j", t=2, j=J)
+        wgrouped = {(1, 1, 1): window[0][:, T:].bitcast(BF16).rearrange("p (t m j) -> p t m j", t=2, j=J)}
         wcodes = {}
         wbytes = {}
-        wpbytes = keep.tile([P, M], U8, name="wpbytes", align_bytes=64)
-        y = [[keep.tile([P, 2, C], F32, name=f"y{e}{u}", align_bytes=64) for u in range(2)] for e in range(E)]
-        c = {}
-        halves = [keep.tile([P, 2, Q], F32, name=f"halves{q}", align_bytes=64) for q in range(CHUNKS)]
-        woven = [keep.tile([P, Q, 2], F32, name=f"woven{q}", align_bytes=64) for q in range(CHUNKS)]
-        ccodes = [keep.tile([P, Q], U32, name=f"ccodes{q}", align_bytes=64) for q in range(CHUNKS)]
-        cbytes = [keep.tile([P, Q], U8, name=f"cbytes{q}", align_bytes=64) for q in range(CHUNKS)]
         ybank = {}
+        y = {(e, u): sbuf([P, 2, C], F32, f"y{e}{u}") for e in range(E) for u in range(2)}
+        c = {(e, u): sbuf([P, C, 2], BF16, f"c{e}{u}") for e in range(E) for u in range(2)}
+        staged = {q: sbuf([P, 2, Q], F32, f"staged{q}") for q in range(1, CHUNKS)}
+        woven = [sbuf([P, Q, 2], F32, f"woven{q}") for q in range(CHUNKS)]
+        ccodes = {t0: sbuf([P, t1 - t0], U32, f"ccodes{t0}") for t0, t1 in RANGES}
+        cbytes = {t0: sbuf([P, t1 - t0], U8, f"cbytes{t0}") for t0, t1 in RANGES}
+        wpgrouped = {}
+        wpcodes = {}
+        wpbytes = sbuf([P, M], U8, "wpbytes")
 
         def move(engine, dst, src):
-            if engine == "v":
+            if engine == "vector":
                 nc.vector.tensor_copy(out=dst, in_=src)
-            elif engine == "s":
+            elif engine == "scalar":
                 nc.scalar.copy(out=dst, in_=src)
             else:
                 nc.gpsimd.tensor_scalar(dst, src, 1.0, 0.0, MULT, ADD)
 
-        def group_x(engine, a, first, lo, hi):
-            t0 = max(s for (pa, s, end) in x_loads if pa == a and s <= lo)
-            order = "p c i j" if engine == "g" else "p c j i"
-            move(
-                engine,
-                xgrouped[a, first][:, lo - first : hi - first, :].rearrange("p (c i) j -> " + order, i=4),
-                xraw[a, t0][:, :, lo - t0 : hi - t0].rearrange("p j (c i) -> " + order, i=4),
-            )
+        def quantize(codes, scales, grouped):
+            nc.vector.quantize_mx(out=codes.bitcast(FP8X4), scales=scales, in_=grouped)
 
-        def group_w(engine, e, a, u, m0=0, m1=P, tag=None):
-            if m0 == m1:
-                return
+        def quantize_x(a, t0, t1, by_vector):
+            loaded = max(first for (pa, first, end) in x_loads if pa == a and first <= t0)
+            grouped = sbuf([P, t1 - t0, J], BF16, f"xgrouped{a}{t0}")
+            for engine, lo, hi in (("vector", 0, by_vector), ("scalar", by_vector, t1 - t0)):
+                if lo < hi:
+                    move(
+                        engine,
+                        grouped[:, lo:hi, :].rearrange("p (x i) j -> p x j i", i=4),
+                        xraw[a, loaded][:, :, t0 - loaded + lo : t0 - loaded + hi].rearrange("p j (x i) -> p x j i", i=4),
+                    )
+            quantize(xcodes[a][:, t0:t1], xbytes[4 * a :, t0:t1], grouped.rearrange("p t j -> p (t j)"))
+
+        def gather_words(a):
+            gcodes[a] = sbuf([P, S], U32, f"gcodes{a}")
+            nc.vector.tensor_copy(gcodes[a], xcodes[a][:].indirect(offsets[:]))
+
+        def gather_bytes(e, tag=None):
+            gbytes[e] = sbuf([P, C], U8, f"gbytes{e}", tag)
+            nc.vector.tensor_copy(gbytes[e], xbytes[:].indirect(offsets[:, e * C // 16 : (e + 1) * C // 16]))
+
+        def group_w(engine, e, a, u, m0, m1, tag=None):
             if (e, a, u) not in wgrouped:
-                name = f"wgrouped{e}{a}{u}"
-                wgrouped[e, a, u] = keep.tile([P, 2, P, J], BF16, name=name, tag=tag or name, align_bytes=64)[:]
-            order = "p m t j" if engine == "g" else "p m j t"
-            columns = wraw[e][a][:].rearrange("p j (m u t) -> p j m u t", u=2, t=2)[:, :, m0:m1, u, :]
-            move(engine, wgrouped[e, a, u][:, :, m0:m1, :].rearrange("p t m j -> " + order), columns.rearrange("p j m t -> " + order))
-
-        def group_wp(engine, lo, hi):
-            order = "p c i j" if engine == "g" else "p c j i"
+                wgrouped[e, a, u] = sbuf([P, 2, P, J], BF16, f"wgrouped{e}{a}{u}", tag)
+            order = "p m t j" if engine == "gpsimd" else "p m j t"
+            columns = wraw[e, a].rearrange("p j (m u t) -> p j m u t", u=2, t=2)[:, :, m0:m1, u, :]
             move(
                 engine,
-                wpgrouped[lo // P][:, lo % P : lo % P + hi - lo, :].rearrange("p (c i) j -> " + order, i=4),
-                wpraw[lo // 256][:, :, lo % 256 : lo % 256 + hi - lo].rearrange("p j (c i) -> " + order, i=4),
+                wgrouped[e, a, u][:, :, m0:m1, :].rearrange("p t m j -> " + order),
+                columns.rearrange("p j m t -> " + order),
             )
 
-        def quantize_x(a, t0, t1):
-            nc.vector.quantize_mx(
-                out=xcodes[a][:, t0:t1].bitcast(FP8X4),
-                scales=xbytes[4 * a :, t0:t1],
-                in_=xgrouped[a, t0][:].rearrange("p t j -> p (t j)"),
-            )
-
-        def quantize_w(e, a, u, tag=None):
-            wcodes[e, a, u] = keep.tile([P, 2 * P], U32, name=f"wcodes{e}{a}{u}", tag=tag or f"wcodes{e}{a}{u}", align_bytes=64)
-            wbytes[e, a, u] = keep.tile([P, 2 * P], U8, name=f"wbytes{e}{a}{u}", align_bytes=64)
-            nc.vector.quantize_mx(
-                out=wcodes[e, a, u][:].bitcast(FP8X4),
-                scales=wbytes[e, a, u][:],
-                in_=wgrouped[e, a, u].rearrange("p t m j -> p (t m j)"),
-            )
-
-        def quantize_wp(g0, g1):
-            nc.vector.quantize_mx(
-                out=wpcodes[g0][:, 0 : (g1 - g0) * P].bitcast(FP8X4),
-                scales=wpbytes[:, g0 * P : g1 * P],
-                in_=wpgrouped[g0][:, 0 : (g1 - g0) * P, :].rearrange("p f j -> p (f j)"),
-            )
-
-        def gather_words(a, e0, e1, tag):
-            words = keep.tile([P, (e1 - e0) * C], U32, name=f"gcodes{a}{e0}", tag=tag, align_bytes=64)
-            nc.vector.tensor_copy(words[:], xcodes[a][:].indirect(offsets[:, e0 * 16 : e1 * 16]))
-            for e in range(e0, e1):
-                gcodes[a, e] = words[:, (e - e0) * C : (e - e0 + 1) * C]
-
-        def gather_bytes(e, tag):
-            gbytes[e] = keep.tile([P, C], U8, name=f"gbytes{e}", tag=tag, align_bytes=64)
-            nc.vector.tensor_copy(gbytes[e][:], xbytes[:].indirect(offsets[:, e * 16 : (e + 1) * 16]))
-
-        def multiply(e, a, t, s0, s1, number):
-            if a == 0 and number is not None:
-                ybank[e, t, s0] = psum.tile([P, s1 - s0], F32, name=f"ybank{e}{t}{s0}", tag=f"bank{number}")[:]
-            nc.tensor.matmul_mx(
-                out=ybank[e, t, s0],
-                lhsT=wcodes[e, a, t // 2][:, t % 2 * P : (t % 2 + 1) * P].bitcast(FP8X4),
-                lhsT_scale=wbytes[e, a, t // 2][:, t % 2 * P : (t % 2 + 1) * P],
-                rhs=gcodes[a, e][:, s0:s1].bitcast(FP8X4),
-                rhs_scale=gbytes[e][4 * a :, s0:s1],
-                start=(a == 0),
-                stop=(a == PASSES - 1),
-            )
-
-        def relu(e, t, s0, s1):
-            nc.scalar.activation(
-                y[e][t // 2][:, t % 2, s0:s1], ybank[e, t, s0], RELU, bias=bias[:, t * E + e : t * E + e + 1]
-            )
-
-        def expert_pair(e, a, u, cuts):
-            for s0, s1, first in cuts:
-                for t in (2 * u, 2 * u + 1):
-                    multiply(e, a, t, s0, s1, first + t % 2)
+        def multiply(e, a, u, spans):
+            wcodes[e, a, u] = sbuf([P, 2 * P], U32, f"wcodes{e}{a}{u}")
+            wbytes[e, a, u] = sbuf([P, 2 * P], U8, f"wbytes{e}{a}{u}")
+            quantize(wcodes[e, a, u], wbytes[e, a, u], wgrouped[e, a, u].rearrange("p t m j -> p (t m j)"))
+            for s0, s1, bank in spans:
+                for i in range(2):
+                    t = 2 * u + i
+                    if a == 0:
+                        ybank[e, t, s0] = psum.tile([P, s1 - s0], F32, name=f"ybank{e}{t}{s0}", tag=f"bank{bank + i}")
+                    nc.tensor.matmul_mx(
+                        out=ybank[e, t, s0][:],
+                        lhsT=wcodes[e, a, u][:, i * P : (i + 1) * P].bitcast(FP8X4),
+                        lhsT_scale=wbytes[e, a, u][:, i * P : (i + 1) * P],
+                        rhs=gcodes[a][:, e * C + s0 : e * C + s1].bitcast(FP8X4),
+                        rhs_scale=gbytes[e][4 * a :, s0:s1],
+                        start=(a == 0),
+                        stop=(a == PASSES - 1),
+                    )
                     if a == PASSES - 1:
-                        relu(e, t, s0, s1)
+                        column = bias[:, t * E + e : t * E + e + 1]
+                        nc.scalar.activation(y[e, u][:, i, s0:s1], ybank[e, t, s0][:], RELU, bias=column)
 
         def gate_vector(e, u, s0, s1):
-            shape = [P, (s1 - s0) // R, R, 2]
+            weights = gbank[:, :, (e * C + s0) // R : (e * C + s1) // R].rearrange("p r m -> p m r")
             nc.vector.tensor_tensor(
-                out=c[e, u, s0][:].rearrange("p (m r) t -> p m r t", r=R),
-                in0=y[e][u][:, :, s0:s1].rearrange("p t (m r) -> p m r t", r=R),
-                in1=gbank[:, :, (e * C + s0) // R : (e * C + s1) // R].rearrange("p r m -> p m r").unsqueeze(3).to_broadcast(shape),
+                out=c[e, u][:, s0:s1, :].rearrange("p (m r) t -> p m r t", r=R),
+                in0=y[e, u][:, :, s0:s1].rearrange("p t (m r) -> p m r t", r=R),
+                in1=weights.unsqueeze(3).to_broadcast([P, (s1 - s0) // R, R, 2]),
                 op=MULT,
             )
 
         def gate_gpsimd(e, u, s0, s1):
             nc.gpsimd.tensor_tensor(
-                out=c[e, u, s0][:].rearrange("p s t -> p t s"),
-                in0=y[e][u][:, :, s0:s1],
+                out=c[e, u][:, s0:s1, :].rearrange("p s t -> p t s"),
+                in0=y[e, u][:, :, s0:s1],
                 in1=gates[:, e * C + s0 : e * C + s1].unsqueeze(1).to_broadcast([P, 2, s1 - s0]),
                 op=MULT,
             )
 
-        def late_pair(e, s0, s1, number):
-            bank = psum.tile([P, 2, s1 - s0], F32, name=f"late{e}{s0}", tag=f"bank{number}")
-            for t in range(2):
-                ybank[e, t, s0] = bank[:, t, :]
-                for a in range(PASSES):
-                    multiply(e, a, t, s0, s1, None)
-            for t in range(2):
-                relu(e, t, s0, s1)
-
-        def apply_gate(engine, e, u, s0, s1, tag=None, part=None):
-            if part is None:
-                c[e, u, s0] = keep.tile([P, s1 - s0, 2], BF16, name=f"c{e}{u}{s0}", tag=tag or f"c{e}{u}{s0}", align_bytes=64)
-            else:
-                c[e, u, s0] = part[:, s0:s1, :]
-            (gate_vector if engine == "v" else gate_gpsimd)(e, u, s0, s1)
-
-        def scatter(e, u, s0, s1, values):
+        def scatter(e, u):
             nc.vector.tensor_copy(
-                window[u][:].indirect(offsets[:, (e * C + s0) // 16 : (e * C + s1) // 16]),
-                values.rearrange("p s t -> p (s t)").bitcast(F32),
+                window[u][:].indirect(offsets[:, e * C // 16 : (e + 1) * C // 16]),
+                c[e, u].rearrange("p s t -> p (s t)").bitcast(F32),
             )
 
-        def weave(engine, q, lo=0, hi=Q):
-            move(engine, woven[q][:, lo:hi, :], halves[q][:, :, lo:hi].rearrange("p u t -> p t u"))
-
-        def stage(engine, q, u):
-            move(engine, halves[q][:, u, :], window[u][:, q * Q : (q + 1) * Q])
-
-        def quantize_c(q, lo=0, hi=Q):
-            nc.vector.quantize_mx(
-                out=ccodes[q][:, lo:hi].bitcast(FP8X4),
-                scales=cbytes[q][:, lo:hi],
-                in_=woven[q][:, lo:hi, :].rearrange("p t u -> p (t u)").bitcast(BF16),
+        def group_wp(engine, g):
+            order = "p x i j" if engine == "gpsimd" else "p x j i"
+            move(
+                engine,
+                wpgrouped[g][:, 0:P, :].rearrange("p (x i) j -> " + order, i=4),
+                wpraw[g // 2][:, :, g % 2 * P : (g % 2 + 1) * P].rearrange("p j (x i) -> " + order, i=4),
             )
 
-        def project(t0, t1, g, engines, banks):
-            result = keep.tile([P, t1 - t0], F32, name=f"result{t0}{g}", align_bytes=64)
-            edges = [t0] + [t for t in (BANK,) if t0 < t < t1 and t1 - t0 > BANK] + [t1]
-            for engine, b0, b1 in zip(engines, edges, edges[1:]):
-                number = banks.pop(0)
-                banks.append(number)
-                bank = psum.tile([P, b1 - b0], F32, name=f"obank{b0}{g}", tag=f"bank{number}")
-                for lo, hi in zip(CUTS, CUTS[1:]):
-                    if b0 <= lo and hi <= b1:
-                        nc.tensor.matmul_mx(
-                            out=bank[:, lo - b0 : hi - b0],
-                            lhsT=wpcodes[g][:, 0:P].bitcast(FP8X4),
-                            lhsT_scale=wpbytes[:, g * P : (g + 1) * P],
-                            rhs=ccodes[lo // Q][:, lo % Q : lo % Q + hi - lo].bitcast(FP8X4),
-                            rhs_scale=cbytes[lo // Q][:, lo % Q : lo % Q + hi - lo],
-                            start=True,
-                            stop=True,
-                        )
-                move(engine, result[:, b0 - t0 : b1 - t0], bank[:])
-            nc.sync.dma_start(out[g * P : (g + 1) * P, t0:t1], result[:])
+        def quantize_wp(g0, g1):
+            width = (g1 - g0) * P
+            grouped = wpgrouped[g0][:, 0:width, :].rearrange("p f j -> p (f j)")
+            quantize(wpcodes[g0][:, 0:width], wpbytes[:, g0 * P : g1 * P], grouped)
 
-        def piece(a, t0, t1, shares, tag=None):
-            name = f"xgrouped{a}{t0}"
-            xgrouped[a, t0] = keep.tile([P, t1 - t0, J], BF16, name=name, tag=tag or name, align_bytes=64)
-            lo = t0
-            for engine, count in shares:
-                group_x(engine, a, t0, lo, lo + count)
-                lo = lo + count
-            quantize_x(a, t0, t1)
+        def stage(q, u):
+            move("scalar", staged[q][:, u, :], window[u][:, q * Q : (q + 1) * Q])
 
-        piece(1, 0, 512, [("v", XV1), ("s", 512 - XV1)])
-        piece(1, 512, T, [("v", XV1), ("s", 512 - XV1)])
-        gather_words(1, 0, E, "gcodes1")
-        piece(0, 256, 512, [("s", 256)])
-        piece(0, 0, 256, [("v", XB), ("s", 256 - XB)])
-        piece(0, 512, T, [("v", XV), ("s", 512 - XV)])
-        gather_words(0, 0, E, "gcodes0")
-        gates = keep.tile([P, S], F32, name="gates", tag=GT, align_bytes=64)
-        nc.scalar.copy(out=gates[:].rearrange("p (m r) -> p m r", r=R), in_=gbank[:].rearrange("p r m -> p m r"))
-        gather_bytes(0, "gbytes0")
-        early = [(0, H, 2), (H, C, 4)]
+        def weave(q):
+            move("vector", woven[q], staged[q].rearrange("p u t -> p t u"))
+
+        def quantize_c(q):
+            t0 = max(first for first, end in RANGES if first <= q * Q)
+            lo = q * Q - t0
+            grouped = woven[q].rearrange("p t u -> p (t u)").bitcast(BF16)
+            quantize(ccodes[t0][:, lo : lo + Q], cbytes[t0][:, lo : lo + Q], grouped)
+
+        def project(t0, t1, g, engine, bank):
+            sums = psum.tile([P, t1 - t0], F32, name=f"obank{t0}{g}", tag=f"bank{bank}")
+            nc.tensor.matmul_mx(
+                out=sums[:],
+                lhsT=wpcodes[g][:, 0:P].bitcast(FP8X4),
+                lhsT_scale=wpbytes[:, g * P : (g + 1) * P],
+                rhs=ccodes[t0].bitcast(FP8X4),
+                rhs_scale=cbytes[t0],
+                start=True,
+                stop=True,
+            )
+            result = sbuf([P, t1 - t0], F32, f"result{t0}{g}")
+            move(engine, result, sums[:])
+            nc.sync.dma_start(out[g * P : (g + 1) * P, t0:t1], result)
+
+        x_vector = HALF * EIGHTHS // 8
+        quantize_x(1, 0, HALF, x_vector)
+        quantize_x(1, HALF, T, x_vector)
+        gather_words(1)
+        quantize_x(0, Q, HALF, 0)
+        quantize_x(0, 0, Q, X_BUSY)
+        quantize_x(0, HALF, T, x_vector)
+        gather_words(0)
+        gates = sbuf([P, S], F32, "gates", f"xraw0{HALF}")
+        nc.scalar.copy(out=gates.rearrange("p (m r) -> p m r", r=R), in_=gbank[:].rearrange("p r m -> p m r"))
+        gather_bytes(0)
+
+        halved = [(0, C // 2, 2), (C // 2, C, 4)]
+        early = [(0, C, 2)]
         late = [(0, C, 0)]
-        group_w("g", 0, 0, 1, 0, W00G, "xgrouped0512")
-        group_w("s", 0, 0, 0)
-        group_w("v", 0, 0, 1, W00G, W00G + W00V)
-        group_w("s", 0, 0, 1, W00G + W00V, P)
-        quantize_w(0, 0, 0)
-        expert_pair(0, 0, 0, late)
-        quantize_w(0, 0, 1)
-        expert_pair(0, 0, 1, early)
-        group_w("v", 0, 1, 1, 0, W01A)
-        group_w("s", 0, 1, 1, W01A, P)
-        group_w("v", 0, 1, 0, 0, W01B)
-        group_w("s", 0, 1, 0, W01B, P)
-        quantize_w(0, 1, 1)
-        expert_pair(0, 1, 1, early)
-        quantize_w(0, 1, 0)
-        expert_pair(0, 1, 0, late)
+        group_w("gpsimd", 0, 0, 1, 0, W_GPSIMD, f"xgrouped0{HALF}")
+        group_w("scalar", 0, 0, 0, 0, P)
+        group_w("scalar", 0, 0, 1, W_GPSIMD, P)
+        multiply(0, 0, 0, late)
+        multiply(0, 0, 1, halved)
+        w_vector = P * EIGHTHS // 8
+        group_w("vector", 0, 1, 1, 0, w_vector)
+        group_w("scalar", 0, 1, 1, w_vector, P)
+        group_w("vector", 0, 1, 0, 0, P - w_vector)
+        group_w("scalar", 0, 1, 0, P - w_vector, P)
+        multiply(0, 1, 1, halved)
+        multiply(0, 1, 0, late)
         gather_bytes(1, "wraw01")
-        c01 = keep.tile([P, C, 2], BF16, name="c01", align_bytes=64)
-        apply_gate("v", 0, 1, 0, H, part=c01)
-        apply_gate("v", 0, 1, H, C, part=c01)
-        scatter(0, 1, 0, C, c01[:])
-        c00 = keep.tile([P, C, 2], BF16, name="c00", tag=CT, align_bytes=64)
-        apply_gate("g", 0, 0, 0, G0, part=c00)
-        if G0 < C:
-            apply_gate("v", 0, 0, G0, C, part=c00)
-        group_w("g", 1, 0, GU, 0, W10G, "wgrouped010")
-        group_w("s", 1, 0, 1 - GU)
-        group_w("s", 1, 0, GU, W10G, P)
-        quantize_w(1, 0, 1)
-        for n in range(W1):
-            idle = psum.tile([P, C], F32, name=f"idle1{n}", tag="bank7")
-            nc.tensor.matmul_mx(out=idle[:], lhsT=wcodes[1, 0, 1][:, 0:P].bitcast(FP8X4), lhsT_scale=wbytes[1, 0, 1][:, 0:P], rhs=wcodes[1, 0, 1][:].bitcast(FP8X4), rhs_scale=wbytes[1, 0, 1][:], start=True, stop=True)
-        expert_pair(1, 0, 1, early)
-        quantize_w(1, 0, 0)
-        expert_pair(1, 0, 0, late)
-        group_w("v", 1, 1, 1, 0, W11A)
-        group_w("s", 1, 1, 1, W11A, P)
-        group_w("v", 1, 1, 0, 0, W11B)
-        group_w("s", 1, 1, 0, W11B, P)
-        quantize_w(1, 1, 1)
-        expert_pair(1, 1, 1, early)
-        quantize_w(1, 1, 0)
-        expert_pair(1, 1, 0, late)
-        scatter(0, 0, 0, C, c00[:])
-        first = keep.tile([P, P, J], BF16, name="wpfirst", align_bytes=64)
-        middle = keep.tile([P, 2 * P, J], BF16, name="wpmiddle", tag="bias", align_bytes=64)
-        wpgrouped = [first[:], middle[:], middle[:, P:, :]]
-        for g in range(3):
-            group_wp("s", g * P, (g + 1) * P)
-        c11 = keep.tile([P, C, 2], BF16, name="c11", align_bytes=64)
-        apply_gate("g", 1, 1, 0, A1, part=c11)
-        apply_gate("v", 1, 1, A1, C, part=c11)
-        c10 = keep.tile([P, C, 2], BF16, name="c10", align_bytes=64)
-        apply_gate("v", 1, 0, 0, B1, part=c10)
-        apply_gate("g", 1, 0, B1, C, part=c10)
-        scatter(1, 1, 0, C, c11[:])
-        fourth = keep.tile([P, P, J], BF16, name="wpfourth", tag="y10", align_bytes=64)
-        wpgrouped.append(fourth[:])
-        group_wp("g", 3 * P, M)
-        move("s", woven[0][:, :, 1], window[1][:, 0:Q])
+        for s0, s1, bank in halved:
+            gate_vector(0, 1, s0, s1)
+        scatter(0, 1)
+        gate_gpsimd(0, 0, 0, LATE_GPSIMD)
+        gate_vector(0, 0, LATE_GPSIMD, C)
+
+        group_w("gpsimd", 1, 0, 0, 0, W_GPSIMD, "wgrouped010")
+        group_w("scalar", 1, 0, 1, 0, P)
+        group_w("scalar", 1, 0, 0, W_GPSIMD, P)
+        multiply(1, 0, 1, early)
+        multiply(1, 0, 0, late)
+        group_w("scalar", 1, 1, 1, 0, P)
+        group_w("vector", 1, 1, 0, 0, W_LAST)
+        group_w("scalar", 1, 1, 0, W_LAST, P)
+        multiply(1, 1, 1, early)
+        multiply(1, 1, 0, late)
+        scatter(0, 0)
+        wpgrouped[0] = sbuf([P, P, J], BF16, "wpgrouped0")
+        wpgrouped[1] = sbuf([P, 2 * P, J], BF16, "wpgrouped1", "bias")
+        wpgrouped[2] = wpgrouped[1][:, P:, :]
+        for g in range(G - 1):
+            group_wp("scalar", g)
+        gate_gpsimd(1, 1, 0, EARLY_GPSIMD)
+        gate_vector(1, 1, EARLY_GPSIMD, C)
+        gate_vector(1, 0, 0, C - LATE_GPSIMD)
+        gate_gpsimd(1, 0, C - LATE_GPSIMD, C)
+        scatter(1, 1)
+        wpgrouped[3] = sbuf([P, P, J], BF16, "wpgrouped3", "y10")
+        group_wp("gpsimd", G - 1)
+
+        move("scalar", woven[0][:, :, 1], window[1][:, 0:Q])
         for q in range(1, CHUNKS):
-            stage("s", q, 1)
-        scatter(1, 0, 0, C, c10[:])
-        wpcodes = {0: keep.tile([P, P], U32, name="wpcodes0", tag=T0, align_bytes=64)[:]}
+            stage(q, 1)
+        scatter(1, 0)
+        wpcodes[0] = sbuf([P, P], U32, "wpcodes0", f"xraw0{HALF}")
         quantize_wp(0, 1)
-        others = keep.tile([P, 3 * P], U32, name="wpcodes1", tag="c10", align_bytes=64)
+        others = sbuf([P, (G - 1) * P], U32, "wpcodes1", "c10")
         for g in range(1, G):
             wpcodes[g] = others[:, (g - 1) * P :]
-        move("v", woven[0][:, :, 0], window[0][:, 0:Q])
-        quantize_wp(1, 3)
+        move("vector", woven[0][:, :, 0], window[0][:, 0:Q])
+        quantize_wp(1, G - 1)
         quantize_c(0)
         for q in range(1, CHUNKS):
-            stage("s", q, 0)
-        quantize_wp(3, 4)
-        weave("v", 1)
-        weave(W2, 2)
-        quantize_c(1)
-        weave("v", 3)
-        quantize_c(2)
-        quantize_c(3)
-        banks = list(range(8))
-        for t0, t1, g, engines in PIECES:
-            project(t0, t1, g, engines, banks)
+            stage(q, 0)
+        quantize_wp(G - 1, G)
+        weave(1)
+        for q in range(1, CHUNKS):
+            if q + 1 < CHUNKS:
+                weave(q + 1)
+            quantize_c(q)
+
+        for n, (t0, t1) in enumerate(RANGES):
+            for g in range(G):
+                engine = "vector" if t1 == T and g % 2 == 0 else "scalar"
+                project(t0, t1, g, engine, (n * G + g) % BANKS)

@@ -33,9 +33,9 @@ RANGES = [(0, Q), (Q, 2 * Q), (2 * Q, T)]
 EIGHTHS = 5
 X_BUSY = 112
 W_LAST = 104
-W_GPSIMD = 88
+W_GPSIMD = 96
 LATE_GPSIMD = 208
-EARLY_GPSIMD = 64
+EARLY_GPSIMD = 88
 
 
 def tile_moe_nxt_lin_relu_kernel(tc, xT, w, b, wp, gate, offs, out):
@@ -241,7 +241,6 @@ def tile_moe_nxt_lin_relu_kernel(tc, xT, w, b, wp, gate, offs, out):
         gather_bytes(0)
 
         halved = [(0, C // 2, 2), (C // 2, C, 4)]
-        early = [(0, C, 2)]
         late = [(0, C, 0)]
         group_w("gpsimd", 0, 0, 1, 0, W_GPSIMD, f"xgrouped0{HALF}")
         group_w("scalar", 0, 0, 0, 0, P)
@@ -265,42 +264,41 @@ def tile_moe_nxt_lin_relu_kernel(tc, xT, w, b, wp, gate, offs, out):
         group_w("gpsimd", 1, 0, 0, 0, W_GPSIMD, "wgrouped010")
         group_w("scalar", 1, 0, 1, 0, P)
         group_w("scalar", 1, 0, 0, W_GPSIMD, P)
-        multiply(1, 0, 1, early)
+        multiply(1, 0, 1, halved)
         multiply(1, 0, 0, late)
         group_w("scalar", 1, 1, 1, 0, P)
         group_w("vector", 1, 1, 0, 0, W_LAST)
         group_w("scalar", 1, 1, 0, W_LAST, P)
-        multiply(1, 1, 1, early)
+        multiply(1, 1, 1, halved)
         multiply(1, 1, 0, late)
         scatter(0, 0)
         wpgrouped[0] = sbuf([P, P, J], BF16, "wpgrouped0")
-        wpgrouped[1] = sbuf([P, 2 * P, J], BF16, "wpgrouped1", "bias")
-        wpgrouped[2] = wpgrouped[1][:, P:, :]
+        after_relus = sbuf([P, (G - 1) * P, J], BF16, "wpgrouped1", "bias")
+        for g in range(1, G):
+            wpgrouped[g] = after_relus[:, (g - 1) * P :, :]
         for g in range(G - 1):
             group_wp("scalar", g)
         gate_gpsimd(1, 1, 0, EARLY_GPSIMD)
         gate_vector(1, 1, EARLY_GPSIMD, C)
         gate_vector(1, 0, 0, C - LATE_GPSIMD)
         gate_gpsimd(1, 0, C - LATE_GPSIMD, C)
-        scatter(1, 1)
-        wpgrouped[3] = sbuf([P, P, J], BF16, "wpgrouped3", "y10")
         group_wp("gpsimd", G - 1)
+        scatter(1, 1)
 
         move("scalar", woven[0][:, :, 1], window[1][:, 0:Q])
         for q in range(1, CHUNKS):
             stage(q, 1)
         scatter(1, 0)
-        wpcodes[0] = sbuf([P, P], U32, "wpcodes0", f"xraw0{HALF}")
-        quantize_wp(0, 1)
-        others = sbuf([P, (G - 1) * P], U32, "wpcodes1", "c10")
-        for g in range(1, G):
-            wpcodes[g] = others[:, (g - 1) * P :]
+        for g, tag in ((0, "c10"), (2, None)):
+            wpcodes[g] = sbuf([P, 2 * P], U32, f"wpcodes{g}", tag)
+            wpcodes[g + 1] = wpcodes[g][:, P:]
         move("vector", woven[0][:, :, 0], window[0][:, 0:Q])
-        quantize_wp(1, G - 1)
+        quantize_wp(0, 1)
+        quantize_wp(1, 2)
         quantize_c(0)
         for q in range(1, CHUNKS):
             stage(q, 0)
-        quantize_wp(G - 1, G)
+        quantize_wp(2, G)
         weave(1)
         for q in range(1, CHUNKS):
             if q + 1 < CHUNKS:

@@ -24,18 +24,18 @@ KP = P * J
 PASSES = K // KP
 G = M // P
 R = S // P
-HALF = T // 2
 Q = T // 4
 CHUNKS = T // Q
 BANKS = 8
 RANGES = [(0, Q), (Q, 2 * Q), (2 * Q, T)]
 
-EIGHTHS = 5
-X_BUSY = 112
-W_LAST = 104
-W_GPSIMD = 96
-LATE_GPSIMD = 208
-EARLY_GPSIMD = 88
+W01_EARLY = 96
+W01_LATE = 48
+W10_GPSIMD = 112
+X_VECTOR = 592
+W_LAST = 96
+W_GPSIMD = 72
+EARLY_GPSIMD = 112
 
 
 def tile_moe_nxt_lin_relu_kernel(tc, xT, w, b, wp, gate, offs, out):
@@ -51,11 +51,10 @@ def tile_moe_nxt_lin_relu_kernel(tc, xT, w, b, wp, gate, offs, out):
         bias = sbuf([P, J * E], F32, "bias")
         gate_row = sbuf([P, R], F32, "gate_row")
         nc.scalar.dma_start(gate_row, gate[0, :].rearrange("(p r) -> p r", r=R))
-        x_loads = [(1, 0, T), (0, 0, HALF), (0, HALF, T)]
         xraw = {}
-        for a, t0, t1 in x_loads:
-            xraw[a, t0] = sbuf([P, J, t1 - t0], F32, f"xraw{a}{t0}")
-            nc.sync.dma_start(xraw[a, t0], xT[a * KP : (a + 1) * KP, t0:t1].rearrange("(p j) t -> p j t", j=J))
+        for a in (1, 0):
+            xraw[a] = sbuf([P, J, T], F32, f"xraw{a}")
+            nc.sync.dma_start(xraw[a], xT[a * KP : (a + 1) * KP, :].rearrange("(p j) t -> p j t", j=J))
             if a == 1:
                 nc.sync.dma_start(offsets[:], offs)
                 nc.scalar.dma_start(bias, b.rearrange("(p t) e -> p (t e)", t=J))
@@ -112,21 +111,28 @@ def tile_moe_nxt_lin_relu_kernel(tc, xT, w, b, wp, gate, offs, out):
         def quantize(codes, scales, grouped):
             nc.vector.quantize_mx(out=codes.bitcast(FP8X4), scales=scales, in_=grouped)
 
-        def quantize_x(a, t0, t1, by_vector):
-            loaded = max(first for (pa, first, end) in x_loads if pa == a and first <= t0)
-            grouped = sbuf([P, t1 - t0, J], BF16, f"xgrouped{a}{t0}")
-            for engine, lo, hi in (("vector", 0, by_vector), ("scalar", by_vector, t1 - t0)):
-                if lo < hi:
-                    move(
-                        engine,
-                        grouped[:, lo:hi, :].rearrange("p (x i) j -> p x j i", i=4),
-                        xraw[a, loaded][:, :, t0 - loaded + lo : t0 - loaded + hi].rearrange("p j (x i) -> p x j i", i=4),
-                    )
-            quantize(xcodes[a][:, t0:t1], xbytes[4 * a :, t0:t1], grouped.rearrange("p t j -> p (t j)"))
+        def quantize_x(a):
+            grouped = sbuf([P, T, J], BF16, f"xgrouped{a}")
+            for engine, lo, hi in (
+                ("vector", 0, Q),
+                ("vector", Q, X_VECTOR),
+                ("scalar", X_VECTOR, T - Q),
+                ("scalar", T - Q, T),
+            ):
+                move(
+                    engine,
+                    grouped[:, lo:hi, :].rearrange("p (x i) j -> p x j i", i=4),
+                    xraw[a][:, :, lo:hi].rearrange("p j (x i) -> p x j i", i=4),
+                )
+            for t0 in range(0, T, Q):
+                part = grouped[:, t0 : t0 + Q, :].rearrange("p t j -> p (t j)")
+                quantize(xcodes[a][:, t0 : t0 + Q], xbytes[4 * a :, t0 : t0 + Q], part)
 
-        def gather_words(a):
-            gcodes[a] = sbuf([P, S], U32, f"gcodes{a}")
-            nc.vector.tensor_copy(gcodes[a], xcodes[a][:].indirect(offsets[:]))
+        def gather_words(a, e0, e1, tag=None):
+            words = sbuf([P, (e1 - e0) * C], U32, f"gcodes{a}{e0}", tag)
+            nc.vector.tensor_copy(words, xcodes[a][:].indirect(offsets[:, e0 * C // 16 : e1 * C // 16]))
+            for e in range(e0, e1):
+                gcodes[a, e] = words[:, (e - e0) * C : (e - e0 + 1) * C]
 
         def gather_bytes(e, tag=None):
             gbytes[e] = sbuf([P, C], U8, f"gbytes{e}", tag)
@@ -156,7 +162,7 @@ def tile_moe_nxt_lin_relu_kernel(tc, xT, w, b, wp, gate, offs, out):
                         out=ybank[e, t, s0][:],
                         lhsT=wcodes[e, a, u][:, i * P : (i + 1) * P].bitcast(FP8X4),
                         lhsT_scale=wbytes[e, a, u][:, i * P : (i + 1) * P],
-                        rhs=gcodes[a][:, e * C + s0 : e * C + s1].bitcast(FP8X4),
+                        rhs=gcodes[a, e][:, s0:s1].bitcast(FP8X4),
                         rhs_scale=gbytes[e][4 * a :, s0:s1],
                         start=(a == 0),
                         stop=(a == PASSES - 1),
@@ -228,42 +234,37 @@ def tile_moe_nxt_lin_relu_kernel(tc, xT, w, b, wp, gate, offs, out):
             move(engine, result, sums[:])
             nc.sync.dma_start(out[g * P : (g + 1) * P, t0:t1], result)
 
-        x_vector = HALF * EIGHTHS // 8
-        quantize_x(1, 0, HALF, x_vector)
-        quantize_x(1, HALF, T, x_vector)
-        gather_words(1)
-        quantize_x(0, Q, HALF, 0)
-        quantize_x(0, 0, Q, X_BUSY)
-        quantize_x(0, HALF, T, x_vector)
-        gather_words(0)
-        gates = sbuf([P, S], F32, "gates", f"xraw0{HALF}")
+        quantize_x(1)
+        gather_words(1, 0, E)
+        gates = sbuf([P, S], F32, "gates", "xraw1")
         nc.scalar.copy(out=gates.rearrange("p (m r) -> p m r", r=R), in_=gbank[:].rearrange("p r m -> p m r"))
+        quantize_x(0)
+        gather_words(0, 0, 1)
         gather_bytes(0)
 
         halved = [(0, C // 2, 2), (C // 2, C, 4)]
         late = [(0, C, 0)]
-        group_w("gpsimd", 0, 0, 1, 0, W_GPSIMD, f"xgrouped0{HALF}")
-        group_w("scalar", 0, 0, 0, 0, P)
-        group_w("scalar", 0, 0, 1, W_GPSIMD, P)
-        multiply(0, 0, 0, late)
+        group_w("gpsimd", 0, 0, 0, 0, W_GPSIMD, "xgrouped0")
+        group_w("scalar", 0, 0, 1, 0, P)
+        group_w("scalar", 0, 0, 0, W_GPSIMD, P)
         multiply(0, 0, 1, halved)
-        w_vector = P * EIGHTHS // 8
-        group_w("vector", 0, 1, 1, 0, w_vector)
-        group_w("scalar", 0, 1, 1, w_vector, P)
-        group_w("vector", 0, 1, 0, 0, P - w_vector)
-        group_w("scalar", 0, 1, 0, P - w_vector, P)
+        multiply(0, 0, 0, late)
+        group_w("vector", 0, 1, 1, 0, W01_EARLY)
+        group_w("scalar", 0, 1, 1, W01_EARLY, P)
+        group_w("vector", 0, 1, 0, 0, W01_LATE)
+        group_w("scalar", 0, 1, 0, W01_LATE, P)
         multiply(0, 1, 1, halved)
         multiply(0, 1, 0, late)
         gather_bytes(1, "wraw01")
+        gather_words(0, 1, E, "wgrouped011")
         for s0, s1, bank in halved:
             gate_vector(0, 1, s0, s1)
         scatter(0, 1)
-        gate_gpsimd(0, 0, 0, LATE_GPSIMD)
-        gate_vector(0, 0, LATE_GPSIMD, C)
+        gate_gpsimd(0, 0, 0, C)
 
-        group_w("gpsimd", 1, 0, 0, 0, W_GPSIMD, "wgrouped010")
+        group_w("gpsimd", 1, 0, 0, 0, W10_GPSIMD, "wgrouped010")
         group_w("scalar", 1, 0, 1, 0, P)
-        group_w("scalar", 1, 0, 0, W_GPSIMD, P)
+        group_w("scalar", 1, 0, 0, W10_GPSIMD, P)
         multiply(1, 0, 1, halved)
         multiply(1, 0, 0, late)
         group_w("scalar", 1, 1, 1, 0, P)
@@ -280,8 +281,7 @@ def tile_moe_nxt_lin_relu_kernel(tc, xT, w, b, wp, gate, offs, out):
             group_wp("scalar", g)
         gate_gpsimd(1, 1, 0, EARLY_GPSIMD)
         gate_vector(1, 1, EARLY_GPSIMD, C)
-        gate_vector(1, 0, 0, C - LATE_GPSIMD)
-        gate_gpsimd(1, 0, C - LATE_GPSIMD, C)
+        gate_gpsimd(1, 0, 0, C)
         group_wp("gpsimd", G - 1)
         scatter(1, 1)
 
@@ -289,16 +289,16 @@ def tile_moe_nxt_lin_relu_kernel(tc, xT, w, b, wp, gate, offs, out):
         for q in range(1, CHUNKS):
             stage(q, 1)
         scatter(1, 0)
-        for g, tag in ((0, "c10"), (2, None)):
+        for g, tag in ((0, "y10"), (2, None)):
             wpcodes[g] = sbuf([P, 2 * P], U32, f"wpcodes{g}", tag)
             wpcodes[g + 1] = wpcodes[g][:, P:]
-        move("vector", woven[0][:, :, 0], window[0][:, 0:Q])
         quantize_wp(0, 1)
         quantize_wp(1, 2)
+        move("vector", woven[0][:, :, 0], window[0][:, 0:Q])
+        quantize_wp(2, G)
         quantize_c(0)
         for q in range(1, CHUNKS):
             stage(q, 0)
-        quantize_wp(2, G)
         weave(1)
         for q in range(1, CHUNKS):
             if q + 1 < CHUNKS:

@@ -25,9 +25,15 @@ PASSES = K // KP
 G = M // P
 R = S // P
 Q = T // 4
-CHUNKS = T // Q
+CHUNKS = [(0, 128), (128, 256), (256, 512), (512, 768), (768, 1024)]
+DIRECT = 1
+TAIL = "p01 p12 d0 p24 q0 w1 w2 q1 s4 w3 q2 q4 q3"
+MERGE = [1, 2, 1]
+STAGE0 = [1, 2, 4, 3]
+LAST = [(g, n) for g in range(4) for n in (3, 4)]
+OUTENG = ["ssss", "ssss", "ssss", "vvvv", "ssss"]
 BANKS = 8
-RANGES = [(0, Q), (Q, 2 * Q), (2 * Q, T)]
+RANGES = CHUNKS
 
 W01_EARLY = 96
 W01_LATE = 48
@@ -92,8 +98,8 @@ def tile_moe_nxt_lin_relu_kernel(tc, xT, w, b, wp, gate, offs, out):
         ybank = {}
         y = {(e, u): sbuf([P, 2, C], F32, f"y{e}{u}") for e in range(E) for u in range(2)}
         c = {(e, u): sbuf([P, C, 2], BF16, f"c{e}{u}") for e in range(E) for u in range(2)}
-        staged = {q: sbuf([P, 2, Q], F32, f"staged{q}") for q in range(1, CHUNKS)}
-        woven = [sbuf([P, Q, 2], F32, f"woven{q}") for q in range(CHUNKS)]
+        staged = {q: sbuf([P, 2, CHUNKS[q][1] - CHUNKS[q][0]], F32, f"staged{q}") for q in range(DIRECT, len(CHUNKS))}
+        woven = [sbuf([P, t1 - t0, 2], F32, f"woven{t0}") for t0, t1 in CHUNKS]
         ccodes = {t0: sbuf([P, t1 - t0], U32, f"ccodes{t0}") for t0, t1 in RANGES}
         cbytes = {t0: sbuf([P, t1 - t0], U8, f"cbytes{t0}") for t0, t1 in RANGES}
         wpgrouped = {}
@@ -208,31 +214,33 @@ def tile_moe_nxt_lin_relu_kernel(tc, xT, w, b, wp, gate, offs, out):
             quantize(wpcodes[g0][:, 0:width], wpbytes[:, g0 * P : g1 * P], grouped)
 
         def stage(q, u):
-            move("scalar", staged[q][:, u, :], window[u][:, q * Q : (q + 1) * Q])
+            move("scalar", staged[q][:, u, :], window[u][:, CHUNKS[q][0] : CHUNKS[q][1]])
 
         def weave(q):
             move("vector", woven[q], staged[q].rearrange("p u t -> p t u"))
 
         def quantize_c(q):
-            t0 = max(first for first, end in RANGES if first <= q * Q)
-            lo = q * Q - t0
+            t0 = max(first for first, end in RANGES if first <= CHUNKS[q][0])
+            lo = CHUNKS[q][0] - t0
+            hi = CHUNKS[q][1] - t0
             grouped = woven[q].rearrange("p t u -> p (t u)").bitcast(BF16)
-            quantize(ccodes[t0][:, lo : lo + Q], cbytes[t0][:, lo : lo + Q], grouped)
+            quantize(ccodes[t0][:, lo:hi], cbytes[t0][:, lo:hi], grouped)
 
-        def project(t0, t1, g, engine, bank):
-            sums = psum.tile([P, t1 - t0], F32, name=f"obank{t0}{g}", tag=f"bank{bank}")
-            nc.tensor.matmul_mx(
-                out=sums[:],
-                lhsT=wpcodes[g][:, 0:P].bitcast(FP8X4),
-                lhsT_scale=wpbytes[:, g * P : (g + 1) * P],
-                rhs=ccodes[t0].bitcast(FP8X4),
-                rhs_scale=cbytes[t0],
-                start=True,
-                stop=True,
-            )
-            result = sbuf([P, t1 - t0], F32, f"result{t0}{g}")
+        def project(t0, t1, g0, g1, engine, bank):
+            sums = psum.tile([P, g1 - g0, t1 - t0], F32, name=f"obank{t0}{g0}", tag=f"bank{bank}")
+            for g in range(g0, g1):
+                nc.tensor.matmul_mx(
+                    out=sums[:, g - g0, :],
+                    lhsT=wpcodes[g][:, 0:P].bitcast(FP8X4),
+                    lhsT_scale=wpbytes[:, g * P : (g + 1) * P],
+                    rhs=ccodes[t0].bitcast(FP8X4),
+                    rhs_scale=cbytes[t0],
+                    start=True,
+                    stop=True,
+                )
+            result = sbuf([P, g1 - g0, t1 - t0], F32, f"result{t0}{g0}")
             move(engine, result, sums[:])
-            nc.sync.dma_start(out[g * P : (g + 1) * P, t0:t1], result)
+            nc.sync.dma_start(out[g0 * P : g1 * P, t0:t1].rearrange("(g p) t -> p g t", p=P), result)
 
         quantize_x(1)
         gather_words(1, 0, E)
@@ -285,27 +293,64 @@ def tile_moe_nxt_lin_relu_kernel(tc, xT, w, b, wp, gate, offs, out):
         group_wp("gpsimd", G - 1)
         scatter(1, 1)
 
-        move("scalar", woven[0][:, :, 1], window[1][:, 0:Q])
-        for q in range(1, CHUNKS):
+        for q in range(DIRECT):
+            t0, t1 = CHUNKS[q]
+            move("scalar", woven[q][:, :, 1], window[1][:, t0:t1])
+        for q in range(DIRECT, len(CHUNKS)):
             stage(q, 1)
         scatter(1, 0)
         for g, tag in ((0, "y10"), (2, None)):
             wpcodes[g] = sbuf([P, 2 * P], U32, f"wpcodes{g}", tag)
             wpcodes[g + 1] = wpcodes[g][:, P:]
-        quantize_wp(0, 1)
-        quantize_wp(1, 2)
-        move("vector", woven[0][:, :, 0], window[0][:, 0:Q])
-        quantize_wp(2, G)
-        quantize_c(0)
-        for q in range(1, CHUNKS):
+        for q in STAGE0:
             stage(q, 0)
-        weave(1)
-        for q in range(1, CHUNKS):
-            if q + 1 < CHUNKS:
-                weave(q + 1)
-            quantize_c(q)
+        for step in TAIL.split():
+            q = int(step[1])
+            if step[0] == "d":
+                t0, t1 = CHUNKS[q]
+                move("vector", woven[q][:, :, 0], window[0][:, t0:t1])
+            elif step[0] == "w":
+                weave(q)
+            elif step[0] == "s":
+                move("scalar", woven[q], staged[q].rearrange("p u t -> p t u"))
+            elif step[0] == "q":
+                quantize_c(q)
+            elif step[0] == "h":
+                warm = psum.tile([P, 2 * P], F32, name="warm", tag="bank7")
+                for i in range(q):
+                    nc.tensor.matmul_mx(
+                        out=warm[:],
+                        lhsT=wpcodes[0][:, 0:P].bitcast(FP8X4),
+                        lhsT_scale=wpbytes[:, 0:P],
+                        rhs=wpcodes[0].bitcast(FP8X4),
+                        rhs_scale=wpbytes[:, 0 : 2 * P],
+                        start=(i == 0),
+                        stop=(i == q - 1),
+                    )
+            else:
+                quantize_wp(q, int(step[2]))
 
-        for n, (t0, t1) in enumerate(RANGES):
-            for g in range(G):
-                engine = "vector" if t1 == T and g % 2 == 0 else "scalar"
-                project(t0, t1, g, engine, (n * G + g) % BANKS)
+        bank = 0
+        for n, (t0, t1) in enumerate(RANGES[: len(MERGE)]):
+            for g in range(0, G, MERGE[n]):
+                project(t0, t1, g, g + MERGE[n], {"v": "vector", "s": "scalar"}[OUTENG[n][g]], bank % BANKS)
+                bank = bank + 1
+        if len(MERGE) < len(RANGES):
+            first = RANGES[len(MERGE)][0]
+            results = [sbuf([P, T - first], F32, f"result{first}{g}") for g in range(G)]
+            for g, n in LAST:
+                t0, t1 = RANGES[n]
+                sums = psum.tile([P, t1 - t0], F32, name=f"obank{t0}{g}", tag=f"bank{bank % BANKS}")
+                bank = bank + 1
+                nc.tensor.matmul_mx(
+                    out=sums[:],
+                    lhsT=wpcodes[g][:, 0:P].bitcast(FP8X4),
+                    lhsT_scale=wpbytes[:, g * P : (g + 1) * P],
+                    rhs=ccodes[t0].bitcast(FP8X4),
+                    rhs_scale=cbytes[t0],
+                    start=True,
+                    stop=True,
+                )
+                move({"v": "vector", "s": "scalar"}[OUTENG[n][g]], results[g][:, t0 - first : t1 - first], sums[:])
+                if t1 == T:
+                    nc.sync.dma_start(out[g * P : (g + 1) * P, first:T], results[g])

@@ -25,23 +25,14 @@ PASSES = K // KP
 G = M // P
 R = S // P
 Q = T // 4
-CHUNKS = [(0, 128), (128, 256), (256, 512), (512, 768), (768, 1024)]
-DIRECT = 1
-TAIL = "p01 p12 d0 p24 q0 w1 w2 q1 s4 w3 q2 q4 q3"
-MERGE = [1, 2, 1]
-STAGE0 = [1, 2, 4, 3]
-LAST = [(g, n) for g in range(4) for n in (3, 4)]
-OUTENG = ["ssss", "ssss", "ssss", "vvvv", "ssss"]
 BANKS = 8
-RANGES = CHUNKS
+CHUNKS = [(0, Q // 2), (Q // 2, Q), (Q, 2 * Q), (2 * Q, 3 * Q), (3 * Q, T)]
 
-W01_EARLY = 96
-W01_LATE = 48
-W10_GPSIMD = 112
 X_VECTOR = 592
+W_VECTOR = 88
+W_FIRST = 72
+W_THIRD = 112
 W_LAST = 96
-W_GPSIMD = 72
-EARLY_GPSIMD = 112
 
 
 def tile_moe_nxt_lin_relu_kernel(tc, xT, w, b, wp, gate, offs, out):
@@ -98,10 +89,10 @@ def tile_moe_nxt_lin_relu_kernel(tc, xT, w, b, wp, gate, offs, out):
         ybank = {}
         y = {(e, u): sbuf([P, 2, C], F32, f"y{e}{u}") for e in range(E) for u in range(2)}
         c = {(e, u): sbuf([P, C, 2], BF16, f"c{e}{u}") for e in range(E) for u in range(2)}
-        staged = {q: sbuf([P, 2, CHUNKS[q][1] - CHUNKS[q][0]], F32, f"staged{q}") for q in range(DIRECT, len(CHUNKS))}
+        staged = {q: sbuf([P, 2, t1 - t0], F32, f"staged{q}") for q, (t0, t1) in enumerate(CHUNKS) if q > 0}
         woven = [sbuf([P, t1 - t0, 2], F32, f"woven{t0}") for t0, t1 in CHUNKS]
-        ccodes = {t0: sbuf([P, t1 - t0], U32, f"ccodes{t0}") for t0, t1 in RANGES}
-        cbytes = {t0: sbuf([P, t1 - t0], U8, f"cbytes{t0}") for t0, t1 in RANGES}
+        ccodes = [sbuf([P, t1 - t0], U32, f"ccodes{t0}") for t0, t1 in CHUNKS]
+        cbytes = [sbuf([P, t1 - t0], U8, f"cbytes{t0}") for t0, t1 in CHUNKS]
         wpgrouped = {}
         wpcodes = {}
         wpbytes = sbuf([P, M], U8, "wpbytes")
@@ -216,31 +207,27 @@ def tile_moe_nxt_lin_relu_kernel(tc, xT, w, b, wp, gate, offs, out):
         def stage(q, u):
             move("scalar", staged[q][:, u, :], window[u][:, CHUNKS[q][0] : CHUNKS[q][1]])
 
-        def weave(q):
-            move("vector", woven[q], staged[q].rearrange("p u t -> p t u"))
+        def weave(engine, q):
+            move(engine, woven[q], staged[q].rearrange("p u t -> p t u"))
 
         def quantize_c(q):
-            t0 = max(first for first, end in RANGES if first <= CHUNKS[q][0])
-            lo = CHUNKS[q][0] - t0
-            hi = CHUNKS[q][1] - t0
-            grouped = woven[q].rearrange("p t u -> p (t u)").bitcast(BF16)
-            quantize(ccodes[t0][:, lo:hi], cbytes[t0][:, lo:hi], grouped)
+            quantize(ccodes[q], cbytes[q], woven[q].rearrange("p t u -> p (t u)").bitcast(BF16))
 
-        def project(t0, t1, g0, g1, engine, bank):
-            sums = psum.tile([P, g1 - g0, t1 - t0], F32, name=f"obank{t0}{g0}", tag=f"bank{bank}")
-            for g in range(g0, g1):
-                nc.tensor.matmul_mx(
-                    out=sums[:, g - g0, :],
-                    lhsT=wpcodes[g][:, 0:P].bitcast(FP8X4),
-                    lhsT_scale=wpbytes[:, g * P : (g + 1) * P],
-                    rhs=ccodes[t0].bitcast(FP8X4),
-                    rhs_scale=cbytes[t0],
-                    start=True,
-                    stop=True,
-                )
-            result = sbuf([P, g1 - g0, t1 - t0], F32, f"result{t0}{g0}")
-            move(engine, result, sums[:])
-            nc.sync.dma_start(out[g0 * P : g1 * P, t0:t1].rearrange("(g p) t -> p g t", p=P), result)
+        def next_bank(shape):
+            n = len(obanks)
+            obanks.append(psum.tile(shape, F32, name=f"obank{n}", tag=f"bank{n % BANKS}"))
+            return obanks[n]
+
+        def project(sums, q, g):
+            nc.tensor.matmul_mx(
+                out=sums,
+                lhsT=wpcodes[g][:, 0:P].bitcast(FP8X4),
+                lhsT_scale=wpbytes[:, g * P : (g + 1) * P],
+                rhs=ccodes[q].bitcast(FP8X4),
+                rhs_scale=cbytes[q],
+                start=True,
+                stop=True,
+            )
 
         quantize_x(1)
         gather_words(1, 0, E)
@@ -252,15 +239,15 @@ def tile_moe_nxt_lin_relu_kernel(tc, xT, w, b, wp, gate, offs, out):
 
         halved = [(0, C // 2, 2), (C // 2, C, 4)]
         late = [(0, C, 0)]
-        group_w("gpsimd", 0, 0, 0, 0, W_GPSIMD, "xgrouped0")
+        group_w("gpsimd", 0, 0, 0, 0, W_FIRST, "xgrouped0")
         group_w("scalar", 0, 0, 1, 0, P)
-        group_w("scalar", 0, 0, 0, W_GPSIMD, P)
+        group_w("scalar", 0, 0, 0, W_FIRST, P)
         multiply(0, 0, 1, halved)
         multiply(0, 0, 0, late)
-        group_w("vector", 0, 1, 1, 0, W01_EARLY)
-        group_w("scalar", 0, 1, 1, W01_EARLY, P)
-        group_w("vector", 0, 1, 0, 0, W01_LATE)
-        group_w("scalar", 0, 1, 0, W01_LATE, P)
+        group_w("vector", 0, 1, 1, 0, W_VECTOR)
+        group_w("scalar", 0, 1, 1, W_VECTOR, P)
+        group_w("vector", 0, 1, 0, 0, P // 2)
+        group_w("scalar", 0, 1, 0, P // 2, P)
         multiply(0, 1, 1, halved)
         multiply(0, 1, 0, late)
         gather_bytes(1, "wraw01")
@@ -270,9 +257,9 @@ def tile_moe_nxt_lin_relu_kernel(tc, xT, w, b, wp, gate, offs, out):
         scatter(0, 1)
         gate_gpsimd(0, 0, 0, C)
 
-        group_w("gpsimd", 1, 0, 0, 0, W10_GPSIMD, "wgrouped010")
+        group_w("gpsimd", 1, 0, 0, 0, W_THIRD, "wgrouped010")
         group_w("scalar", 1, 0, 1, 0, P)
-        group_w("scalar", 1, 0, 0, W10_GPSIMD, P)
+        group_w("scalar", 1, 0, 0, W_THIRD, P)
         multiply(1, 0, 1, halved)
         multiply(1, 0, 0, late)
         group_w("scalar", 1, 1, 1, 0, P)
@@ -287,70 +274,51 @@ def tile_moe_nxt_lin_relu_kernel(tc, xT, w, b, wp, gate, offs, out):
             wpgrouped[g] = after_relus[:, (g - 1) * P :, :]
         for g in range(G - 1):
             group_wp("scalar", g)
-        gate_gpsimd(1, 1, 0, EARLY_GPSIMD)
-        gate_vector(1, 1, EARLY_GPSIMD, C)
+        gate_gpsimd(1, 1, 0, C // 2)
+        gate_vector(1, 1, C // 2, C)
         gate_gpsimd(1, 0, 0, C)
         group_wp("gpsimd", G - 1)
         scatter(1, 1)
 
-        for q in range(DIRECT):
-            t0, t1 = CHUNKS[q]
-            move("scalar", woven[q][:, :, 1], window[1][:, t0:t1])
-        for q in range(DIRECT, len(CHUNKS)):
+        first_end = CHUNKS[0][1]
+        last = len(CHUNKS) - 1
+        move("scalar", woven[0][:, :, 1], window[1][:, 0:first_end])
+        for q in staged:
             stage(q, 1)
         scatter(1, 0)
         for g, tag in ((0, "y10"), (2, None)):
             wpcodes[g] = sbuf([P, 2 * P], U32, f"wpcodes{g}", tag)
             wpcodes[g + 1] = wpcodes[g][:, P:]
-        for q in STAGE0:
+        for q in (1, 2, last, last - 1):
             stage(q, 0)
-        for step in TAIL.split():
-            q = int(step[1])
-            if step[0] == "d":
-                t0, t1 = CHUNKS[q]
-                move("vector", woven[q][:, :, 0], window[0][:, t0:t1])
-            elif step[0] == "w":
-                weave(q)
-            elif step[0] == "s":
-                move("scalar", woven[q], staged[q].rearrange("p u t -> p t u"))
-            elif step[0] == "q":
-                quantize_c(q)
-            elif step[0] == "h":
-                warm = psum.tile([P, 2 * P], F32, name="warm", tag="bank7")
-                for i in range(q):
-                    nc.tensor.matmul_mx(
-                        out=warm[:],
-                        lhsT=wpcodes[0][:, 0:P].bitcast(FP8X4),
-                        lhsT_scale=wpbytes[:, 0:P],
-                        rhs=wpcodes[0].bitcast(FP8X4),
-                        rhs_scale=wpbytes[:, 0 : 2 * P],
-                        start=(i == 0),
-                        stop=(i == q - 1),
-                    )
-            else:
-                quantize_wp(q, int(step[2]))
+        quantize_wp(0, 1)
+        quantize_wp(1, 2)
+        move("vector", woven[0][:, :, 0], window[0][:, 0:first_end])
+        quantize_wp(2, G)
+        quantize_c(0)
+        weave("vector", 1)
+        weave("vector", 2)
+        quantize_c(1)
+        weave("scalar", last)
+        weave("vector", last - 1)
+        for q in (2, last, last - 1):
+            quantize_c(q)
 
-        bank = 0
-        for n, (t0, t1) in enumerate(RANGES[: len(MERGE)]):
-            for g in range(0, G, MERGE[n]):
-                project(t0, t1, g, g + MERGE[n], {"v": "vector", "s": "scalar"}[OUTENG[n][g]], bank % BANKS)
-                bank = bank + 1
-        if len(MERGE) < len(RANGES):
-            first = RANGES[len(MERGE)][0]
-            results = [sbuf([P, T - first], F32, f"result{first}{g}") for g in range(G)]
-            for g, n in LAST:
-                t0, t1 = RANGES[n]
-                sums = psum.tile([P, t1 - t0], F32, name=f"obank{t0}{g}", tag=f"bank{bank % BANKS}")
-                bank = bank + 1
-                nc.tensor.matmul_mx(
-                    out=sums[:],
-                    lhsT=wpcodes[g][:, 0:P].bitcast(FP8X4),
-                    lhsT_scale=wpbytes[:, g * P : (g + 1) * P],
-                    rhs=ccodes[t0].bitcast(FP8X4),
-                    rhs_scale=cbytes[t0],
-                    start=True,
-                    stop=True,
-                )
-                move({"v": "vector", "s": "scalar"}[OUTENG[n][g]], results[g][:, t0 - first : t1 - first], sums[:])
-                if t1 == T:
-                    nc.sync.dma_start(out[g * P : (g + 1) * P, first:T], results[g])
+        obanks = []
+        for q, groups in ((0, 1), (1, 2), (2, 1)):
+            t0, t1 = CHUNKS[q]
+            for g0 in range(0, G, groups):
+                sums = next_bank([P, groups, t1 - t0])
+                for i in range(groups):
+                    project(sums[:, i, :], q, g0 + i)
+                result = sbuf([P, groups, t1 - t0], F32, f"result{t0}{g0}")
+                move("scalar", result, sums[:])
+                nc.sync.dma_start(out[g0 * P : (g0 + groups) * P, t0:t1].rearrange("(g p) t -> p g t", p=P), result)
+        t0 = CHUNKS[last - 1][0]
+        results = [sbuf([P, T - t0], F32, f"result{t0}{g}") for g in range(G)]
+        for g in range(G):
+            for q, engine in ((last - 1, "vector"), (last, "scalar")):
+                sums = next_bank([P, Q])
+                project(sums[:], q, g)
+                move(engine, results[g][:, CHUNKS[q][0] - t0 : CHUNKS[q][1] - t0], sums[:])
+            nc.sync.dma_start(out[g * P : (g + 1) * P, t0:T], results[g])

@@ -32,7 +32,8 @@ X_VECTOR = 592
 W_VECTOR = 88
 W_FIRST = 72
 W_THIRD = 112
-W_LAST = 96
+W_LAST = 72
+W_AHEAD = 24
 
 
 def tile_moe_nxt_lin_relu_kernel(tc, xT, w, b, wp, gate, offs, out):
@@ -262,9 +263,10 @@ def tile_moe_nxt_lin_relu_kernel(tc, xT, w, b, wp, gate, offs, out):
         group_w("scalar", 1, 0, 0, W_THIRD, P)
         multiply(1, 0, 1, halved)
         multiply(1, 0, 0, late)
+        group_w("scalar", 1, 1, 0, W_LAST, W_LAST + W_AHEAD)
         group_w("scalar", 1, 1, 1, 0, P)
         group_w("vector", 1, 1, 0, 0, W_LAST)
-        group_w("scalar", 1, 1, 0, W_LAST, P)
+        group_w("scalar", 1, 1, 0, W_LAST + W_AHEAD, P)
         multiply(1, 1, 1, halved)
         multiply(1, 1, 0, late)
         scatter(0, 0)

@@ -5,18 +5,19 @@ from concourse.masks import make_identity
 
 K, T, E, C, N, M = 1024, 1024, 2, 256, 512, 512
 S = E * C
-FLOPS = 2 * K * N * S + 2 * N * M * T
+FLOPS = 2 * K * N * S + 2 * N * M * S
 
 F32 = mybir.dt.float32
 BF16 = mybir.dt.bfloat16
 U32 = mybir.dt.uint32
-I32 = mybir.dt.int32
 U16 = mybir.dt.uint16
 U8 = mybir.dt.uint8
 FP8X4 = mybir.dt.float8_e4m3fn_x4
 RELU = mybir.ActivationFunctionType.Relu
+COPY = mybir.ActivationFunctionType.Copy
 MULT = mybir.AluOpType.mult
 ADD = mybir.AluOpType.add
+MAX = mybir.AluOpType.max
 
 P = 128
 J = 4
@@ -24,16 +25,9 @@ KP = P * J
 PASSES = K // KP
 G = M // P
 R = S // P
-Q = T // 4
-BANKS = 8
-CHUNKS = [(0, Q // 2), (Q // 2, Q), (Q, 2 * Q), (2 * Q, 3 * Q), (3 * Q, T)]
+H = C // 2
 
-X_VECTOR = 592
-W_VECTOR = 88
-W_FIRST = 72
-W_THIRD = 112
-W_LAST = 72
-W_AHEAD = 24
+W_VECTOR = 16
 
 
 def tile_moe_nxt_lin_relu_kernel(tc, xT, w, b, wp, gate, offs, out):
@@ -48,279 +42,259 @@ def tile_moe_nxt_lin_relu_kernel(tc, xT, w, b, wp, gate, offs, out):
         offsets = keep.tile([P, S // 16], U16, name="offsets")
         bias = sbuf([P, J * E], F32, "bias")
         gate_row = sbuf([P, R], F32, "gate_row")
-        nc.scalar.dma_start(gate_row, gate[0, :].rearrange("(p r) -> p r", r=R))
-        xraw = {}
-        for a in (1, 0):
-            xraw[a] = sbuf([P, J, T], F32, f"xraw{a}")
-            nc.sync.dma_start(xraw[a], xT[a * KP : (a + 1) * KP, :].rearrange("(p j) t -> p j t", j=J))
-            if a == 1:
-                nc.sync.dma_start(offsets[:], offs)
-                nc.scalar.dma_start(bias, b.rearrange("(p t) e -> p (t e)", t=J))
+        xrow = {}
         wraw = {}
-        for e in range(E):
-            for a in range(PASSES):
-                wraw[e, a] = sbuf([P, J, N], F32, f"wraw{e}{a}")
-                nc.sync.dma_start(wraw[e, a], w[e, a * KP : (a + 1) * KP, :].rearrange("(p j) n -> p j n", j=J))
-        wpraw = []
-        for h in range(2):
-            wpraw.append(sbuf([P, J, M // 2], F32, f"wpraw{h}"))
+        wpraw = {}
+
+        def load_x(a, j):
+            xrow[a, j] = keep.tile([P, T], F32, name=f"xrow{a}{j}", align_bytes=64)
+            nc.sync.dma_start(xrow[a, j][:], xT[a * KP : (a + 1) * KP, :].rearrange("(p j) t -> p j t", j=J)[:, j, :])
+
+        def load_w(e, a):
+            wraw[e, a] = sbuf([P, J, N], F32, f"wraw{e}{a}")
+            nc.sync.dma_start(wraw[e, a], w[e, a * KP : (a + 1) * KP, :].rearrange("(p j) n -> p j n", j=J))
+
+        def load_wp(h):
+            wpraw[h] = sbuf([P, J, M // 2], F32, f"wpraw{h}")
             nc.sync.dma_start(wpraw[h], wp[:, h * M // 2 : (h + 1) * M // 2].rearrange("(p j) f -> p j f", j=J))
+
+        nc.scalar.dma_start(gate_row, gate[0, :].rearrange("(p r) -> p r", r=R))
+        nc.scalar.dma_start(bias, b.rearrange("(p t) e -> p (t e)", t=J))
+        load_x(0, 0)
+        nc.sync.dma_start(offsets[:], offs)
+        for j in range(1, J):
+            load_x(0, j)
+        load_w(0, 0)
+        load_w(0, 1)
+        for j in range(J):
+            load_x(1, j)
+        load_wp(0)
+        load_w(1, 0)
+        load_w(1, 1)
+        load_wp(1)
 
         identity = sbuf([P, P], F32, "identity")
         make_identity(nc, identity)
-        gbank = psum.tile([P, R, P], F32, name="gbank", tag="bank6")
+        gbank = psum.tile([P, R, P], F32, name="gbank", tag="bank4")
         for r in range(R):
             nc.tensor.transpose(gbank[:, r, :], gate_row[:, r : r + 1].to_broadcast([P, P]), identity)
 
-        xbytes = keep.tile([P, T], U8, name="xbytes", align_bytes=64)
-        nc.vector.memset(xbytes[:].bitcast(I32), 0)
-        window = [keep.tile([P, T + (1 - u) * P * J], F32, name=f"window{u}", align_bytes=64) for u in range(2)]
+        spare = [0, 0, 0, C * J]
+        window = [keep.tile([P, T + spare[g]], F32, name=f"window{g}", align_bytes=64) for g in range(G)]
         zeros = sbuf([P, 8], F32, "zeros")
         nc.vector.memset(zeros, 0.0)
-        nc.scalar.activation(window[1][:, 0:8], zeros, RELU)
-        nc.gpsimd.memset(window[1][:, 8:T], 0.0)
-        nc.gpsimd.memset(window[0][:, 0:T], 0.0)
+        nc.scalar.activation(window[0][:, 0:8], zeros, RELU)
+        nc.gpsimd.memset(window[0][:, 8:T], 0.0)
+        for g in range(1, G):
+            nc.gpsimd.memset(window[g][:, 0:T], 0.0)
 
-        xcodes = [keep.tile([P, T], U32, name=f"xcodes{a}", align_bytes=64) for a in range(PASSES)]
-        gcodes = {}
-        gbytes = {}
-        wgrouped = {(1, 1, 1): window[0][:, T:].bitcast(BF16).rearrange("p (t m j) -> p t m j", t=2, j=J)}
+        xgrouped = {(e, a): sbuf([P, C, J], BF16, f"xgrouped{e}{a}") for e in range(E) for a in range(PASSES)}
+        xcodes = {}
+        xbytes = {}
+        wgrouped = {}
         wcodes = {}
         wbytes = {}
         ybank = {}
-        y = {(e, u): sbuf([P, 2, C], F32, f"y{e}{u}") for e in range(E) for u in range(2)}
-        c = {(e, u): sbuf([P, C, 2], BF16, f"c{e}{u}") for e in range(E) for u in range(2)}
-        staged = {q: sbuf([P, 2, t1 - t0], F32, f"staged{q}") for q, (t0, t1) in enumerate(CHUNKS) if q > 0}
-        woven = [sbuf([P, t1 - t0, 2], F32, f"woven{t0}") for t0, t1 in CHUNKS]
-        ccodes = [sbuf([P, t1 - t0], U32, f"ccodes{t0}") for t0, t1 in CHUNKS]
-        cbytes = [sbuf([P, t1 - t0], U8, f"cbytes{t0}") for t0, t1 in CHUNKS]
+        y = {(1, 0): window[3][:, T:].rearrange("p (t s) -> p t s", t=J)}
+        c_last = sbuf([P, C, J], BF16, "c1")
+        c = {(1, 0): c_last[:, 0:H, :], (1, H): c_last[:, H:C, :]}
+        ccodes = [sbuf([P, C], U32, f"ccodes{e}") for e in range(E)]
+        cbytes = [sbuf([P, C], U8, f"cbytes{e}") for e in range(E)]
         wpgrouped = {}
         wpcodes = {}
-        wpbytes = sbuf([P, M], U8, "wpbytes")
+        wpbytes = {}
+        obanks = []
+        result = {}
+
+        def slots(e, s0, s1):
+            return offsets[:, (e * C + s0) // 16 : (e * C + s1) // 16]
 
         def move(engine, dst, src):
             if engine == "vector":
                 nc.vector.tensor_copy(out=dst, in_=src)
-            elif engine == "scalar":
-                nc.scalar.copy(out=dst, in_=src)
             else:
-                nc.gpsimd.tensor_scalar(dst, src, 1.0, 0.0, MULT, ADD)
+                nc.scalar.copy(out=dst, in_=src)
+
+        def move_indirect(engine, dst, src):
+            if engine == "vector":
+                nc.vector.tensor_copy(dst, src)
+            else:
+                nc.scalar.activation(dst, src, COPY)
 
         def quantize(codes, scales, grouped):
             nc.vector.quantize_mx(out=codes.bitcast(FP8X4), scales=scales, in_=grouped)
 
-        def quantize_x(a):
-            grouped = sbuf([P, T, J], BF16, f"xgrouped{a}")
-            for engine, lo, hi in (
-                ("vector", 0, Q),
-                ("vector", Q, X_VECTOR),
-                ("scalar", X_VECTOR, T - Q),
-                ("scalar", T - Q, T),
-            ):
-                move(
-                    engine,
-                    grouped[:, lo:hi, :].rearrange("p (x i) j -> p x j i", i=4),
-                    xraw[a][:, :, lo:hi].rearrange("p j (x i) -> p x j i", i=4),
-                )
-            for t0 in range(0, T, Q):
-                part = grouped[:, t0 : t0 + Q, :].rearrange("p t j -> p (t j)")
-                quantize(xcodes[a][:, t0 : t0 + Q], xbytes[4 * a :, t0 : t0 + Q], part)
+        def gather(engine, a, j, e, s0, s1):
+            move_indirect(engine, xgrouped[e, a][:, s0:s1, j], xrow[a, j][:].indirect(slots(e, s0, s1)))
 
-        def gather_words(a, e0, e1, tag=None):
-            words = sbuf([P, (e1 - e0) * C], U32, f"gcodes{a}{e0}", tag)
-            nc.vector.tensor_copy(words, xcodes[a][:].indirect(offsets[:, e0 * C // 16 : e1 * C // 16]))
-            for e in range(e0, e1):
-                gcodes[a, e] = words[:, (e - e0) * C : (e - e0 + 1) * C]
-
-        def gather_bytes(e, tag=None):
-            gbytes[e] = sbuf([P, C], U8, f"gbytes{e}", tag)
-            nc.vector.tensor_copy(gbytes[e], xbytes[:].indirect(offsets[:, e * C // 16 : (e + 1) * C // 16]))
+        def quantize_x(e, a, tag=None):
+            xcodes[e, a] = sbuf([P, C], U32, f"xcodes{e}{a}", tag)
+            xbytes[e, a] = sbuf([P, C], U8, f"xbytes{e}{a}")
+            quantize(xcodes[e, a], xbytes[e, a], xgrouped[e, a].rearrange("p s j -> p (s j)"))
 
         def group_w(engine, e, a, u, m0, m1, tag=None):
             if (e, a, u) not in wgrouped:
                 wgrouped[e, a, u] = sbuf([P, 2, P, J], BF16, f"wgrouped{e}{a}{u}", tag)
-            order = "p m t j" if engine == "gpsimd" else "p m j t"
             columns = wraw[e, a].rearrange("p j (m u t) -> p j m u t", u=2, t=2)[:, :, m0:m1, u, :]
             move(
                 engine,
-                wgrouped[e, a, u][:, :, m0:m1, :].rearrange("p t m j -> " + order),
-                columns.rearrange("p j m t -> " + order),
+                wgrouped[e, a, u][:, :, m0:m1, :].rearrange("p t m j -> p m j t"),
+                columns.rearrange("p j m t -> p m j t"),
             )
 
-        def multiply(e, a, u, spans):
+        def quantize_w(e, a, u):
             wcodes[e, a, u] = sbuf([P, 2 * P], U32, f"wcodes{e}{a}{u}")
             wbytes[e, a, u] = sbuf([P, 2 * P], U8, f"wbytes{e}{a}{u}")
             quantize(wcodes[e, a, u], wbytes[e, a, u], wgrouped[e, a, u].rearrange("p t m j -> p (t m j)"))
-            for s0, s1, bank in spans:
-                for i in range(2):
-                    t = 2 * u + i
-                    if a == 0:
-                        ybank[e, t, s0] = psum.tile([P, s1 - s0], F32, name=f"ybank{e}{t}{s0}", tag=f"bank{bank + i}")
-                    nc.tensor.matmul_mx(
-                        out=ybank[e, t, s0][:],
-                        lhsT=wcodes[e, a, u][:, i * P : (i + 1) * P].bitcast(FP8X4),
-                        lhsT_scale=wbytes[e, a, u][:, i * P : (i + 1) * P],
-                        rhs=gcodes[a, e][:, s0:s1].bitcast(FP8X4),
-                        rhs_scale=gbytes[e][4 * a :, s0:s1],
-                        start=(a == 0),
-                        stop=(a == PASSES - 1),
-                    )
-                    if a == PASSES - 1:
-                        column = bias[:, t * E + e : t * E + e + 1]
-                        nc.scalar.activation(y[e, u][:, i, s0:s1], ybank[e, t, s0][:], RELU, bias=column)
 
-        def gate_vector(e, u, s0, s1):
+        def prepare_w(e, a):
+            group_w("vector", e, a, 0, 0, P)
+            group_w("scalar", e, a, 1, W_VECTOR, P)
+            group_w("vector", e, a, 1, 0, W_VECTOR)
+            quantize_w(e, a, 0)
+            quantize_w(e, a, 1)
+
+        def multiply(e, a, s0, s1, banks):
+            for t in range(J):
+                u, i = divmod(t, 2)
+                sharers = [x for x in range(J) if banks[x] == banks[t]]
+                if a == 0 and t == sharers[0]:
+                    bank = psum.tile([P, len(sharers), s1 - s0], F32, name=f"ybank{e}{t}{s0}", tag=f"bank{banks[t]}")
+                    for n, x in enumerate(sharers):
+                        ybank[e, x, s0] = bank[:, n, :]
+                nc.tensor.matmul_mx(
+                    out=ybank[e, t, s0],
+                    lhsT=wcodes[e, a, u][:, i * P : (i + 1) * P].bitcast(FP8X4),
+                    lhsT_scale=wbytes[e, a, u][:, i * P : (i + 1) * P],
+                    rhs=xcodes[e, a][:, s0:s1].bitcast(FP8X4),
+                    rhs_scale=xbytes[e, a][:, s0:s1],
+                    start=(a == 0 and t == sharers[0]),
+                    stop=(a == PASSES - 1 and t == sharers[-1]),
+                )
+
+        def relu(engine, e, t, s0, s1):
+            if (e, s0) not in y:
+                y[e, s0] = sbuf([P, J, s1 - s0], F32, f"y{e}{s0}")
+            column = bias[:, t * E + e : t * E + e + 1]
+            if engine == "vector":
+                nc.vector.tensor_scalar(y[e, s0][:, t, :], ybank[e, t, s0], column, 0.0, ADD, MAX)
+            else:
+                nc.scalar.activation(y[e, s0][:, t, :], ybank[e, t, s0], RELU, bias=column)
+
+        def gate_product(e, s0, s1, y0):
+            if (e, s0) not in c:
+                c[e, s0] = sbuf([P, s1 - s0, J], BF16, f"c{e}{s0}")
             weights = gbank[:, :, (e * C + s0) // R : (e * C + s1) // R].rearrange("p r m -> p m r")
             nc.vector.tensor_tensor(
-                out=c[e, u][:, s0:s1, :].rearrange("p (m r) t -> p m r t", r=R),
-                in0=y[e, u][:, :, s0:s1].rearrange("p t (m r) -> p m r t", r=R),
-                in1=weights.unsqueeze(3).to_broadcast([P, (s1 - s0) // R, R, 2]),
+                out=c[e, s0].rearrange("p (m r) t -> p m t r", r=R),
+                in0=y[e, y0][:, :, s0 - y0 : s1 - y0].rearrange("p t (m r) -> p m t r", r=R),
+                in1=weights.unsqueeze(2).to_broadcast([P, (s1 - s0) // R, J, R]),
                 op=MULT,
             )
 
-        def gate_gpsimd(e, u, s0, s1):
-            nc.gpsimd.tensor_tensor(
-                out=c[e, u][:, s0:s1, :].rearrange("p s t -> p t s"),
-                in0=y[e, u][:, :, s0:s1],
-                in1=gates[:, e * C + s0 : e * C + s1].unsqueeze(1).to_broadcast([P, 2, s1 - s0]),
-                op=MULT,
-            )
+        def quantize_c(e, s0, s1):
+            quantize(ccodes[e][:, s0:s1], cbytes[e][:, s0:s1], c[e, s0].rearrange("p s t -> p (s t)"))
 
-        def scatter(e, u):
+        def group_wp(h):
+            wpgrouped[h] = sbuf([P, 2 * P, J], BF16, f"wpgrouped{h}")
             nc.vector.tensor_copy(
-                window[u][:].indirect(offsets[:, e * C // 16 : (e + 1) * C // 16]),
-                c[e, u].rearrange("p s t -> p (s t)").bitcast(F32),
+                out=wpgrouped[h].rearrange("p (x i) j -> p x j i", i=4),
+                in_=wpraw[h].rearrange("p j (x i) -> p x j i", i=4),
             )
 
-        def group_wp(engine, g):
-            order = "p x i j" if engine == "gpsimd" else "p x j i"
-            move(
-                engine,
-                wpgrouped[g][:, 0:P, :].rearrange("p (x i) j -> " + order, i=4),
-                wpraw[g // 2][:, :, g % 2 * P : (g % 2 + 1) * P].rearrange("p j (x i) -> " + order, i=4),
-            )
+        def quantize_wp(h):
+            wpcodes[h] = sbuf([P, 2 * P], U32, f"wpcodes{h}")
+            wpbytes[h] = sbuf([P, 2 * P], U8, f"wpbytes{h}")
+            quantize(wpcodes[h], wpbytes[h], wpgrouped[h].rearrange("p f j -> p (f j)"))
 
-        def quantize_wp(g0, g1):
-            width = (g1 - g0) * P
-            grouped = wpgrouped[g0][:, 0:width, :].rearrange("p f j -> p (f j)")
-            quantize(wpcodes[g0][:, 0:width], wpbytes[:, g0 * P : g1 * P], grouped)
-
-        def stage(q, u):
-            move("scalar", staged[q][:, u, :], window[u][:, CHUNKS[q][0] : CHUNKS[q][1]])
-
-        def weave(engine, q):
-            move(engine, woven[q], staged[q].rearrange("p u t -> p t u"))
-
-        def quantize_c(q):
-            quantize(ccodes[q], cbytes[q], woven[q].rearrange("p t u -> p (t u)").bitcast(BF16))
-
-        def next_bank(shape):
+        def project(engine, e, g, bank, tag=None):
             n = len(obanks)
-            obanks.append(psum.tile(shape, F32, name=f"obank{n}", tag=f"bank{n % BANKS}"))
-            return obanks[n]
-
-        def project(sums, q, g):
+            obanks.append(psum.tile([P, C], F32, name=f"obank{n}", tag=f"bank{bank}"))
+            h, i = divmod(g, 2)
             nc.tensor.matmul_mx(
-                out=sums,
-                lhsT=wpcodes[g][:, 0:P].bitcast(FP8X4),
-                lhsT_scale=wpbytes[:, g * P : (g + 1) * P],
-                rhs=ccodes[q].bitcast(FP8X4),
-                rhs_scale=cbytes[q],
+                out=obanks[n][:],
+                lhsT=wpcodes[h][:, i * P : (i + 1) * P].bitcast(FP8X4),
+                lhsT_scale=wpbytes[h][:, i * P : (i + 1) * P],
+                rhs=ccodes[e].bitcast(FP8X4),
+                rhs_scale=cbytes[e],
                 start=True,
                 stop=True,
             )
+            result[e, g] = sbuf([P, C], F32, f"result{e}{g}", tag)
+            move(engine, result[e, g], obanks[n][:])
 
-        quantize_x(1)
-        gather_words(1, 0, E)
-        gates = sbuf([P, S], F32, "gates", "xraw1")
-        nc.scalar.copy(out=gates.rearrange("p (m r) -> p m r", r=R), in_=gbank[:].rearrange("p r m -> p m r"))
-        quantize_x(0)
-        gather_words(0, 0, 1)
-        gather_bytes(0)
+        def scatter(engine, e, g):
+            move_indirect(engine, window[g][:].indirect(slots(e, 0, C)), result[e, g])
 
-        halved = [(0, C // 2, 2), (C // 2, C, 4)]
-        late = [(0, C, 0)]
-        group_w("gpsimd", 0, 0, 0, 0, W_FIRST, "xgrouped0")
-        group_w("scalar", 0, 0, 1, 0, P)
-        group_w("scalar", 0, 0, 0, W_FIRST, P)
-        multiply(0, 0, 1, halved)
-        multiply(0, 0, 0, late)
-        group_w("vector", 0, 1, 1, 0, W_VECTOR)
-        group_w("scalar", 0, 1, 1, W_VECTOR, P)
-        group_w("vector", 0, 1, 0, 0, P // 2)
-        group_w("scalar", 0, 1, 0, P // 2, P)
-        multiply(0, 1, 1, halved)
-        multiply(0, 1, 0, late)
-        gather_bytes(1, "wraw01")
-        gather_words(0, 1, E, "wgrouped011")
-        for s0, s1, bank in halved:
-            gate_vector(0, 1, s0, s1)
-        scatter(0, 1)
-        gate_gpsimd(0, 0, 0, C)
+        def store(g):
+            queue = nc.scalar if g == 2 else nc.sync
+            queue.dma_start(out[g * P : (g + 1) * P, :], window[g][:, 0:T])
 
-        group_w("gpsimd", 1, 0, 0, 0, W_THIRD, "wgrouped010")
+        for j in range(J):
+            gather("vector", 0, j, 0, 0, C)
+            gather("scalar", 0, j, 1, 0, C)
+        quantize_x(0, 0)
+        quantize_x(1, 0)
+        first = [(0, H, [0, 1, 2, 3]), (H, C, [5, 5, 6, 6])]
+        prepare_w(0, 0)
+        for s0, s1, banks in first:
+            multiply(0, 0, s0, s1, banks)
+        prepare_w(0, 1)
+        for j in range(2):
+            gather("vector", 1, j, 0, 0, C)
+            gather("scalar", 1, j, 1, 0, C)
+        for j in range(2, J):
+            for e in range(E):
+                gather("vector", 1, j, e, 0, H)
+                gather("scalar", 1, j, e, H, C)
+        quantize_x(0, 1)
+        for s0, s1, banks in first:
+            multiply(0, 1, s0, s1, banks)
+        group_wp(0)
+        for s0 in (0, H):
+            for t in range(J):
+                relu("scalar", 0, t, s0, s0 + H)
+        quantize_x(1, 1)
+        quantize_wp(0)
+        for s0 in (0, H):
+            gate_product(0, s0, s0 + H, s0)
         group_w("scalar", 1, 0, 1, 0, P)
-        group_w("scalar", 1, 0, 0, W_THIRD, P)
-        multiply(1, 0, 1, halved)
-        multiply(1, 0, 0, late)
-        group_w("scalar", 1, 1, 0, W_LAST, W_LAST + W_AHEAD)
-        group_w("scalar", 1, 1, 1, 0, P)
-        group_w("vector", 1, 1, 0, 0, W_LAST)
-        group_w("scalar", 1, 1, 0, W_LAST + W_AHEAD, P)
-        multiply(1, 1, 1, halved)
-        multiply(1, 1, 0, late)
-        scatter(0, 0)
-        wpgrouped[0] = sbuf([P, P, J], BF16, "wpgrouped0")
-        after_relus = sbuf([P, (G - 1) * P, J], BF16, "wpgrouped1", "bias")
-        for g in range(1, G):
-            wpgrouped[g] = after_relus[:, (g - 1) * P :, :]
-        for g in range(G - 1):
-            group_wp("scalar", g)
-        gate_gpsimd(1, 1, 0, C // 2)
-        gate_vector(1, 1, C // 2, C)
-        gate_gpsimd(1, 0, 0, C)
-        group_wp("gpsimd", G - 1)
-        scatter(1, 1)
-
-        first_end = CHUNKS[0][1]
-        last = len(CHUNKS) - 1
-        move("scalar", woven[0][:, :, 1], window[1][:, 0:first_end])
-        for q in staged:
-            stage(q, 1)
-        scatter(1, 0)
-        for g, tag in ((0, "y10"), (2, None)):
-            wpcodes[g] = sbuf([P, 2 * P], U32, f"wpcodes{g}", tag)
-            wpcodes[g + 1] = wpcodes[g][:, P:]
-        for q in (1, 2, last, last - 1):
-            stage(q, 0)
-        quantize_wp(0, 1)
-        quantize_wp(1, 2)
-        move("vector", woven[0][:, :, 0], window[0][:, 0:first_end])
-        quantize_wp(2, G)
-        quantize_c(0)
-        weave("vector", 1)
-        weave("vector", 2)
-        quantize_c(1)
-        weave("scalar", last)
-        weave("vector", last - 1)
-        for q in (2, last, last - 1):
-            quantize_c(q)
-
-        obanks = []
-        for q, groups in ((0, 1), (1, 2), (2, 1)):
-            t0, t1 = CHUNKS[q]
-            for g0 in range(0, G, groups):
-                sums = next_bank([P, groups, t1 - t0])
-                for i in range(groups):
-                    project(sums[:, i, :], q, g0 + i)
-                result = sbuf([P, groups, t1 - t0], F32, f"result{t0}{g0}")
-                move("scalar", result, sums[:])
-                nc.sync.dma_start(out[g0 * P : (g0 + groups) * P, t0:t1].rearrange("(g p) t -> p g t", p=P), result)
-        t0 = CHUNKS[last - 1][0]
-        results = [sbuf([P, T - t0], F32, f"result{t0}{g}") for g in range(G)]
-        for g in range(G):
-            for q, engine in ((last - 1, "vector"), (last, "scalar")):
-                sums = next_bank([P, Q])
-                project(sums[:], q, g)
-                move(engine, results[g][:, CHUNKS[q][0] - t0 : CHUNKS[q][1] - t0], sums[:])
-            nc.sync.dma_start(out[g * P : (g + 1) * P, t0:T], results[g])
+        for s0 in (0, H):
+            quantize_c(0, s0, s0 + H)
+        group_w("vector", 1, 0, 0, 0, P, f"y0{H}")
+        project("scalar", 0, 0, 7)
+        project("vector", 0, 1, 5)
+        scatter("scalar", 0, 0)
+        scatter("scalar", 0, 1)
+        quantize_w(1, 0, 1)
+        quantize_w(1, 0, 0)
+        multiply(1, 0, 0, C, [0, 1, 2, 3])
+        for u in range(2):
+            group_w("vector", 1, 1, u, 0, P)
+        for u in range(2):
+            quantize_w(1, 1, u)
+        multiply(1, 1, 0, C, [0, 1, 2, 3])
+        group_wp(1)
+        for t in range(J - 1):
+            relu("scalar", 1, t, 0, C)
+        relu("vector", 1, J - 1, 0, C)
+        quantize_wp(1)
+        project("scalar", 0, 2, 6)
+        for s0 in (0, H):
+            gate_product(1, s0, s0 + H, 0)
+        scatter("scalar", 0, 2)
+        project("vector", 0, 3, 3)
+        quantize(ccodes[1], cbytes[1], c_last.rearrange("p s t -> p (s t)"))
+        scatter("vector", 0, 3)
+        project("scalar", 1, 0, 5)
+        project("scalar", 1, 2, 0)
+        scatter("scalar", 1, 0)
+        store(0)
+        project("vector", 1, 1, 5)
+        project("vector", 1, 3, 1)
+        scatter("vector", 1, 1)
+        store(1)
+        scatter("scalar", 1, 2)
+        store(2)
+        scatter("vector", 1, 3)
+        store(3)

@@ -27,6 +27,7 @@ G = M // P
 R = S // P
 H = C // 2
 
+W_SCALAR = 104
 W_VECTOR = 16
 
 
@@ -79,8 +80,7 @@ def tile_moe_nxt_lin_relu_kernel(tc, xT, w, b, wp, gate, offs, out):
         for r in range(R):
             nc.tensor.transpose(gbank[:, r, :], gate_row[:, r : r + 1].to_broadcast([P, P]), identity)
 
-        spare = [0, 0, 0, C * J]
-        window = [keep.tile([P, T + spare[g]], F32, name=f"window{g}", align_bytes=64) for g in range(G)]
+        window = [keep.tile([P, T], F32, name=f"window{g}", align_bytes=64) for g in range(G)]
         zeros = sbuf([P, 8], F32, "zeros")
         nc.vector.memset(zeros, 0.0)
         nc.scalar.activation(window[0][:, 0:8], zeros, RELU)
@@ -95,15 +95,14 @@ def tile_moe_nxt_lin_relu_kernel(tc, xT, w, b, wp, gate, offs, out):
         wcodes = {}
         wbytes = {}
         ybank = {}
-        y = {(1, 0): window[3][:, T:].rearrange("p (t s) -> p t s", t=J)}
-        c_last = sbuf([P, C, J], BF16, "c1")
-        c = {(1, 0): c_last[:, 0:H, :], (1, H): c_last[:, H:C, :]}
+        ysums = {}
+        y = {}
+        c = {}
         ccodes = [sbuf([P, C], U32, f"ccodes{e}") for e in range(E)]
         cbytes = [sbuf([P, C], U8, f"cbytes{e}") for e in range(E)]
         wpgrouped = {}
         wpcodes = {}
         wpbytes = {}
-        obanks = []
         result = {}
 
         def slots(e, s0, s1):
@@ -162,6 +161,8 @@ def tile_moe_nxt_lin_relu_kernel(tc, xT, w, b, wp, gate, offs, out):
                     bank = psum.tile([P, len(sharers), s1 - s0], F32, name=f"ybank{e}{t}{s0}", tag=f"bank{banks[t]}")
                     for n, x in enumerate(sharers):
                         ybank[e, x, s0] = bank[:, n, :]
+                        for h0 in range(s0, s1, H):
+                            ysums[e, x, h0] = bank[:, n, h0 - s0 : h0 - s0 + H]
                 nc.tensor.matmul_mx(
                     out=ybank[e, t, s0],
                     lhsT=wcodes[e, a, u][:, i * P : (i + 1) * P].bitcast(FP8X4),
@@ -177,13 +178,12 @@ def tile_moe_nxt_lin_relu_kernel(tc, xT, w, b, wp, gate, offs, out):
                 y[e, s0] = sbuf([P, J, s1 - s0], F32, f"y{e}{s0}")
             column = bias[:, t * E + e : t * E + e + 1]
             if engine == "vector":
-                nc.vector.tensor_scalar(y[e, s0][:, t, :], ybank[e, t, s0], column, 0.0, ADD, MAX)
+                nc.vector.tensor_scalar(y[e, s0][:, t, :], ysums[e, t, s0], column, 0.0, ADD, MAX)
             else:
-                nc.scalar.activation(y[e, s0][:, t, :], ybank[e, t, s0], RELU, bias=column)
+                nc.scalar.activation(y[e, s0][:, t, :], ysums[e, t, s0], RELU, bias=column)
 
-        def gate_product(e, s0, s1, y0):
-            if (e, s0) not in c:
-                c[e, s0] = sbuf([P, s1 - s0, J], BF16, f"c{e}{s0}")
+        def gate_product(e, s0, s1, y0, tag=None):
+            c[e, s0] = sbuf([P, s1 - s0, J], BF16, f"c{e}{s0}", tag)
             weights = gbank[:, :, (e * C + s0) // R : (e * C + s1) // R].rearrange("p r m -> p m r")
             nc.vector.tensor_tensor(
                 out=c[e, s0].rearrange("p (m r) t -> p m t r", r=R),
@@ -207,46 +207,50 @@ def tile_moe_nxt_lin_relu_kernel(tc, xT, w, b, wp, gate, offs, out):
             wpbytes[h] = sbuf([P, 2 * P], U8, f"wpbytes{h}")
             quantize(wpcodes[h], wpbytes[h], wpgrouped[h].rearrange("p f j -> p (f j)"))
 
-        def project(engine, e, g, bank, tag=None):
-            n = len(obanks)
-            obanks.append(psum.tile([P, C], F32, name=f"obank{n}", tag=f"bank{bank}"))
-            h, i = divmod(g, 2)
-            nc.tensor.matmul_mx(
-                out=obanks[n][:],
-                lhsT=wpcodes[h][:, i * P : (i + 1) * P].bitcast(FP8X4),
-                lhsT_scale=wpbytes[h][:, i * P : (i + 1) * P],
-                rhs=ccodes[e].bitcast(FP8X4),
-                rhs_scale=cbytes[e],
-                start=True,
-                stop=True,
-            )
-            result[e, g] = sbuf([P, C], F32, f"result{e}{g}", tag)
-            move(engine, result[e, g], obanks[n][:])
+        def project(engine, e, groups, s0, s1, bank, tag=None):
+            name = f"{e}{groups[0]}{s0}"
+            sums = psum.tile([P, len(groups), s1 - s0], F32, name=f"obank{name}", tag=f"bank{bank}")
+            rows = sbuf([P, len(groups), s1 - s0], F32, f"result{name}", tag)
+            for n, g in enumerate(groups):
+                h, i = divmod(g, 2)
+                nc.tensor.matmul_mx(
+                    out=sums[:, n, :],
+                    lhsT=wpcodes[h][:, i * P : (i + 1) * P].bitcast(FP8X4),
+                    lhsT_scale=wpbytes[h][:, i * P : (i + 1) * P],
+                    rhs=ccodes[e][:, s0:s1].bitcast(FP8X4),
+                    rhs_scale=cbytes[e][:, s0:s1],
+                    start=True,
+                    stop=True,
+                )
+                result[e, g] = result.get((e, g), []) + [(s0, s1, rows[:, n, :])]
+            move(engine, rows, sums[:])
 
-        def scatter(engine, e, g):
-            move_indirect(engine, window[g][:].indirect(slots(e, 0, C)), result[e, g])
+        def scatter(engine, e, g, s0, s1):
+            for r0, r1, rows in result[e, g]:
+                if r0 <= s0 and s1 <= r1:
+                    move_indirect(engine, window[g][:].indirect(slots(e, s0, s1)), rows[:, s0 - r0 : s1 - r0])
 
         def store(g):
-            queue = nc.scalar if g == 2 else nc.sync
+            queue = nc.scalar if g == 3 else nc.sync
             queue.dma_start(out[g * P : (g + 1) * P, :], window[g][:, 0:T])
 
         for j in range(J):
             gather("vector", 0, j, 0, 0, C)
             gather("scalar", 0, j, 1, 0, C)
-        quantize_x(0, 0)
         quantize_x(1, 0)
         first = [(0, H, [0, 1, 2, 3]), (H, C, [5, 5, 6, 6])]
         prepare_w(0, 0)
-        for s0, s1, banks in first:
-            multiply(0, 0, s0, s1, banks)
         prepare_w(0, 1)
         for j in range(2):
             gather("vector", 1, j, 0, 0, C)
             gather("scalar", 1, j, 1, 0, C)
+        quantize_x(0, 0, "xrow11")
+        for s0, s1, banks in first:
+            multiply(0, 0, s0, s1, banks)
         for j in range(2, J):
-            for e in range(E):
-                gather("vector", 1, j, e, 0, H)
-                gather("scalar", 1, j, e, H, C)
+            gather("vector", 1, j, 0, 0, H)
+            gather("scalar", 1, j, 0, H, C)
+            gather("scalar", 1, j, 1, 0, C)
         quantize_x(0, 1)
         for s0, s1, banks in first:
             multiply(0, 1, s0, s1, banks)
@@ -254,18 +258,22 @@ def tile_moe_nxt_lin_relu_kernel(tc, xT, w, b, wp, gate, offs, out):
         for s0 in (0, H):
             for t in range(J):
                 relu("scalar", 0, t, s0, s0 + H)
-        quantize_x(1, 1)
+        quantize_x(1, 1, "wpraw0")
         quantize_wp(0)
-        for s0 in (0, H):
-            gate_product(0, s0, s0 + H, s0)
-        group_w("scalar", 1, 0, 1, 0, P)
-        for s0 in (0, H):
-            quantize_c(0, s0, s0 + H)
-        group_w("vector", 1, 0, 0, 0, P, f"y0{H}")
-        project("scalar", 0, 0, 7)
-        project("vector", 0, 1, 5)
-        scatter("scalar", 0, 0)
-        scatter("scalar", 0, 1)
+        gate_product(0, 0, H, 0)
+        quantize_c(0, 0, H)
+        group_w("scalar", 1, 0, 1, 0, W_SCALAR)
+        project("scalar", 0, [0, 1], 0, H, 7)
+        gate_product(0, H, C, H, "y00")
+        group_w("vector", 1, 0, 1, W_SCALAR, P)
+        group_w("vector", 1, 0, 0, 0, P // 2, "c00")
+        quantize_c(0, H, C)
+        group_w("vector", 1, 0, 0, P // 2, P)
+        scatter("scalar", 0, 0, 0, H)
+        project("scalar", 0, [0, 1], H, C, 5)
+        scatter("scalar", 0, 1, 0, H)
+        scatter("scalar", 0, 0, H, C)
+        scatter("scalar", 0, 1, H, C)
         quantize_w(1, 0, 1)
         quantize_w(1, 0, 0)
         multiply(1, 0, 0, C, [0, 1, 2, 3])
@@ -275,26 +283,33 @@ def tile_moe_nxt_lin_relu_kernel(tc, xT, w, b, wp, gate, offs, out):
             quantize_w(1, 1, u)
         multiply(1, 1, 0, C, [0, 1, 2, 3])
         group_wp(1)
-        for t in range(J - 1):
-            relu("scalar", 1, t, 0, C)
-        relu("vector", 1, J - 1, 0, C)
+        for t in range(2):
+            relu("scalar", 1, t, 0, H)
+        relu("vector", 1, 2, 0, H)
+        relu("vector", 1, 3, 0, H)
+        relu("vector", 1, 3, H, C)
+        for t in range(3):
+            relu("scalar", 1, t, H, C)
         quantize_wp(1)
-        project("scalar", 0, 2, 6)
+        project("scalar", 0, [2], 0, C, 6)
         for s0 in (0, H):
-            gate_product(1, s0, s0 + H, 0)
-        scatter("scalar", 0, 2)
-        project("vector", 0, 3, 3)
-        quantize(ccodes[1], cbytes[1], c_last.rearrange("p s t -> p (s t)"))
-        scatter("vector", 0, 3)
-        project("scalar", 1, 0, 5)
-        project("scalar", 1, 2, 0)
-        scatter("scalar", 1, 0)
+            gate_product(1, s0, s0 + H, s0)
+        project("vector", 0, [3], 0, H, 7, "y10")
+        scatter("scalar", 0, 2, 0, C)
+        for s0 in (0, H):
+            quantize_c(1, s0, s0 + H)
+        scatter("vector", 0, 3, 0, H)
+        project("vector", 1, [0], 0, C, 5)
+        project("scalar", 1, [1], 0, C, 0)
+        project("scalar", 1, [2], 0, C, 1)
+        scatter("vector", 1, 0, 0, C)
         store(0)
-        project("vector", 1, 1, 5)
-        project("vector", 1, 3, 1)
-        scatter("vector", 1, 1)
+        project("vector", 1, [3], 0, C, 2)
+        scatter("scalar", 1, 1, 0, C)
         store(1)
-        scatter("scalar", 1, 2)
+        project("scalar", 0, [3], H, C, 0)
+        scatter("vector", 1, 3, 0, C)
+        scatter("scalar", 1, 2, 0, C)
         store(2)
-        scatter("vector", 1, 3)
+        scatter("scalar", 0, 3, H, C)
         store(3)

@@ -28,7 +28,7 @@ R = S // P
 H = C // 2
 
 W_SCALAR = 104
-W_VECTOR = 16
+W_VECTOR = 96
 
 
 def tile_moe_nxt_lin_relu_kernel(tc, xT, w, b, wp, gate, offs, out):
@@ -89,6 +89,7 @@ def tile_moe_nxt_lin_relu_kernel(tc, xT, w, b, wp, gate, offs, out):
             nc.gpsimd.memset(window[g][:, 0:T], 0.0)
 
         xgrouped = {(e, a): sbuf([P, C, J], BF16, f"xgrouped{e}{a}") for e in range(E) for a in range(PASSES)}
+        xplain = [sbuf([P, J, C], BF16, f"xplain{a}") for a in range(PASSES)]
         xcodes = {}
         xbytes = {}
         wgrouped = {}
@@ -126,6 +127,15 @@ def tile_moe_nxt_lin_relu_kernel(tc, xT, w, b, wp, gate, offs, out):
         def gather(engine, a, j, e, s0, s1):
             move_indirect(engine, xgrouped[e, a][:, s0:s1, j], xrow[a, j][:].indirect(slots(e, s0, s1)))
 
+        def gather_plain(a, j):
+            move_indirect("scalar", xplain[a][:, j, :], xrow[a, j][:].indirect(slots(1, 0, C)))
+
+        def group_x(a):
+            nc.scalar.copy(
+                out=xgrouped[1, a].rearrange("p (x i) j -> p x j i", i=4),
+                in_=xplain[a].rearrange("p j (x i) -> p x j i", i=4),
+            )
+
         def quantize_x(e, a, tag=None):
             xcodes[e, a] = sbuf([P, C], U32, f"xcodes{e}{a}", tag)
             xbytes[e, a] = sbuf([P, C], U8, f"xbytes{e}{a}")
@@ -147,9 +157,9 @@ def tile_moe_nxt_lin_relu_kernel(tc, xT, w, b, wp, gate, offs, out):
             quantize(wcodes[e, a, u], wbytes[e, a, u], wgrouped[e, a, u].rearrange("p t m j -> p (t m j)"))
 
         def prepare_w(e, a):
-            group_w("vector", e, a, 0, 0, P)
-            group_w("scalar", e, a, 1, W_VECTOR, P)
-            group_w("vector", e, a, 1, 0, W_VECTOR)
+            group_w("vector", e, a, 0, 0, W_VECTOR)
+            group_w("scalar", e, a, 0, W_VECTOR, P)
+            group_w("scalar", e, a, 1, 0, P)
             quantize_w(e, a, 0)
             quantize_w(e, a, 1)
 
@@ -236,21 +246,22 @@ def tile_moe_nxt_lin_relu_kernel(tc, xT, w, b, wp, gate, offs, out):
 
         for j in range(J):
             gather("vector", 0, j, 0, 0, C)
-            gather("scalar", 0, j, 1, 0, C)
+            gather_plain(0, j)
+        group_x(0)
         quantize_x(1, 0)
         first = [(0, H, [0, 1, 2, 3]), (H, C, [5, 5, 6, 6])]
         prepare_w(0, 0)
         prepare_w(0, 1)
         for j in range(2):
             gather("vector", 1, j, 0, 0, C)
-            gather("scalar", 1, j, 1, 0, C)
+            gather_plain(1, j)
         quantize_x(0, 0, "xrow11")
         for s0, s1, banks in first:
             multiply(0, 0, s0, s1, banks)
         for j in range(2, J):
-            gather("vector", 1, j, 0, 0, H)
-            gather("scalar", 1, j, 0, H, C)
-            gather("scalar", 1, j, 1, 0, C)
+            gather("vector", 1, j, 0, 0, C)
+            gather_plain(1, j)
+        group_x(1)
         quantize_x(0, 1)
         for s0, s1, banks in first:
             multiply(0, 1, s0, s1, banks)

@@ -99,8 +99,8 @@ def tile_moe_nxt_lin_relu_kernel(tc, xT, w, b, wp, gate, offs, out):
         ysums = {}
         y = {}
         c = {}
-        ccodes = [sbuf([P, C], U32, f"ccodes{e}") for e in range(E)]
-        cbytes = [sbuf([P, C], U8, f"cbytes{e}") for e in range(E)]
+        ccodes = sbuf([P, S], U32, "ccodes")
+        cbytes = sbuf([P, S], U8, "cbytes")
         wpgrouped = {}
         wpcodes = {}
         wpbytes = {}
@@ -203,7 +203,7 @@ def tile_moe_nxt_lin_relu_kernel(tc, xT, w, b, wp, gate, offs, out):
             )
 
         def quantize_c(e, s0, s1):
-            quantize(ccodes[e][:, s0:s1], cbytes[e][:, s0:s1], c[e, s0].rearrange("p s t -> p (s t)"))
+            quantize(ccodes[:, e * C + s0 : e * C + s1], cbytes[:, e * C + s0 : e * C + s1], c[e, s0].rearrange("p s t -> p (s t)"))
 
         def group_wp(h):
             wpgrouped[h] = sbuf([P, 2 * P, J], BF16, f"wpgrouped{h}")
@@ -217,28 +217,29 @@ def tile_moe_nxt_lin_relu_kernel(tc, xT, w, b, wp, gate, offs, out):
             wpbytes[h] = sbuf([P, 2 * P], U8, f"wpbytes{h}")
             quantize(wpcodes[h], wpbytes[h], wpgrouped[h].rearrange("p f j -> p (f j)"))
 
-        def project(engine, e, groups, s0, s1, bank, tag=None):
-            name = f"{e}{groups[0]}{s0}"
-            sums = psum.tile([P, len(groups), s1 - s0], F32, name=f"obank{name}", tag=f"bank{bank}")
-            rows = sbuf([P, len(groups), s1 - s0], F32, f"result{name}", tag)
-            for n, g in enumerate(groups):
+        def project(engine, pieces, bank, tag=None):
+            width = sum(s1 - s0 for g, s0, s1 in pieces)
+            name = f"{pieces[0][0]}_{pieces[0][1]}"
+            sums = psum.tile([P, width], F32, name=f"obank{name}", tag=f"bank{bank}")
+            rows = sbuf([P, width], F32, f"result{name}", tag)
+            at = 0
+            for g, s0, s1 in pieces:
                 h, i = divmod(g, 2)
                 nc.tensor.matmul_mx(
-                    out=sums[:, n, :],
+                    out=sums[:, at : at + s1 - s0],
                     lhsT=wpcodes[h][:, i * P : (i + 1) * P].bitcast(FP8X4),
                     lhsT_scale=wpbytes[h][:, i * P : (i + 1) * P],
-                    rhs=ccodes[e][:, s0:s1].bitcast(FP8X4),
-                    rhs_scale=cbytes[e][:, s0:s1],
+                    rhs=ccodes[:, s0:s1].bitcast(FP8X4),
+                    rhs_scale=cbytes[:, s0:s1],
                     start=True,
                     stop=True,
                 )
-                result[e, g] = result.get((e, g), []) + [(s0, s1, rows[:, n, :])]
+                result[g, s0] = rows[:, at:]
+                at = at + s1 - s0
             move(engine, rows, sums[:])
 
-        def scatter(engine, e, g, s0, s1):
-            for r0, r1, rows in result[e, g]:
-                if r0 <= s0 and s1 <= r1:
-                    move_indirect(engine, window[g][:].indirect(slots(e, s0, s1)), rows[:, s0 - r0 : s1 - r0])
+        def scatter(engine, g, s0, s1):
+            move_indirect(engine, window[g][:].indirect(slots(0, s0, s1)), result[g, s0][:, 0 : s1 - s0])
 
         def store(g):
             queue = nc.scalar if g == 3 else nc.sync
@@ -274,17 +275,16 @@ def tile_moe_nxt_lin_relu_kernel(tc, xT, w, b, wp, gate, offs, out):
         gate_product(0, 0, H, 0)
         quantize_c(0, 0, H)
         group_w("scalar", 1, 0, 1, 0, W_SCALAR)
-        project("scalar", 0, [0, 1], 0, H, 7)
+        project("scalar", [(0, 0, H), (1, 0, H)], 7)
+        group_w("scalar", 1, 0, 1, W_SCALAR, P)
         gate_product(0, H, C, H, "y00")
-        group_w("vector", 1, 0, 1, W_SCALAR, P)
         group_w("vector", 1, 0, 0, 0, P // 2, "c00")
         quantize_c(0, H, C)
         group_w("vector", 1, 0, 0, P // 2, P)
-        scatter("scalar", 0, 0, 0, H)
-        project("scalar", 0, [0, 1], H, C, 5)
-        scatter("scalar", 0, 1, 0, H)
-        scatter("scalar", 0, 0, H, C)
-        scatter("scalar", 0, 1, H, C)
+        scatter("scalar", 0, 0, H)
+        project("scalar", [(0, H, C)], 5)
+        scatter("scalar", 1, 0, H)
+        scatter("scalar", 0, H, C)
         quantize_w(1, 0, 1)
         quantize_w(1, 0, 0)
         multiply(1, 0, 0, C, [0, 1, 2, 3])
@@ -294,33 +294,28 @@ def tile_moe_nxt_lin_relu_kernel(tc, xT, w, b, wp, gate, offs, out):
             quantize_w(1, 1, u)
         multiply(1, 1, 0, C, [0, 1, 2, 3])
         group_wp(1)
-        for t in range(2):
-            relu("scalar", 1, t, 0, H)
-        relu("vector", 1, 2, 0, H)
-        relu("vector", 1, 3, 0, H)
-        relu("vector", 1, 3, H, C)
-        for t in range(3):
-            relu("scalar", 1, t, H, C)
+        for t in range(J):
+            relu("vector", 1, t, 0, H)
         quantize_wp(1)
-        project("scalar", 0, [2], 0, C, 6)
+        for t in range(J):
+            relu("scalar", 1, t, H, C)
+        project("scalar", [(2, 0, C)], 6)
         for s0 in (0, H):
             gate_product(1, s0, s0 + H, s0)
-        project("vector", 0, [3], 0, H, 7, "y10")
-        scatter("scalar", 0, 2, 0, C)
+        project("vector", [(1, H, C)], 7, "y10")
+        scatter("scalar", 2, 0, C)
         for s0 in (0, H):
             quantize_c(1, s0, s0 + H)
-        scatter("vector", 0, 3, 0, H)
-        project("vector", 1, [0], 0, C, 5)
-        project("scalar", 1, [1], 0, C, 0)
-        project("scalar", 1, [2], 0, C, 1)
-        scatter("vector", 1, 0, 0, C)
+        scatter("vector", 1, H, C)
+        project("vector", [(0, C, S)], 5)
+        project("vector", [(1, C, S)], 0)
+        project("scalar", [(2, C, S)], 1)
+        scatter("vector", 0, C, S)
         store(0)
-        project("vector", 1, [3], 0, C, 2)
-        scatter("scalar", 1, 1, 0, C)
+        scatter("scalar", 1, C, S)
         store(1)
-        project("scalar", 0, [3], H, C, 0)
-        scatter("vector", 1, 3, 0, C)
-        scatter("scalar", 1, 2, 0, C)
+        project("vector", [(3, 0, S)], 2)
+        scatter("vector", 3, 0, S)
+        scatter("scalar", 2, C, S)
         store(2)
-        scatter("scalar", 0, 3, H, C)
         store(3)

@@ -270,23 +270,23 @@ def tile_moe_nxt_lin_relu_kernel(tc, xT, w, b, wp, gate, offs, out):
         for s0 in (0, H):
             for t in range(J):
                 relu("scalar", 0, t, s0, s0 + H)
-        quantize_x(1, 1, "wpraw0")
         quantize_wp(0)
+        quantize_x(1, 1, "wpraw0")
         gate_product(0, 0, H, 0)
+        group_w("vector", 1, 0, 0, 0, P // 2, "xgrouped11")
         quantize_c(0, 0, H)
         group_w("scalar", 1, 0, 1, 0, W_SCALAR)
         project("scalar", [(0, 0, H), (1, 0, H)], 7)
         group_w("scalar", 1, 0, 1, W_SCALAR, P)
         gate_product(0, H, C, H, "y00")
-        group_w("vector", 1, 0, 0, 0, P // 2, "c00")
-        quantize_c(0, H, C)
         group_w("vector", 1, 0, 0, P // 2, P)
+        quantize_c(0, H, C)
         scatter("scalar", 0, 0, H)
-        project("scalar", [(0, H, C)], 5)
         scatter("scalar", 1, 0, H)
-        scatter("scalar", 0, H, C)
         quantize_w(1, 0, 1)
         quantize_w(1, 0, 0)
+        project("vector", [(0, H, C)], 5)
+        scatter("scalar", 0, H, C)
         multiply(1, 0, 0, C, [0, 1, 2, 3])
         for u in range(2):
             group_w("vector", 1, 1, u, 0, P)
@@ -295,10 +295,10 @@ def tile_moe_nxt_lin_relu_kernel(tc, xT, w, b, wp, gate, offs, out):
         multiply(1, 1, 0, C, [0, 1, 2, 3])
         group_wp(1)
         for t in range(J):
-            relu("vector", 1, t, 0, H)
+            relu("vector" if t < 1 else "scalar", 1, t, 0, H)
         quantize_wp(1)
         for t in range(J):
-            relu("scalar", 1, t, H, C)
+            relu("vector" if t < 1 else "scalar", 1, t, H, C)
         project("scalar", [(2, 0, C)], 6)
         for s0 in (0, H):
             gate_product(1, s0, s0 + H, s0)
@@ -309,12 +309,12 @@ def tile_moe_nxt_lin_relu_kernel(tc, xT, w, b, wp, gate, offs, out):
         scatter("vector", 1, H, C)
         project("vector", [(0, C, S)], 5)
         project("vector", [(1, C, S)], 0)
+        project("scalar", [(3, 0, C), (3, C, S)], 2)
         project("scalar", [(2, C, S)], 1)
         scatter("vector", 0, C, S)
         store(0)
         scatter("scalar", 1, C, S)
         store(1)
-        project("vector", [(3, 0, S)], 2)
         scatter("vector", 3, 0, S)
         scatter("scalar", 2, C, S)
         store(2)

@@ -84,9 +84,9 @@ def tile_moe_nxt_lin_relu_kernel(tc, xT, w, b, wp, gate, offs, out):
         zeros = sbuf([P, 8], F32, "zeros")
         nc.vector.memset(zeros, 0.0)
         nc.scalar.activation(window[0][:, 0:8], zeros, RELU)
-        nc.gpsimd.memset(window[0][:, 8:T], 0.0)
+        nc.vector.memset(window[0][:, 8:T], 0.0)
         for g in range(1, G):
-            nc.gpsimd.memset(window[g][:, 0:T], 0.0)
+            nc.vector.memset(window[g][:], 0.0)
 
         xgrouped = {(e, a): sbuf([P, C, J], BF16, f"xgrouped{e}{a}") for e in range(E) for a in range(PASSES)}
         xplain = [sbuf([P, J, C], BF16, f"xplain{a}") for a in range(PASSES)]
@@ -249,16 +249,16 @@ def tile_moe_nxt_lin_relu_kernel(tc, xT, w, b, wp, gate, offs, out):
             gather("vector", 0, j, 0, 0, C)
             gather_plain(0, j)
         group_x(0)
+        quantize_x(0, 0)
         quantize_x(1, 0)
         first = [(0, H, [0, 1, 2, 3]), (H, C, [5, 5, 6, 6])]
         prepare_w(0, 0)
+        for s0, s1, banks in first:
+            multiply(0, 0, s0, s1, banks)
         prepare_w(0, 1)
         for j in range(2):
             gather("vector", 1, j, 0, 0, C)
             gather_plain(1, j)
-        quantize_x(0, 0, "xrow11")
-        for s0, s1, banks in first:
-            multiply(0, 0, s0, s1, banks)
         for j in range(2, J):
             gather("vector", 1, j, 0, 0, C)
             gather_plain(1, j)
@@ -310,9 +310,9 @@ def tile_moe_nxt_lin_relu_kernel(tc, xT, w, b, wp, gate, offs, out):
         project("vector", [(0, C, S)], 5)
         project("vector", [(1, C, S)], 0)
         project("scalar", [(3, 0, C), (3, C, S)], 2)
-        project("scalar", [(2, C, S)], 1)
         scatter("vector", 0, C, S)
         store(0)
+        project("vector", [(2, C, S)], 1)
         scatter("scalar", 1, C, S)
         store(1)
         scatter("vector", 3, 0, S)

@@ -10,6 +10,7 @@ FLOPS = 2 * K * N * S + 2 * N * M * S
 F32 = mybir.dt.float32
 BF16 = mybir.dt.bfloat16
 U32 = mybir.dt.uint32
+I32 = mybir.dt.int32
 U16 = mybir.dt.uint16
 U8 = mybir.dt.uint8
 FP8X4 = mybir.dt.float8_e4m3fn_x4
@@ -27,6 +28,7 @@ G = M // P
 R = S // P
 H = C // 2
 
+W_FIRST = 176
 W_SCALAR = 104
 W_VECTOR = 96
 
@@ -47,9 +49,12 @@ def tile_moe_nxt_lin_relu_kernel(tc, xT, w, b, wp, gate, offs, out):
         wraw = {}
         wpraw = {}
 
-        def load_x(a, j):
-            xrow[a, j] = keep.tile([P, T], F32, name=f"xrow{a}{j}", align_bytes=64)
-            nc.sync.dma_start(xrow[a, j][:], xT[a * KP : (a + 1) * KP, :].rearrange("(p j) t -> p j t", j=J)[:, j, :])
+        def load_x(a, j, rows):
+            tile = sbuf([P, rows * T], F32, f"xrow{a}{j}")
+            source = xT[a * KP : (a + 1) * KP, :].rearrange("(p j) t -> p (j t)", j=J)
+            nc.sync.dma_start(tile, source[:, j * T : (j + rows) * T])
+            for i in range(rows):
+                xrow[a, j + i] = tile[:, i * T : (i + 1) * T]
 
         def load_w(e, a):
             wraw[e, a] = sbuf([P, J, N], F32, f"wraw{e}{a}")
@@ -61,14 +66,13 @@ def tile_moe_nxt_lin_relu_kernel(tc, xT, w, b, wp, gate, offs, out):
 
         nc.scalar.dma_start(gate_row, gate[0, :].rearrange("(p r) -> p r", r=R))
         nc.scalar.dma_start(bias, b.rearrange("(p t) e -> p (t e)", t=J))
-        load_x(0, 0)
+        load_x(0, 0, 2)
         nc.sync.dma_start(offsets[:], offs)
-        for j in range(1, J):
-            load_x(0, j)
+        load_x(0, 2, 2)
         load_w(0, 0)
         load_w(0, 1)
         for j in range(J):
-            load_x(1, j)
+            load_x(1, j, 1)
         load_wp(0)
         load_w(1, 0)
         load_w(1, 1)
@@ -84,12 +88,15 @@ def tile_moe_nxt_lin_relu_kernel(tc, xT, w, b, wp, gate, offs, out):
         zeros = sbuf([P, 8], F32, "zeros")
         nc.vector.memset(zeros, 0.0)
         nc.scalar.activation(window[0][:, 0:8], zeros, RELU)
-        nc.vector.memset(window[0][:, 8:T], 0.0)
+        nc.vector.memset(window[0][:, 8:T].bitcast(I32), 0)
         for g in range(1, G):
-            nc.vector.memset(window[g][:], 0.0)
+            nc.vector.memset(window[g][:].bitcast(I32), 0)
+
+        gates = sbuf([P, S], F32, "gates")
+        nc.scalar.copy(out=gates.rearrange("p (m r) -> p m r", r=R), in_=gbank[:].rearrange("p r m -> p m r"))
 
         xgrouped = {(e, a): sbuf([P, C, J], BF16, f"xgrouped{e}{a}") for e in range(E) for a in range(PASSES)}
-        xplain = [sbuf([P, J, C], BF16, f"xplain{a}") for a in range(PASSES)]
+        xplain = [sbuf([P, J, C], BF16 if a else F32, f"xplain{a}") for a in range(PASSES)]
         xcodes = {}
         xbytes = {}
         wgrouped = {}
@@ -125,10 +132,10 @@ def tile_moe_nxt_lin_relu_kernel(tc, xT, w, b, wp, gate, offs, out):
             nc.vector.quantize_mx(out=codes.bitcast(FP8X4), scales=scales, in_=grouped)
 
         def gather(engine, a, j, e, s0, s1):
-            move_indirect(engine, xgrouped[e, a][:, s0:s1, j], xrow[a, j][:].indirect(slots(e, s0, s1)))
+            move_indirect(engine, xgrouped[e, a][:, s0:s1, j], xrow[a, j].indirect(slots(e, s0, s1)))
 
         def gather_plain(a, j):
-            move_indirect("scalar", xplain[a][:, j, :], xrow[a, j][:].indirect(slots(1, 0, C)))
+            move_indirect("scalar", xplain[a][:, j, :], xrow[a, j].indirect(slots(1, 0, C)))
 
         def group_x(a):
             nc.scalar.copy(
@@ -156,12 +163,13 @@ def tile_moe_nxt_lin_relu_kernel(tc, xT, w, b, wp, gate, offs, out):
             wbytes[e, a, u] = sbuf([P, 2 * P], U8, f"wbytes{e}{a}{u}")
             quantize(wcodes[e, a, u], wbytes[e, a, u], wgrouped[e, a, u].rearrange("p t m j -> p (t m j)"))
 
-        def prepare_w(e, a):
-            group_w("vector", e, a, 0, 0, W_VECTOR)
-            group_w("scalar", e, a, 0, W_VECTOR, P)
-            group_w("scalar", e, a, 1, 0, P)
-            quantize_w(e, a, 0)
-            quantize_w(e, a, 1)
+        def prepare_w(e, a, share):
+            for engine, lo, hi in (("vector", 0, share), ("scalar", share, 2 * P)):
+                for u in range(2):
+                    if min(hi - u * P, P) > max(lo - u * P, 0):
+                        group_w(engine, e, a, u, max(lo - u * P, 0), min(hi - u * P, P))
+            for u in range(2):
+                quantize_w(e, a, u)
 
         def multiply(e, a, s0, s1, banks):
             for t in range(J):
@@ -194,11 +202,11 @@ def tile_moe_nxt_lin_relu_kernel(tc, xT, w, b, wp, gate, offs, out):
 
         def gate_product(e, s0, s1, y0, tag=None):
             c[e, s0] = sbuf([P, s1 - s0, J], BF16, f"c{e}{s0}", tag)
-            weights = gbank[:, :, (e * C + s0) // R : (e * C + s1) // R].rearrange("p r m -> p m r")
+            weights = gates[:, e * C + s0 : e * C + s1].rearrange("p (m r) -> p m r", r=2)
             nc.vector.tensor_tensor(
-                out=c[e, s0].rearrange("p (m r) t -> p m t r", r=R),
-                in0=y[e, y0][:, :, s0 - y0 : s1 - y0].rearrange("p t (m r) -> p m t r", r=R),
-                in1=weights.unsqueeze(2).to_broadcast([P, (s1 - s0) // R, J, R]),
+                out=c[e, s0].rearrange("p (m r) t -> p m t r", r=2),
+                in0=y[e, y0][:, :, s0 - y0 : s1 - y0].rearrange("p t (m r) -> p m t r", r=2),
+                in1=weights.unsqueeze(2).to_broadcast([P, (s1 - s0) // 2, J, 2]),
                 op=MULT,
             )
 
@@ -252,10 +260,10 @@ def tile_moe_nxt_lin_relu_kernel(tc, xT, w, b, wp, gate, offs, out):
         quantize_x(0, 0)
         quantize_x(1, 0)
         first = [(0, H, [0, 1, 2, 3]), (H, C, [5, 5, 6, 6])]
-        prepare_w(0, 0)
+        prepare_w(0, 0, W_FIRST)
         for s0, s1, banks in first:
             multiply(0, 0, s0, s1, banks)
-        prepare_w(0, 1)
+        prepare_w(0, 1, W_VECTOR)
         for j in range(2):
             gather("vector", 1, j, 0, 0, C)
             gather_plain(1, j)

@@ -29,7 +29,8 @@ R = S // P
 H = C // 2
 
 W_FIRST = 176
-W_SCALAR = 104
+X_SCALAR = 176
+W_SCALAR = 112
 W_VECTOR = 96
 
 
@@ -137,10 +138,11 @@ def tile_moe_nxt_lin_relu_kernel(tc, xT, w, b, wp, gate, offs, out):
         def gather_plain(a, j):
             move_indirect("scalar", xplain[a][:, j, :], xrow[a, j].indirect(slots(1, 0, C)))
 
-        def group_x(a):
-            nc.scalar.copy(
-                out=xgrouped[1, a].rearrange("p (x i) j -> p x j i", i=4),
-                in_=xplain[a].rearrange("p j (x i) -> p x j i", i=4),
+        def group_x(engine, a, s0, s1):
+            move(
+                engine,
+                xgrouped[1, a][:, s0:s1, :].rearrange("p (x i) j -> p x j i", i=4),
+                xplain[a][:, :, s0:s1].rearrange("p j (x i) -> p x j i", i=4),
             )
 
         def quantize_x(e, a, tag=None):
@@ -256,7 +258,7 @@ def tile_moe_nxt_lin_relu_kernel(tc, xT, w, b, wp, gate, offs, out):
         for j in range(J):
             gather("vector", 0, j, 0, 0, C)
             gather_plain(0, j)
-        group_x(0)
+        group_x("scalar", 0, 0, C)
         quantize_x(0, 0)
         quantize_x(1, 0)
         first = [(0, H, [0, 1, 2, 3]), (H, C, [5, 5, 6, 6])]
@@ -270,7 +272,8 @@ def tile_moe_nxt_lin_relu_kernel(tc, xT, w, b, wp, gate, offs, out):
         for j in range(2, J):
             gather("vector", 1, j, 0, 0, C)
             gather_plain(1, j)
-        group_x(1)
+        group_x("scalar", 1, 0, X_SCALAR)
+        group_x("vector", 1, X_SCALAR, C)
         quantize_x(0, 1)
         for s0, s1, banks in first:
             multiply(0, 1, s0, s1, banks)
@@ -285,14 +288,14 @@ def tile_moe_nxt_lin_relu_kernel(tc, xT, w, b, wp, gate, offs, out):
         quantize_c(0, 0, H)
         group_w("scalar", 1, 0, 1, 0, W_SCALAR)
         project("scalar", [(0, 0, H), (1, 0, H)], 7)
-        group_w("scalar", 1, 0, 1, W_SCALAR, P)
         gate_product(0, H, C, H, "y00")
         group_w("vector", 1, 0, 0, P // 2, P)
         quantize_c(0, H, C)
+        group_w("vector", 1, 0, 1, W_SCALAR, P)
         scatter("scalar", 0, 0, H)
         scatter("scalar", 1, 0, H)
-        quantize_w(1, 0, 1)
         quantize_w(1, 0, 0)
+        quantize_w(1, 0, 1)
         project("vector", [(0, H, C)], 5)
         scatter("scalar", 0, H, C)
         multiply(1, 0, 0, C, [0, 1, 2, 3])

@@ -29,8 +29,7 @@ R = S // P
 H = C // 2
 
 W_FIRST = 176
-X_SCALAR = 176
-W_SCALAR = 112
+W_SECOND = 112
 W_VECTOR = 96
 
 
@@ -96,7 +95,7 @@ def tile_moe_nxt_lin_relu_kernel(tc, xT, w, b, wp, gate, offs, out):
         gates = sbuf([P, S], F32, "gates")
         nc.scalar.copy(out=gates.rearrange("p (m r) -> p m r", r=R), in_=gbank[:].rearrange("p r m -> p m r"))
 
-        xgrouped = {(e, a): sbuf([P, C, J], BF16, f"xgrouped{e}{a}") for e in range(E) for a in range(PASSES)}
+        xgrouped = {}
         xplain = [sbuf([P, J, C], BF16 if a else F32, f"xplain{a}") for a in range(PASSES)]
         xcodes = {}
         xbytes = {}
@@ -133,22 +132,27 @@ def tile_moe_nxt_lin_relu_kernel(tc, xT, w, b, wp, gate, offs, out):
             nc.vector.quantize_mx(out=codes.bitcast(FP8X4), scales=scales, in_=grouped)
 
         def gather(engine, a, j, e, s0, s1):
-            move_indirect(engine, xgrouped[e, a][:, s0:s1, j], xrow[a, j].indirect(slots(e, s0, s1)))
+            if j == 0:
+                xgrouped[e, a, s0] = sbuf([P, s1 - s0, J], BF16, f"xgrouped{e}{a}{s0}")
+            move_indirect(engine, xgrouped[e, a, s0][:, :, j], xrow[a, j].indirect(slots(e, s0, s1)))
 
         def gather_plain(a, j):
             move_indirect("scalar", xplain[a][:, j, :], xrow[a, j].indirect(slots(1, 0, C)))
 
-        def group_x(engine, a, s0, s1):
+        def group_x(engine, a, s0, s1, tag=None):
+            xgrouped[1, a, s0] = sbuf([P, s1 - s0, J], BF16, f"xgrouped1{a}{s0}", tag)
             move(
                 engine,
-                xgrouped[1, a][:, s0:s1, :].rearrange("p (x i) j -> p x j i", i=4),
+                xgrouped[1, a, s0].rearrange("p (x i) j -> p x j i", i=4),
                 xplain[a][:, :, s0:s1].rearrange("p j (x i) -> p x j i", i=4),
             )
 
-        def quantize_x(e, a, tag=None):
-            xcodes[e, a] = sbuf([P, C], U32, f"xcodes{e}{a}", tag)
-            xbytes[e, a] = sbuf([P, C], U8, f"xbytes{e}{a}")
-            quantize(xcodes[e, a], xbytes[e, a], xgrouped[e, a].rearrange("p s j -> p (s j)"))
+        def quantize_x(e, a, s0, s1, tag=None):
+            if s0 == 0:
+                xcodes[e, a] = sbuf([P, C], U32, f"xcodes{e}{a}", tag)
+                xbytes[e, a] = sbuf([P, C], U8, f"xbytes{e}{a}")
+            grouped = xgrouped[e, a, s0].rearrange("p s j -> p (s j)")
+            quantize(xcodes[e, a][:, s0:s1], xbytes[e, a][:, s0:s1], grouped)
 
         def group_w(engine, e, a, u, m0, m1, tag=None):
             if (e, a, u) not in wgrouped:
@@ -227,11 +231,12 @@ def tile_moe_nxt_lin_relu_kernel(tc, xT, w, b, wp, gate, offs, out):
             wpbytes[h] = sbuf([P, 2 * P], U8, f"wpbytes{h}")
             quantize(wpcodes[h], wpbytes[h], wpgrouped[h].rearrange("p f j -> p (f j)"))
 
-        def project(engine, pieces, bank, tag=None):
+        def project(engine, pieces, bank, tag=None, rows=None):
             width = sum(s1 - s0 for g, s0, s1 in pieces)
             name = f"{pieces[0][0]}_{pieces[0][1]}"
             sums = psum.tile([P, width], F32, name=f"obank{name}", tag=f"bank{bank}")
-            rows = sbuf([P, width], F32, f"result{name}", tag)
+            if rows is None:
+                rows = sbuf([P, width], F32, f"result{name}", tag)
             at = 0
             for g, s0, s1 in pieces:
                 h, i = divmod(g, 2)
@@ -246,7 +251,7 @@ def tile_moe_nxt_lin_relu_kernel(tc, xT, w, b, wp, gate, offs, out):
                 )
                 result[g, s0] = rows[:, at:]
                 at = at + s1 - s0
-            move(engine, rows, sums[:])
+            move(engine, rows[:, 0:width], sums[:])
 
         def scatter(engine, g, s0, s1):
             move_indirect(engine, window[g][:].indirect(slots(0, s0, s1)), result[g, s0][:, 0 : s1 - s0])
@@ -259,48 +264,46 @@ def tile_moe_nxt_lin_relu_kernel(tc, xT, w, b, wp, gate, offs, out):
             gather("vector", 0, j, 0, 0, C)
             gather_plain(0, j)
         group_x("scalar", 0, 0, C)
-        quantize_x(0, 0)
-        quantize_x(1, 0)
+        quantize_x(0, 0, 0, C)
+        quantize_x(1, 0, 0, C)
         first = [(0, H, [0, 1, 2, 3]), (H, C, [5, 5, 6, 6])]
         prepare_w(0, 0, W_FIRST)
         for s0, s1, banks in first:
             multiply(0, 0, s0, s1, banks)
         prepare_w(0, 1, W_VECTOR)
-        for j in range(2):
-            gather("vector", 1, j, 0, 0, C)
+        for j in range(J):
+            for s0 in (0, H):
+                gather("vector", 1, j, 0, s0, s0 + H)
             gather_plain(1, j)
-        for j in range(2, J):
-            gather("vector", 1, j, 0, 0, C)
-            gather_plain(1, j)
-        group_x("scalar", 1, 0, X_SCALAR)
-        group_x("vector", 1, X_SCALAR, C)
-        quantize_x(0, 1)
+        group_x("scalar", 1, 0, H)
         for s0, s1, banks in first:
+            quantize_x(0, 1, s0, s1)
             multiply(0, 1, s0, s1, banks)
+        group_x("vector", 1, H, C)
         group_wp(0)
         for s0 in (0, H):
             for t in range(J):
                 relu("scalar", 0, t, s0, s0 + H)
+        quantize_x(1, 1, 0, H)
+        quantize_x(1, 1, H, C)
         quantize_wp(0)
-        quantize_x(1, 1, "wpraw0")
-        gate_product(0, 0, H, 0)
-        group_w("vector", 1, 0, 0, 0, P // 2, "xgrouped11")
+        for s0 in (0, H):
+            gate_product(0, s0, s0 + H, s0)
         quantize_c(0, 0, H)
-        group_w("scalar", 1, 0, 1, 0, W_SCALAR)
-        project("scalar", [(0, 0, H), (1, 0, H)], 7)
-        gate_product(0, H, C, H, "y00")
-        group_w("vector", 1, 0, 0, P // 2, P)
+        group_w("scalar", 1, 0, 1, 0, P)
+        group_w("scalar", 1, 0, 0, W_SECOND, P, "y00")
+        early = sbuf([P, H + C], F32, "early")
+        project("scalar", [(1, 0, H), (0, 0, H)], 7, None, early)
         quantize_c(0, H, C)
-        group_w("vector", 1, 0, 1, W_SCALAR, P)
-        scatter("scalar", 0, 0, H)
+        group_w("vector", 1, 0, 0, 0, W_SECOND)
         scatter("scalar", 1, 0, H)
-        quantize_w(1, 0, 0)
         quantize_w(1, 0, 1)
-        project("vector", [(0, H, C)], 5)
-        scatter("scalar", 0, H, C)
+        quantize_w(1, 0, 0)
+        project("vector", [(0, H, C)], 5, None, early[:, C:])
+        scatter("scalar", 0, 0, C)
         multiply(1, 0, 0, C, [0, 1, 2, 3])
-        for u in range(2):
-            group_w("vector", 1, 1, u, 0, P)
+        group_w("vector", 1, 1, 0, 0, P)
+        group_w("vector", 1, 1, 1, 0, P)
         for u in range(2):
             quantize_w(1, 1, u)
         multiply(1, 1, 0, C, [0, 1, 2, 3])

@@ -29,6 +29,7 @@ R = S // P
 H = C // 2
 
 W_FIRST = 176
+X_SCALAR = 160
 W_SECOND = 112
 W_VECTOR = 96
 
@@ -95,7 +96,7 @@ def tile_moe_nxt_lin_relu_kernel(tc, xT, w, b, wp, gate, offs, out):
         gates = sbuf([P, S], F32, "gates")
         nc.scalar.copy(out=gates.rearrange("p (m r) -> p m r", r=R), in_=gbank[:].rearrange("p r m -> p m r"))
 
-        xgrouped = {}
+        xgrouped = {(e, a): sbuf([P, C, J], BF16, f"xgrouped{e}{a}") for e in range(E) for a in range(PASSES)}
         xplain = [sbuf([P, J, C], BF16 if a else F32, f"xplain{a}") for a in range(PASSES)]
         xcodes = {}
         xbytes = {}
@@ -105,7 +106,7 @@ def tile_moe_nxt_lin_relu_kernel(tc, xT, w, b, wp, gate, offs, out):
         ybank = {}
         ysums = {}
         y = {}
-        c = {}
+        c = [sbuf([P, C, J], BF16, f"c{e}") for e in range(E)]
         ccodes = sbuf([P, S], U32, "ccodes")
         cbytes = sbuf([P, S], U8, "cbytes")
         wpgrouped = {}
@@ -132,18 +133,15 @@ def tile_moe_nxt_lin_relu_kernel(tc, xT, w, b, wp, gate, offs, out):
             nc.vector.quantize_mx(out=codes.bitcast(FP8X4), scales=scales, in_=grouped)
 
         def gather(engine, a, j, e, s0, s1):
-            if j == 0:
-                xgrouped[e, a, s0] = sbuf([P, s1 - s0, J], BF16, f"xgrouped{e}{a}{s0}")
-            move_indirect(engine, xgrouped[e, a, s0][:, :, j], xrow[a, j].indirect(slots(e, s0, s1)))
+            move_indirect(engine, xgrouped[e, a][:, s0:s1, j], xrow[a, j].indirect(slots(e, s0, s1)))
 
         def gather_plain(a, j):
             move_indirect("scalar", xplain[a][:, j, :], xrow[a, j].indirect(slots(1, 0, C)))
 
-        def group_x(engine, a, s0, s1, tag=None):
-            xgrouped[1, a, s0] = sbuf([P, s1 - s0, J], BF16, f"xgrouped1{a}{s0}", tag)
+        def group_x(engine, a, s0, s1):
             move(
                 engine,
-                xgrouped[1, a, s0].rearrange("p (x i) j -> p x j i", i=4),
+                xgrouped[1, a][:, s0:s1, :].rearrange("p (x i) j -> p x j i", i=4),
                 xplain[a][:, :, s0:s1].rearrange("p j (x i) -> p x j i", i=4),
             )
 
@@ -151,7 +149,7 @@ def tile_moe_nxt_lin_relu_kernel(tc, xT, w, b, wp, gate, offs, out):
             if s0 == 0:
                 xcodes[e, a] = sbuf([P, C], U32, f"xcodes{e}{a}", tag)
                 xbytes[e, a] = sbuf([P, C], U8, f"xbytes{e}{a}")
-            grouped = xgrouped[e, a, s0].rearrange("p s j -> p (s j)")
+            grouped = xgrouped[e, a][:, s0:s1, :].rearrange("p s j -> p (s j)")
             quantize(xcodes[e, a][:, s0:s1], xbytes[e, a][:, s0:s1], grouped)
 
         def group_w(engine, e, a, u, m0, m1, tag=None):
@@ -206,18 +204,17 @@ def tile_moe_nxt_lin_relu_kernel(tc, xT, w, b, wp, gate, offs, out):
             else:
                 nc.scalar.activation(y[e, s0][:, t, :], ysums[e, t, s0], RELU, bias=column)
 
-        def gate_product(e, s0, s1, y0, tag=None):
-            c[e, s0] = sbuf([P, s1 - s0, J], BF16, f"c{e}{s0}", tag)
+        def gate_product(e, s0, s1, y0):
             weights = gates[:, e * C + s0 : e * C + s1].rearrange("p (m r) -> p m r", r=2)
             nc.vector.tensor_tensor(
-                out=c[e, s0].rearrange("p (m r) t -> p m t r", r=2),
+                out=c[e][:, s0:s1, :].rearrange("p (m r) t -> p m t r", r=2),
                 in0=y[e, y0][:, :, s0 - y0 : s1 - y0].rearrange("p t (m r) -> p m t r", r=2),
                 in1=weights.unsqueeze(2).to_broadcast([P, (s1 - s0) // 2, J, 2]),
                 op=MULT,
             )
 
         def quantize_c(e, s0, s1):
-            quantize(ccodes[:, e * C + s0 : e * C + s1], cbytes[:, e * C + s0 : e * C + s1], c[e, s0].rearrange("p s t -> p (s t)"))
+            quantize(ccodes[:, e * C + s0 : e * C + s1], cbytes[:, e * C + s0 : e * C + s1], c[e][:, s0:s1, :].rearrange("p s t -> p (s t)"))
 
         def group_wp(h):
             wpgrouped[h] = sbuf([P, 2 * P, J], BF16, f"wpgrouped{h}")
@@ -272,20 +269,19 @@ def tile_moe_nxt_lin_relu_kernel(tc, xT, w, b, wp, gate, offs, out):
             multiply(0, 0, s0, s1, banks)
         prepare_w(0, 1, W_VECTOR)
         for j in range(J):
-            for s0 in (0, H):
-                gather("vector", 1, j, 0, s0, s0 + H)
+            for s0, s1 in [(0, C)] if j < J - 1 else [(0, H), (H, C)]:
+                gather("vector", 1, j, 0, s0, s1)
             gather_plain(1, j)
-        group_x("scalar", 1, 0, H)
+        group_x("scalar", 1, 0, X_SCALAR)
         for s0, s1, banks in first:
             quantize_x(0, 1, s0, s1)
             multiply(0, 1, s0, s1, banks)
-        group_x("vector", 1, H, C)
+        group_x("vector", 1, X_SCALAR, C)
         group_wp(0)
         for s0 in (0, H):
             for t in range(J):
                 relu("scalar", 0, t, s0, s0 + H)
-        quantize_x(1, 1, 0, H)
-        quantize_x(1, 1, H, C)
+        quantize_x(1, 1, 0, C)
         quantize_wp(0)
         for s0 in (0, H):
             gate_product(0, s0, s0 + H, s0)
@@ -318,8 +314,7 @@ def tile_moe_nxt_lin_relu_kernel(tc, xT, w, b, wp, gate, offs, out):
             gate_product(1, s0, s0 + H, s0)
         project("vector", [(1, H, C)], 7, "y10")
         scatter("scalar", 2, 0, C)
-        for s0 in (0, H):
-            quantize_c(1, s0, s0 + H)
+        quantize_c(1, 0, C)
         scatter("vector", 1, H, C)
         project("vector", [(0, C, S)], 5)
         project("vector", [(1, C, S)], 0)

@@ -28,10 +28,11 @@ G = M // P
 R = S // P
 H = C // 2
 
-W_FIRST = 176
+W_FIRST = 112
 X_SCALAR = 160
-W_SECOND = 112
-W_VECTOR = 96
+W_SECOND = 56
+W_PAIRS = 80
+W_VECTOR = 64
 
 
 def tile_moe_nxt_lin_relu_kernel(tc, xT, w, b, wp, gate, offs, out):
@@ -152,32 +153,29 @@ def tile_moe_nxt_lin_relu_kernel(tc, xT, w, b, wp, gate, offs, out):
             grouped = xgrouped[e, a][:, s0:s1, :].rearrange("p s j -> p (s j)")
             quantize(xcodes[e, a][:, s0:s1], xbytes[e, a][:, s0:s1], grouped)
 
-        def group_w(engine, e, a, u, m0, m1, tag=None):
-            if (e, a, u) not in wgrouped:
-                wgrouped[e, a, u] = sbuf([P, 2, P, J], BF16, f"wgrouped{e}{a}{u}", tag)
-            columns = wraw[e, a].rearrange("p j (m u t) -> p j m u t", u=2, t=2)[:, :, m0:m1, u, :]
+        def group_w(engine, e, a, m0, m1, t0, t1):
+            if (e, a) not in wgrouped:
+                wgrouped[e, a] = sbuf([P, J, P, J], BF16, f"wgrouped{e}{a}")
             move(
                 engine,
-                wgrouped[e, a, u][:, :, m0:m1, :].rearrange("p t m j -> p m j t"),
-                columns.rearrange("p j m t -> p m j t"),
+                wgrouped[e, a][:, t0:t1, m0:m1, :].rearrange("p t m j -> p m j t"),
+                wraw[e, a].rearrange("p j (m t) -> p m j t", t=J)[:, m0:m1, :, t0:t1],
             )
 
-        def quantize_w(e, a, u):
-            wcodes[e, a, u] = sbuf([P, 2 * P], U32, f"wcodes{e}{a}{u}")
-            wbytes[e, a, u] = sbuf([P, 2 * P], U8, f"wbytes{e}{a}{u}")
-            quantize(wcodes[e, a, u], wbytes[e, a, u], wgrouped[e, a, u].rearrange("p t m j -> p (t m j)"))
+        def quantize_w(e, a, t0, t1):
+            if t0 == 0:
+                wcodes[e, a] = sbuf([P, N], U32, f"wcodes{e}{a}")
+                wbytes[e, a] = sbuf([P, N], U8, f"wbytes{e}{a}")
+            grouped = wgrouped[e, a][:, t0:t1, :, :].rearrange("p t m j -> p (t m j)")
+            quantize(wcodes[e, a][:, t0 * P : t1 * P], wbytes[e, a][:, t0 * P : t1 * P], grouped)
 
         def prepare_w(e, a, share):
-            for engine, lo, hi in (("vector", 0, share), ("scalar", share, 2 * P)):
-                for u in range(2):
-                    if min(hi - u * P, P) > max(lo - u * P, 0):
-                        group_w(engine, e, a, u, max(lo - u * P, 0), min(hi - u * P, P))
-            for u in range(2):
-                quantize_w(e, a, u)
+            group_w("vector", e, a, 0, share, 0, J)
+            group_w("scalar", e, a, share, P, 0, J)
+            quantize_w(e, a, 0, J)
 
         def multiply(e, a, s0, s1, banks):
             for t in range(J):
-                u, i = divmod(t, 2)
                 sharers = [x for x in range(J) if banks[x] == banks[t]]
                 if a == 0 and t == sharers[0]:
                     bank = psum.tile([P, len(sharers), s1 - s0], F32, name=f"ybank{e}{t}{s0}", tag=f"bank{banks[t]}")
@@ -187,8 +185,8 @@ def tile_moe_nxt_lin_relu_kernel(tc, xT, w, b, wp, gate, offs, out):
                             ysums[e, x, h0] = bank[:, n, h0 - s0 : h0 - s0 + H]
                 nc.tensor.matmul_mx(
                     out=ybank[e, t, s0],
-                    lhsT=wcodes[e, a, u][:, i * P : (i + 1) * P].bitcast(FP8X4),
-                    lhsT_scale=wbytes[e, a, u][:, i * P : (i + 1) * P],
+                    lhsT=wcodes[e, a][:, t * P : (t + 1) * P].bitcast(FP8X4),
+                    lhsT_scale=wbytes[e, a][:, t * P : (t + 1) * P],
                     rhs=xcodes[e, a][:, s0:s1].bitcast(FP8X4),
                     rhs_scale=xbytes[e, a][:, s0:s1],
                     start=(a == 0 and t == sharers[0]),
@@ -286,22 +284,21 @@ def tile_moe_nxt_lin_relu_kernel(tc, xT, w, b, wp, gate, offs, out):
         for s0 in (0, H):
             gate_product(0, s0, s0 + H, s0)
         quantize_c(0, 0, H)
-        group_w("scalar", 1, 0, 1, 0, P)
-        group_w("scalar", 1, 0, 0, W_SECOND, P, "y00")
+        group_w("scalar", 1, 0, W_SECOND, P, 0, J)
         early = sbuf([P, H + C], F32, "early")
         project("scalar", [(1, 0, H), (0, 0, H)], 7, None, early)
         quantize_c(0, H, C)
-        group_w("vector", 1, 0, 0, 0, W_SECOND)
+        group_w("vector", 1, 0, 0, W_SECOND, 0, J)
         scatter("scalar", 1, 0, H)
-        quantize_w(1, 0, 1)
-        quantize_w(1, 0, 0)
+        quantize_w(1, 0, 0, J)
         project("vector", [(0, H, C)], 5, None, early[:, C:])
         scatter("scalar", 0, 0, C)
         multiply(1, 0, 0, C, [0, 1, 2, 3])
-        group_w("vector", 1, 1, 0, 0, P)
-        group_w("vector", 1, 1, 1, 0, P)
-        for u in range(2):
-            quantize_w(1, 1, u)
+        group_w("vector", 1, 1, 0, W_PAIRS, 0, J)
+        for t in (0, 2):
+            group_w("vector", 1, 1, W_PAIRS, P, t, t + 2)
+        for t in (0, 2):
+            quantize_w(1, 1, t, t + 2)
         multiply(1, 1, 0, C, [0, 1, 2, 3])
         group_wp(1)
         for t in range(J):

from contextlib import ExitStack

import concourse.mybir as mybir
from concourse.masks import make_identity

K, T, E, C, N, M = 1024, 1024, 2, 256, 512, 512
S = E * C
FLOPS = 2 * K * N * S + 2 * N * M * S

F32 = mybir.dt.float32
BF16 = mybir.dt.bfloat16
U32 = mybir.dt.uint32
I32 = mybir.dt.int32
U16 = mybir.dt.uint16
U8 = mybir.dt.uint8
FP8X4 = mybir.dt.float8_e4m3fn_x4
RELU = mybir.ActivationFunctionType.Relu
COPY = mybir.ActivationFunctionType.Copy
MULT = mybir.AluOpType.mult
ADD = mybir.AluOpType.add
MAX = mybir.AluOpType.max

P = 128
J = 4
KP = P * J
PASSES = K // KP
G = M // P
R = S // P
H = C // 2

W_FIRST = 112
X_SCALAR = 160
W_SECOND = 56
W_PAIRS = 80
W_VECTOR = 64


def tile_moe_nxt_lin_relu_kernel(tc, xT, w, b, wp, gate, offs, out):
    nc = tc.nc
    with ExitStack() as ctx:
        keep = ctx.enter_context(tc.tile_pool(name="keep", bufs=1))
        psum = ctx.enter_context(tc.psum_pool(name="psum", bufs=1))

        def sbuf(shape, dtype, name, tag=None):
            return keep.tile(shape, dtype, name=name, tag=tag or name, align_bytes=64)[:]

        offsets = keep.tile([P, S // 16], U16, name="offsets")
        bias = sbuf([P, J * E], F32, "bias")
        gate_row = sbuf([P, R], F32, "gate_row")
        xrow = {}
        wraw = {}
        wpraw = {}

        def load_x(a, j, rows):
            tile = sbuf([P, rows * T], F32, f"xrow{a}{j}")
            source = xT[a * KP : (a + 1) * KP, :].rearrange("(p j) t -> p (j t)", j=J)
            nc.sync.dma_start(tile, source[:, j * T : (j + rows) * T])
            for i in range(rows):
                xrow[a, j + i] = tile[:, i * T : (i + 1) * T]

        def load_w(e, a):
            wraw[e, a] = sbuf([P, J, N], F32, f"wraw{e}{a}")
            nc.sync.dma_start(wraw[e, a], w[e, a * KP : (a + 1) * KP, :].rearrange("(p j) n -> p j n", j=J))

        def load_wp(h):
            wpraw[h] = sbuf([P, J, M // 2], F32, f"wpraw{h}")
            nc.sync.dma_start(wpraw[h], wp[:, h * M // 2 : (h + 1) * M // 2].rearrange("(p j) f -> p j f", j=J))

        nc.scalar.dma_start(gate_row, gate[0, :].rearrange("(p r) -> p r", r=R))
        nc.scalar.dma_start(bias, b.rearrange("(p t) e -> p (t e)", t=J))
        load_x(0, 0, 2)
        nc.sync.dma_start(offsets[:], offs)
        load_x(0, 2, 2)
        load_w(0, 0)
        load_w(0, 1)
        for j in range(J):
            load_x(1, j, 1)
        load_wp(0)
        load_w(1, 0)
        load_w(1, 1)
        load_wp(1)

        identity = sbuf([P, P], F32, "identity")
        make_identity(nc, identity)
        gbank = psum.tile([P, R, P], F32, name="gbank", tag="bank4")
        for r in range(R):
            nc.tensor.transpose(gbank[:, r, :], gate_row[:, r : r + 1].to_broadcast([P, P]), identity)

        window = [keep.tile([P, T], F32, name=f"window{g}", align_bytes=64) for g in range(G)]
        zeros = sbuf([P, 8], F32, "zeros")
        nc.vector.memset(zeros, 0.0)
        nc.scalar.activation(window[0][:, 0:8], zeros, RELU)
        nc.vector.memset(window[0][:, 8:T].bitcast(I32), 0)
        for g in range(1, G):
            nc.vector.memset(window[g][:].bitcast(I32), 0)

        gates = sbuf([P, S], F32, "gates")
        nc.scalar.copy(out=gates.rearrange("p (m r) -> p m r", r=R), in_=gbank[:].rearrange("p r m -> p m r"))

        xgrouped = {(e, a): sbuf([P, C, J], BF16, f"xgrouped{e}{a}") for e in range(E) for a in range(PASSES)}
        xplain = [sbuf([P, J, C], BF16 if a else F32, f"xplain{a}") for a in range(PASSES)]
        xcodes = {}
        xbytes = {}
        wgrouped = {}
        wcodes = {}
        wbytes = {}
        ybank = {}
        ysums = {}
        y = {}
        c = [sbuf([P, C, J], BF16, f"c{e}") for e in range(E)]
        ccodes = sbuf([P, S], U32, "ccodes")
        cbytes = sbuf([P, S], U8, "cbytes")
        wpgrouped = {}
        wpcodes = {}
        wpbytes = {}
        result = {}

        def slots(e, s0, s1):
            return offsets[:, (e * C + s0) // 16 : (e * C + s1) // 16]

        def move(engine, dst, src):
            if engine == "vector":
                nc.vector.tensor_copy(out=dst, in_=src)
            else:
                nc.scalar.copy(out=dst, in_=src)

        def move_indirect(engine, dst, src):
            if engine == "vector":
                nc.vector.tensor_copy(dst, src)
            else:
                nc.scalar.activation(dst, src, COPY)

        def quantize(codes, scales, grouped):
            nc.vector.quantize_mx(out=codes.bitcast(FP8X4), scales=scales, in_=grouped)

        def gather(engine, a, j, e, s0, s1):
            move_indirect(engine, xgrouped[e, a][:, s0:s1, j], xrow[a, j].indirect(slots(e, s0, s1)))

        def gather_plain(a, j):
            move_indirect("scalar", xplain[a][:, j, :], xrow[a, j].indirect(slots(1, 0, C)))

        def group_x(engine, a, s0, s1):
            move(
                engine,
                xgrouped[1, a][:, s0:s1, :].rearrange("p (x i) j -> p x j i", i=4),
                xplain[a][:, :, s0:s1].rearrange("p j (x i) -> p x j i", i=4),
            )

        def quantize_x(e, a, s0, s1, tag=None):
            if s0 == 0:
                xcodes[e, a] = sbuf([P, C], U32, f"xcodes{e}{a}", tag)
                xbytes[e, a] = sbuf([P, C], U8, f"xbytes{e}{a}")
            grouped = xgrouped[e, a][:, s0:s1, :].rearrange("p s j -> p (s j)")
            quantize(xcodes[e, a][:, s0:s1], xbytes[e, a][:, s0:s1], grouped)

        def group_w(engine, e, a, m0, m1, t0, t1):
            if (e, a) not in wgrouped:
                wgrouped[e, a] = sbuf([P, J, P, J], BF16, f"wgrouped{e}{a}")
            move(
                engine,
                wgrouped[e, a][:, t0:t1, m0:m1, :].rearrange("p t m j -> p m j t"),
                wraw[e, a].rearrange("p j (m t) -> p m j t", t=J)[:, m0:m1, :, t0:t1],
            )

        def quantize_w(e, a, t0, t1):
            if t0 == 0:
                wcodes[e, a] = sbuf([P, N], U32, f"wcodes{e}{a}")
                wbytes[e, a] = sbuf([P, N], U8, f"wbytes{e}{a}")
            grouped = wgrouped[e, a][:, t0:t1, :, :].rearrange("p t m j -> p (t m j)")
            quantize(wcodes[e, a][:, t0 * P : t1 * P], wbytes[e, a][:, t0 * P : t1 * P], grouped)

        def prepare_w(e, a, share):
            group_w("vector", e, a, 0, share, 0, J)
            group_w("scalar", e, a, share, P, 0, J)
            quantize_w(e, a, 0, J)

        def multiply(e, a, s0, s1, banks):
            for t in range(J):
                sharers = [x for x in range(J) if banks[x] == banks[t]]
                if a == 0 and t == sharers[0]:
                    bank = psum.tile([P, len(sharers), s1 - s0], F32, name=f"ybank{e}{t}{s0}", tag=f"bank{banks[t]}")
                    for n, x in enumerate(sharers):
                        ybank[e, x, s0] = bank[:, n, :]
                        for h0 in range(s0, s1, H):
                            ysums[e, x, h0] = bank[:, n, h0 - s0 : h0 - s0 + H]
                nc.tensor.matmul_mx(
                    out=ybank[e, t, s0],
                    lhsT=wcodes[e, a][:, t * P : (t + 1) * P].bitcast(FP8X4),
                    lhsT_scale=wbytes[e, a][:, t * P : (t + 1) * P],
                    rhs=xcodes[e, a][:, s0:s1].bitcast(FP8X4),
                    rhs_scale=xbytes[e, a][:, s0:s1],
                    start=(a == 0 and t == sharers[0]),
                    stop=(a == PASSES - 1 and t == sharers[-1]),
                )

        def relu(engine, e, t, s0, s1):
            if (e, s0) not in y:
                y[e, s0] = sbuf([P, J, s1 - s0], F32, f"y{e}{s0}")
            column = bias[:, t * E + e : t * E + e + 1]
            if engine == "vector":
                nc.vector.tensor_scalar(y[e, s0][:, t, :], ysums[e, t, s0], column, 0.0, ADD, MAX)
            else:
                nc.scalar.activation(y[e, s0][:, t, :], ysums[e, t, s0], RELU, bias=column)

        def gate_product(e, s0, s1, y0):
            weights = gates[:, e * C + s0 : e * C + s1].rearrange("p (m r) -> p m r", r=2)
            nc.vector.tensor_tensor(
                out=c[e][:, s0:s1, :].rearrange("p (m r) t -> p m t r", r=2),
                in0=y[e, y0][:, :, s0 - y0 : s1 - y0].rearrange("p t (m r) -> p m t r", r=2),
                in1=weights.unsqueeze(2).to_broadcast([P, (s1 - s0) // 2, J, 2]),
                op=MULT,
            )

        def quantize_c(e, s0, s1):
            quantize(ccodes[:, e * C + s0 : e * C + s1], cbytes[:, e * C + s0 : e * C + s1], c[e][:, s0:s1, :].rearrange("p s t -> p (s t)"))

        def group_wp(h):
            wpgrouped[h] = sbuf([P, 2 * P, J], BF16, f"wpgrouped{h}")
            nc.vector.tensor_copy(
                out=wpgrouped[h].rearrange("p (x i) j -> p x j i", i=4),
                in_=wpraw[h].rearrange("p j (x i) -> p x j i", i=4),
            )

        def quantize_wp(h):
            wpcodes[h] = sbuf([P, 2 * P], U32, f"wpcodes{h}")
            wpbytes[h] = sbuf([P, 2 * P], U8, f"wpbytes{h}")
            quantize(wpcodes[h], wpbytes[h], wpgrouped[h].rearrange("p f j -> p (f j)"))

        def project(engine, pieces, bank, tag=None, rows=None):
            width = sum(s1 - s0 for g, s0, s1 in pieces)
            name = f"{pieces[0][0]}_{pieces[0][1]}"
            sums = psum.tile([P, width], F32, name=f"obank{name}", tag=f"bank{bank}")
            if rows is None:
                rows = sbuf([P, width], F32, f"result{name}", tag)
            at = 0
            for g, s0, s1 in pieces:
                h, i = divmod(g, 2)
                nc.tensor.matmul_mx(
                    out=sums[:, at : at + s1 - s0],
                    lhsT=wpcodes[h][:, i * P : (i + 1) * P].bitcast(FP8X4),
                    lhsT_scale=wpbytes[h][:, i * P : (i + 1) * P],
                    rhs=ccodes[:, s0:s1].bitcast(FP8X4),
                    rhs_scale=cbytes[:, s0:s1],
                    start=True,
                    stop=True,
                )
                result[g, s0] = rows[:, at:]
                at = at + s1 - s0
            move(engine, rows[:, 0:width], sums[:])

        def scatter(engine, g, s0, s1):
            move_indirect(engine, window[g][:].indirect(slots(0, s0, s1)), result[g, s0][:, 0 : s1 - s0])

        def store(g):
            queue = nc.scalar if g == 3 else nc.sync
            queue.dma_start(out[g * P : (g + 1) * P, :], window[g][:, 0:T])

        for j in range(J):
            gather("vector", 0, j, 0, 0, C)
            gather_plain(0, j)
        group_x("scalar", 0, 0, C)
        quantize_x(0, 0, 0, C)
        quantize_x(1, 0, 0, C)
        first = [(0, H, [0, 1, 2, 3]), (H, C, [5, 5, 6, 6])]
        prepare_w(0, 0, W_FIRST)
        for s0, s1, banks in first:
            multiply(0, 0, s0, s1, banks)
        prepare_w(0, 1, W_VECTOR)
        for j in range(J):
            for s0, s1 in [(0, C)] if j < J - 1 else [(0, H), (H, C)]:
                gather("vector", 1, j, 0, s0, s1)
            gather_plain(1, j)
        group_x("scalar", 1, 0, X_SCALAR)
        for s0, s1, banks in first:
            quantize_x(0, 1, s0, s1)
            multiply(0, 1, s0, s1, banks)
        group_x("vector", 1, X_SCALAR, C)
        group_wp(0)
        for s0 in (0, H):
            for t in range(J):
                relu("scalar", 0, t, s0, s0 + H)
        quantize_x(1, 1, 0, C)
        quantize_wp(0)
        for s0 in (0, H):
            gate_product(0, s0, s0 + H, s0)
        quantize_c(0, 0, H)
        group_w("scalar", 1, 0, W_SECOND, P, 0, J)
        early = sbuf([P, H + C], F32, "early")
        project("scalar", [(1, 0, H), (0, 0, H)], 7, None, early)
        quantize_c(0, H, C)
        group_w("vector", 1, 0, 0, W_SECOND, 0, J)
        scatter("scalar", 1, 0, H)
        quantize_w(1, 0, 0, J)
        project("vector", [(0, H, C)], 5, None, early[:, C:])
        scatter("scalar", 0, 0, C)
        multiply(1, 0, 0, C, [0, 1, 2, 3])
        group_w("vector", 1, 1, 0, W_PAIRS, 0, J)
        for t in (0, 2):
            group_w("vector", 1, 1, W_PAIRS, P, t, t + 2)
        for t in (0, 2):
            quantize_w(1, 1, t, t + 2)
        multiply(1, 1, 0, C, [0, 1, 2, 3])
        group_wp(1)
        for t in range(J):
            relu("vector" if t < 1 else "scalar", 1, t, 0, H)
        quantize_wp(1)
        for t in range(J):
            relu("vector" if t < 1 else "scalar", 1, t, H, C)
        project("scalar", [(2, 0, C)], 6)
        for s0 in (0, H):
            gate_product(1, s0, s0 + H, s0)
        project("vector", [(1, H, C)], 7, "y10")
        scatter("scalar", 2, 0, C)
        quantize_c(1, 0, C)
        scatter("vector", 1, H, C)
        project("vector", [(0, C, S)], 5)
        project("vector", [(1, C, S)], 0)
        project("scalar", [(3, 0, C), (3, C, S)], 2)
        scatter("vector", 0, C, S)
        store(0)
        project("vector", [(2, C, S)], 1)
        scatter("scalar", 1, C, S)
        store(1)
        scatter("vector", 3, 0, S)
        scatter("scalar", 2, C, S)
        store(2)
        store(3)
